import numpy as np
import ml_dtypes


def mxq(x, axis, fmt="e4m3"):
    dtype, down = {"e4m3": (ml_dtypes.float8_e4m3fn, 7), "e5m2": (ml_dtypes.float8_e5m2, 14)}[fmt]
    v = np.moveaxis(np.asarray(x, np.float32).astype(ml_dtypes.bfloat16).astype(np.float64), axis, -1)
    blocks = v.reshape(v.shape[:-1] + (-1, 32))
    amax = np.abs(blocks).max(-1, keepdims=True)
    byte = np.maximum(np.where(amax > 0, np.frexp(amax)[1] - 1 + 127, 0) - down, 1)
    scale = np.exp2(byte - 127.0)
    codes = (blocks / scale).astype(np.float32).astype(dtype).astype(np.float64)
    return np.moveaxis((codes * scale).reshape(v.shape), -1, axis)


WIDE = False


def mx_kscale(k):
    if not WIDE:
        return np.ones(k)
    levels = np.array([10, -10, 5, -5, 0])
    if k % 512:
        return np.exp2(np.random.permutation(np.resize(levels, k // 32))).repeat(32)
    a = np.empty((k // 512, 16))
    for p in range(k // 512):
        a[p, :8] = np.random.permutation(np.resize(levels, 8))
        for g in range(8):
            far = levels[np.abs(levels - a[p, g]) >= 10]
            a[p, g + 8] = far[np.random.randint(len(far))]
    return np.exp2(a.ravel()).repeat(32)


def f64(x):
    return np.asarray(x).astype(np.float64)


def striped(idx):
    return np.tile(idx.reshape(-1, 16).T, (8, 1)).astype(np.uint16)


def unstriped(offs):
    return offs[:16].T.reshape(-1).astype(np.int64)


E2M1 = np.array([0.0, 0.5, 1.0, 1.5, 2.0, 3.0, 4.0, 6.0, -0.0, -0.5, -1.0, -1.5, -2.0, -3.0, -4.0, -6.0])


def pack_weight(w, fmt):
    k, n = w.shape
    w = f64(np.asarray(w, np.float32).astype(ml_dtypes.bfloat16)).reshape(k // 32, 32, n)
    amax = np.abs(w).max(1)
    if fmt == "e4m3":
        byte = np.frexp(amax)[1] - 1 + 127 - 7
    else:
        mant, ex = np.frexp(amax / 6.0)
        byte = np.where(mant > 0.5, ex, ex - 1) + 127
    byte = np.clip(np.where(amax > 0, byte, 1), 1, 254)
    scaled = (w * np.exp2(127.0 - byte)[:, None, :]).reshape(k, n).astype(np.float32)
    by_word = np.ascontiguousarray(scaled.reshape(k // 512, 128, 4, n).transpose(0, 1, 3, 2))
    if fmt == "e4m3":
        words = by_word.astype(ml_dtypes.float8_e4m3fn).view(np.uint8)
    else:
        c = by_word.astype(ml_dtypes.float4_e2m1fn).view(np.uint8) & 0xF
        words = (c[..., 0::2] | (c[..., 1::2] << 4)).reshape(k // 512, 128, 2 * n)
    return np.ascontiguousarray(words), np.ascontiguousarray(byte.astype(np.uint8).reshape(k // 512, 16, n))


def unpack_weight(words, scales, fmt):
    g, _, n = scales.shape
    words = np.ascontiguousarray(words).reshape(g, 128, n, -1)
    if fmt == "e4m3":
        vals = words.view(ml_dtypes.float8_e4m3fn).astype(np.float64)
    else:
        nib = np.empty((g, 128, n, 4), np.uint8)
        nib[..., 0::2] = words & 0xF
        nib[..., 1::2] = words >> 4
        vals = E2M1[nib]
    vals = vals * np.repeat(np.exp2(scales.astype(np.float64) - 127.0), 8, axis=1)[..., None]
    return vals.transpose(0, 1, 3, 2).reshape(g * 512, n)


D, T, E, C, H, N = 2, 768, 12, 256, 512, 256


def by_expert(wq, xq):
    return np.concatenate([wq[e].T @ xq[:, e * C:(e + 1) * C] for e in range(E)], axis=1)


def setup_inputs():
    n = np.random.standard_normal
    s = np.tile(mx_kscale(H), D)
    u = mx_kscale(H)
    X = D * T
    first = np.random.permutation(np.repeat(np.arange(E), X // E))
    second = (first + 1 + np.random.permutation(np.repeat(np.arange(E - 1), -(-X // (E - 1)))[:X])) % E
    while np.bincount(second, minlength=E).max() != X // E:
        load = np.bincount(second, minlength=E); hi, lo = int(load.argmax()), int(load.argmin())
        t = np.flatnonzero((second == hi) & (first != lo))[0]; second[t] = lo
    slot_sub = np.empty(E * C, np.int64); pos = np.empty((2, X), np.int64); fill = np.zeros(E, np.int64)
    place = np.stack([np.random.permutation(C) for _ in range(E)])
    for r, deal in enumerate((first, second)):
        for t in np.random.permutation(X):
            e = deal[t]; j = e * C + place[e, fill[e]]; fill[e] += 1; slot_sub[j] = t; pos[r, t] = j
    g = np.random.uniform(0.2, 0.8, X)
    x = pack_weight(n((D * H, T)) * s[:, None], "e4m3")
    w = [pack_weight(m, "e2m1") for m in n((E, H, H)) / np.sqrt(H) / s[None, :H, None] * u]
    wm = pack_weight(n((D * H, N)) / np.sqrt(D * H) / np.tile(u, D)[:, None], "e2m1")
    return {
        "x_words": x[0],
        "x_scales": x[1],
        "w_words": np.stack([m[0] for m in w]),
        "w_scales": np.stack([m[1] for m in w]),
        "wm_words": wm[0],
        "wm_scales": wm[1],
        "gate": np.stack([np.tile(g, (128, 1)), np.tile(1.0 - g, (128, 1))]).astype(np.float32),
        "offs": striped(slot_sub),
        "pos1": striped(pos[0]),
        "pos2": striped(pos[1]),
    }


def reference(x_words, x_scales, w_words, w_scales, wm_words, wm_scales, gate, offs, pos1, pos2):
    w = np.stack([unpack_weight(w_words[e], w_scales[e], "e2m1") for e in range(E)])
    wm = unpack_weight(wm_words, wm_scales, "e2m1")
    idx = unstriped(offs)
    x = unpack_weight(x_words, x_scales, "e4m3")
    sub = x.reshape(D, H, T).transpose(1, 0, 2).reshape(H, D * T)
    y = by_expert(w, sub[:, idx])
    c = sum(f64(gate[r, :1]) * y[:, unstriped(p)] for r, p in enumerate((pos1, pos2)))
    cq = mxq(c, 0, "e4m3").reshape(H, D, T).transpose(1, 0, 2).reshape(D * H, T)
    return wm.T @ cq

@@ -1,0 +1,215 @@
+from contextlib import ExitStack
+
+import concourse.mybir as mybir
+from concourse.masks import make_identity
+
+D, T, E, C, H, N = 2, 768, 12, 256, 512, 256
+Z = D * T
+S = E * C
+FLOPS = 2 * H * H * S + 2 * D * H * N * T
+
+F32 = mybir.dt.float32
+BF16 = mybir.dt.bfloat16
+I32 = mybir.dt.int32
+U32 = mybir.dt.uint32
+U16 = mybir.dt.uint16
+U8 = mybir.dt.uint8
+FP8X4 = mybir.dt.float8_e4m3fn_x4
+FP4X4 = mybir.dt.float4_e2m1fn_x4
+MULT = mybir.AluOpType.mult
+
+P = 128
+LT = H // P
+BANK = 512
+PER_COL = 16
+W_LOAD = 4
+
+
+def tile_moe_mhm_none_kernel(
+    tc, x_words, x_scales, w_words, w_scales, wm_words, wm_scales, gate, offs, pos1, pos2, out
+):
+    nc = tc.nc
+    with ExitStack() as ctx:
+        keep = ctx.enter_context(tc.tile_pool(name="keep", bufs=1))
+        ring = ctx.enter_context(tc.tile_pool(name="ring", bufs=3))
+        psum = ctx.enter_context(tc.psum_pool(name="psum", bufs=8))
+
+        offs_sb = keep.tile([P, S // PER_COL], U16, name="offs_sb")
+        pos_sb = [keep.tile([P, Z // PER_COL], U16, name=f"pos_sb{r}") for r in range(2)]
+        xw = keep.tile([P, Z], U32, name="xw", align_bytes=64)
+        xs = keep.tile([P, Z], U8, name="xs", align_bytes=64)
+        ws = keep.tile([P, E, H], U8, name="ws", align_bytes=64)
+        wms = keep.tile([P, D, N], U8, name="wms", align_bytes=64)
+        ww = [keep.tile([P, W_LOAD, 2 * H], U8, name=f"ww{i}", align_bytes=64) for i in range(E // W_LOAD)]
+        wmw = keep.tile([P, D, 2 * N], U8, name="wmw", align_bytes=64)
+        gate_sb = [keep.tile([P, Z], F32, name=f"gate_sb{r}") for r in range(2)]
+        ident = keep.tile([P, P], F32, name="ident")
+
+        def load_scale_rows(queue, plane, rows):
+            for q in range(4):
+                queue.dma_start(
+                    plane[32 * q : 32 * q + 4].bitcast(I32),
+                    rows[:, 4 * q : 4 * q + 4, :].rearrange("a r c -> r a c").bitcast(I32),
+                )
+
+        nc.vector.memset(xs[:].bitcast(I32), 0)
+        nc.vector.memset(ws[:].rearrange("p e l -> p (e l)").bitcast(I32), 0)
+        nc.vector.memset(wms[:].rearrange("p o n -> p (o n)").bitcast(I32), 0)
+        make_identity(nc, ident[:])
+
+        nc.sync.dma_start(offs_sb[:], offs)
+        nc.sync.dma_start(
+            xw[:].bitcast(I32).rearrange("p (o t) -> p o t", o=D),
+            x_words.rearrange("o p t d -> p o (t d)").bitcast(I32),
+        )
+        load_scale_rows(nc.sync, xs[:].rearrange("p (o t) -> p o t", o=D), x_scales)
+        load_scale_rows(nc.sync, ws[:], w_scales[:, 0])
+        for i in range(E // W_LOAD):
+            (nc.sync if i == 0 else nc.gpsimd).dma_start(
+                ww[i][:].bitcast(I32),
+                w_words[W_LOAD * i : W_LOAD * (i + 1), 0].rearrange("e p b -> p e b").bitcast(I32),
+            )
+        nc.sync.dma_start(pos_sb[0][:], pos1)
+        nc.sync.dma_start(pos_sb[1][:], pos2)
+        for r in range(2):
+            nc.gpsimd.dma_start(gate_sb[r][:], gate[r])
+        nc.gpsimd.dma_start(wmw[:].bitcast(I32), wm_words.rearrange("o p b -> p o b").bitcast(I32))
+        load_scale_rows(nc.gpsimd, wms[:], wm_scales)
+
+        xw_slots = keep.tile([P, S], U32, name="xw_slots", align_bytes=64)
+        xs_slots = keep.tile([P, S], U8, name="xs_slots", align_bytes=64)
+
+        def gather_slots(dst, window, e0, e1):
+            cols = slice(e0 * C // PER_COL, e1 * C // PER_COL)
+            nc.vector.tensor_copy(dst[:, e0 * C : e1 * C], window[:].indirect(offs_sb[:, cols]))
+
+        y = [keep.tile([P, S], F32, name=f"y{j}") for j in range(LT)]
+
+        def experts(j, e0, e1):
+            bank = psum.tile([P, BANK], F32, name="bank")
+            for e in range(e0, e1):
+                nc.tensor.matmul_mx(
+                    out=bank[:, (e - e0) * C : (e - e0 + 1) * C],
+                    lhsT=ww[e // W_LOAD][:, e % W_LOAD, 2 * P * j : 2 * P * (j + 1)].bitcast(FP4X4),
+                    lhsT_scale=ws[:, e, P * j : P * (j + 1)],
+                    rhs=xw_slots[:, e * C : (e + 1) * C].bitcast(FP8X4),
+                    rhs_scale=xs_slots[:, e * C : (e + 1) * C],
+                    start=True,
+                    stop=True,
+                )
+            nc.scalar.copy(y[j][:, e0 * C : e1 * C], bank[:, : (e1 - e0) * C])
+
+        gather_slots(xw_slots, xw, 0, 4)
+        gather_slots(xs_slots, xs, 0, 4)
+        gather_slots(xw_slots, xw, 4, 8)
+        gather_slots(xs_slots, xs, 4, 8)
+        gather_slots(xs_slots, xs, 8, 12)
+        gather_slots(xw_slots, xw, 8, 11)
+        gather_slots(xw_slots, xw, 11, 12)
+        for j in range(LT):
+            experts(j, 0, 2)
+            experts(j, 2, 4)
+        for j in range(2):
+            experts(j, 4, 6)
+            experts(j, 6, 8)
+        experts(0, 8, 10)
+        experts(0, 10, 11)
+        experts(0, 11, 12)
+        experts(1, 8, 10)
+        experts(1, 10, 12)
+        for j in range(2, LT):
+            for e in range(4, E, 2):
+                experts(j, e, e + 2)
+
+        gated = [[keep.tile([P, Z], F32, name=f"gated{r}_{j}") for j in range(LT)] for r in range(2)]
+        grouped = keep.tile([P, Z, 4], BF16, name="grouped", align_bytes=64)
+        c_codes = keep.tile([P, Z], U32, name="c_codes", align_bytes=64)
+        c_scales = keep.tile([P, Z], U8, name="c_scales", align_bytes=64)
+
+        def fetch(j, z0, z1):
+            for r in range(2):
+                nc.vector.tensor_tensor(
+                    gated[r][j][:, z0:z1],
+                    y[j][:].indirect(pos_sb[r][:, z0 // PER_COL : z1 // PER_COL]),
+                    gate_sb[r][:, z0:z1],
+                    MULT,
+                )
+
+        def combine(z0):
+            cols = slice(z0, z0 + P)
+            total = psum.tile([P, BANK], F32, name="bank")
+            for j in range(LT):
+                for r in range(2):
+                    nc.tensor.matmul(
+                        total[:, P * j : P * (j + 1)],
+                        lhsT=gated[r][j][:, cols],
+                        rhs=ident[:],
+                        is_transpose=True,
+                        start=(r == 0),
+                        stop=(r == 1),
+                    )
+            rounded = ring.tile([P, 2, P, 2], BF16, name="rounded")
+            nc.scalar.copy(rounded[:], total[:].rearrange("z (p u e) -> z u p e", u=2, e=2))
+            pairs = rounded[:].rearrange("z u p e -> z (u p e)").bitcast(F32)
+            back = psum.tile([P, BANK], F32, name="bank")
+            for u in range(2):
+                nc.tensor.transpose(back[:, P * u : P * (u + 1)], pairs[:, P * u : P * (u + 1)], ident[:])
+            nc.scalar.copy(
+                grouped[:, cols, :].rearrange("p z t -> p (z t)").bitcast(F32).rearrange("p (z u) -> p z u", u=2),
+                back[:, : 2 * P].rearrange("p (u z) -> p z u", u=2),
+            )
+
+        def quantize(z0, z1):
+            nc.vector.quantize_mx(
+                out=c_codes[:, z0:z1].bitcast(FP8X4),
+                scales=c_scales[:, z0:z1],
+                in_=grouped[:, z0:z1, :].rearrange("p z t -> p (z t)"),
+            )
+
+        out_v = out.rearrange("(h p) t -> p h t", p=P)
+
+        def merge(t0, t1):
+            width = t1 - t0
+            acc = psum.tile([P, BANK], F32, name="bank")
+            for h in range(N // P):
+                for t in range(t0, t1, P):
+                    for o in range(D):
+                        nc.tensor.matmul_mx(
+                            out=acc[:, h * width + t - t0 : h * width + t - t0 + P],
+                            lhsT=wmw[:, o, 2 * P * h : 2 * P * (h + 1)].bitcast(FP4X4),
+                            lhsT_scale=wms[:, o, P * h : P * (h + 1)],
+                            rhs=c_codes[:, o * T + t : o * T + t + P].bitcast(FP8X4),
+                            rhs_scale=c_scales[:, o * T + t : o * T + t + P],
+                            start=(o == 0),
+                            stop=(o == D - 1),
+                        )
+            staged = ring.tile([P, N // P, width], F32, name="staged")
+            nc.scalar.copy(staged[:].rearrange("p h t -> p (h t)"), acc[:, : (N // P) * width])
+            nc.sync.dma_start(out_v[:, :, t0:t1], staged[:])
+
+        for j in range(LT):
+            fetch(j, 0, 768)
+        for z in range(0, 768, P):
+            combine(z)
+        for j in range(LT):
+            fetch(j, 768, 1152)
+        quantize(0, 512)
+        quantize(512, 768)
+        for z in range(768, 1152, P):
+            combine(z)
+        for j in range(LT):
+            fetch(j, 1152, 1408)
+        quantize(768, 1024)
+        merge(0, 256)
+        for z in range(1152, 1408, P):
+            combine(z)
+        fetch(0, 1408, 1536)
+        quantize(1024, 1152)
+        merge(256, 384)
+        for j in range(1, LT):
+            fetch(j, 1408, 1536)
+        quantize(1152, 1408)
+        merge(384, 640)
+        combine(1408)
+        quantize(1408, 1536)
+        merge(640, 768)

@@ -45,9 +45,9 @@ def tile_moe_mhm_none_kernel(
         gate_sb = [keep.tile([P, Z], F32, name=f"gate_sb{r}") for r in range(2)]
         ident = keep.tile([P, P], F32, name="ident")
 
-        def load_scale_rows(queue, plane, rows):
+        def load_scale_rows(plane, rows):
             for q in range(4):
-                queue.dma_start(
+                nc.sync.dma_start(
                     plane[32 * q : 32 * q + 4].bitcast(I32),
                     rows[:, 4 * q : 4 * q + 4, :].rearrange("a r c -> r a c").bitcast(I32),
                 )
@@ -62,19 +62,19 @@ def tile_moe_mhm_none_kernel(
             xw[:].bitcast(I32).rearrange("p (o t) -> p o t", o=D),
             x_words.rearrange("o p t d -> p o (t d)").bitcast(I32),
         )
-        load_scale_rows(nc.sync, xs[:].rearrange("p (o t) -> p o t", o=D), x_scales)
-        load_scale_rows(nc.sync, ws[:], w_scales[:, 0])
+        load_scale_rows(xs[:].rearrange("p (o t) -> p o t", o=D), x_scales)
+        load_scale_rows(ws[:], w_scales[:, 0])
         for i in range(E // W_LOAD):
-            (nc.sync if i == 0 else nc.gpsimd).dma_start(
+            nc.sync.dma_start(
                 ww[i][:].bitcast(I32),
                 w_words[W_LOAD * i : W_LOAD * (i + 1), 0].rearrange("e p b -> p e b").bitcast(I32),
             )
         nc.sync.dma_start(pos_sb[0][:], pos1)
         nc.sync.dma_start(pos_sb[1][:], pos2)
         for r in range(2):
-            nc.gpsimd.dma_start(gate_sb[r][:], gate[r])
-        nc.gpsimd.dma_start(wmw[:].bitcast(I32), wm_words.rearrange("o p b -> p o b").bitcast(I32))
-        load_scale_rows(nc.gpsimd, wms[:], wm_scales)
+            nc.sync.dma_start(gate_sb[r][:], gate[r])
+        load_scale_rows(wms[:], wm_scales)
+        nc.sync.dma_start(wmw[:].bitcast(I32), wm_words.rearrange("o p b -> p o b").bitcast(I32))
 
         xw_slots = keep.tile([P, S], U32, name="xw_slots", align_bytes=64)
         xs_slots = keep.tile([P, S], U8, name="xs_slots", align_bytes=64)
@@ -99,26 +99,20 @@ def tile_moe_mhm_none_kernel(
                 )
             nc.scalar.copy(y[j][:, e0 * C : e1 * C], bank[:, : (e1 - e0) * C])
 
-        gather_slots(xw_slots, xw, 0, 4)
-        gather_slots(xs_slots, xs, 0, 4)
-        gather_slots(xw_slots, xw, 4, 8)
-        gather_slots(xs_slots, xs, 4, 8)
-        gather_slots(xs_slots, xs, 8, 12)
-        gather_slots(xw_slots, xw, 8, 11)
-        gather_slots(xw_slots, xw, 11, 12)
-        for j in range(LT):
-            experts(j, 0, 2)
-            experts(j, 2, 4)
-        for j in range(2):
-            experts(j, 4, 6)
-            experts(j, 6, 8)
-        experts(0, 8, 10)
-        experts(0, 10, 11)
-        experts(0, 11, 12)
-        experts(1, 8, 10)
-        experts(1, 10, 12)
+        for e in range(0, E, 4):
+            gather_slots(xw_slots, xw, e, e + 4)
+        for e in range(0, E - 2, 2):
+            gather_slots(xs_slots, xs, e, e + 2)
+            experts(0, e, e + 2)
+            if e < E - 4:
+                experts(1, e, e + 2)
+        for e in range(E - 2, E):
+            gather_slots(xs_slots, xs, e, e + 1)
+            experts(0, e, e + 1)
+        for e in range(E - 4, E, 2):
+            experts(1, e, e + 2)
         for j in range(2, LT):
-            for e in range(4, E, 2):
+            for e in range(0, E, 2):
                 experts(j, e, e + 2)
 
         gated = [[keep.tile([P, Z], F32, name=f"gated{r}_{j}") for j in range(LT)] for r in range(2)]
@@ -135,28 +129,38 @@ def tile_moe_mhm_none_kernel(
                     MULT,
                 )
 
-        def combine(z0):
-            cols = slice(z0, z0 + P)
+        rounded = keep.tile([P, Z // P, 2, P, 2], BF16, name="rounded")
+
+        def add_up(j, z0, z1):
+            blocks = (z1 - z0) // P
             total = psum.tile([P, BANK], F32, name="bank")
-            for j in range(LT):
-                for r in range(2):
+            for r in range(2):
+                for b in range(blocks):
                     nc.tensor.matmul(
-                        total[:, P * j : P * (j + 1)],
-                        lhsT=gated[r][j][:, cols],
+                        total[:, P * b : P * (b + 1)],
+                        lhsT=gated[r][j][:, z0 + P * b : z0 + P * (b + 1)],
                         rhs=ident[:],
                         is_transpose=True,
-                        start=(r == 0),
-                        stop=(r == 1),
+                        start=(r == 0 and b == 0),
+                        stop=(r == 1 and b == blocks - 1),
                     )
-            rounded = ring.tile([P, 2, P, 2], BF16, name="rounded")
-            nc.scalar.copy(rounded[:], total[:].rearrange("z (p u e) -> z u p e", u=2, e=2))
-            pairs = rounded[:].rearrange("z u p e -> z (u p e)").bitcast(F32)
-            back = psum.tile([P, BANK], F32, name="bank")
-            for u in range(2):
-                nc.tensor.transpose(back[:, P * u : P * (u + 1)], pairs[:, P * u : P * (u + 1)], ident[:])
             nc.scalar.copy(
-                grouped[:, cols, :].rearrange("p z t -> p (z t)").bitcast(F32).rearrange("p (z u) -> p z u", u=2),
-                back[:, : 2 * P].rearrange("p (u z) -> p z u", u=2),
+                rounded[:, z0 // P : z1 // P, :, 32 * j : 32 * (j + 1), :].rearrange("z b u p e -> z u b p e"),
+                total[:, : z1 - z0].rearrange("z (b p u e) -> z u b p e", p=32, u=2, e=2),
+            )
+
+        def turn_back(z0, z1):
+            blocks = (z1 - z0) // P
+            back = psum.tile([P, BANK], F32, name="bank")
+            for b in range(blocks):
+                pairs = rounded[:, z0 // P + b].rearrange("z u p e -> z (u p e)").bitcast(F32)
+                for u in range(2):
+                    nc.tensor.transpose(
+                        back[:, P * (2 * b + u) : P * (2 * b + u + 1)], pairs[:, P * u : P * (u + 1)], ident[:]
+                    )
+            nc.scalar.copy(
+                grouped[:, z0:z1, :].rearrange("p z t -> p (z t)").bitcast(F32).rearrange("p (b z u) -> p b z u", z=P, u=2),
+                back[:, : 2 * (z1 - z0)].rearrange("p (b u z) -> p b z u", u=2, z=P),
             )
 
         def quantize(z0, z1):
@@ -168,7 +172,7 @@ def tile_moe_mhm_none_kernel(
 
         out_v = out.rearrange("(h p) t -> p h t", p=P)
 
-        def merge(t0, t1):
+        def merge(t0, t1, copy):
             width = t1 - t0
             acc = psum.tile([P, BANK], F32, name="bank")
             for h in range(N // P):
@@ -184,32 +188,31 @@ def tile_moe_mhm_none_kernel(
                             stop=(o == D - 1),
                         )
             staged = ring.tile([P, N // P, width], F32, name="staged")
-            nc.scalar.copy(staged[:].rearrange("p h t -> p (h t)"), acc[:, : (N // P) * width])
+            copy(staged[:].rearrange("p h t -> p (h t)"), acc[:, : (N // P) * width])
             nc.sync.dma_start(out_v[:, :, t0:t1], staged[:])
 
         for j in range(LT):
-            fetch(j, 0, 768)
-        for z in range(0, 768, P):
-            combine(z)
+            fetch(j, 0, 1024)
+            add_up(j, 0, 512)
+            add_up(j, 512, 1024)
+        for z in range(0, 1024, 256):
+            turn_back(z, z + 256)
         for j in range(LT):
-            fetch(j, 768, 1152)
-        quantize(0, 512)
-        quantize(512, 768)
-        for z in range(768, 1152, P):
-            combine(z)
+            fetch(j, 1024, 1408)
+            add_up(j, 1024, 1408)
+            if j == 2:
+                quantize(0, 512)
+        quantize(512, 1024)
+        turn_back(1024, 1280)
+        turn_back(1280, 1408)
+        merge(0, 256, nc.scalar.copy)
         for j in range(LT):
-            fetch(j, 1152, 1408)
-        quantize(768, 1024)
-        merge(0, 256)
-        for z in range(1152, 1408, P):
-            combine(z)
-        fetch(0, 1408, 1536)
-        quantize(1024, 1152)
-        merge(256, 384)
-        for j in range(1, LT):
             fetch(j, 1408, 1536)
-        quantize(1152, 1408)
-        merge(384, 640)
-        combine(1408)
+            add_up(j, 1408, 1536)
+        quantize(1024, 1280)
+        quantize(1280, 1408)
+        turn_back(1408, 1536)
+        merge(256, 512, nc.vector.tensor_copy)
+        merge(512, 640, nc.vector.tensor_copy)
         quantize(1408, 1536)
-        merge(640, 768)
+        merge(640, 768, nc.scalar.copy)

@@ -31,18 +31,17 @@ def tile_moe_mhm_none_kernel(
     nc = tc.nc
     with ExitStack() as ctx:
         keep = ctx.enter_context(tc.tile_pool(name="keep", bufs=1))
-        ring = ctx.enter_context(tc.tile_pool(name="ring", bufs=3))
-        psum = ctx.enter_context(tc.psum_pool(name="psum", bufs=8))
+        psum = ctx.enter_context(tc.psum_pool(name="psum", bufs=4))
+        psum_end = ctx.enter_context(tc.psum_pool(name="psum_end", bufs=1))
 
         offs_sb = keep.tile([P, S // PER_COL], U16, name="offs_sb")
         pos_sb = [keep.tile([P, Z // PER_COL], U16, name=f"pos_sb{r}") for r in range(2)]
-        xw = keep.tile([P, Z], U32, name="xw", align_bytes=64)
-        xs = keep.tile([P, Z], U8, name="xs", align_bytes=64)
+        xw = keep.tile([P, Z], U32, name="xw", tag="xw_then_gate", align_bytes=64)
+        xs = keep.tile([P, Z], U8, name="xs", tag="xs_then_gate", align_bytes=64)
         ws = keep.tile([P, E, H], U8, name="ws", align_bytes=64)
         wms = keep.tile([P, D, N], U8, name="wms", align_bytes=64)
         ww = [keep.tile([P, W_LOAD, 2 * H], U8, name=f"ww{i}", align_bytes=64) for i in range(E // W_LOAD)]
         wmw = keep.tile([P, D, 2 * N], U8, name="wmw", align_bytes=64)
-        gate_sb = [keep.tile([P, Z], F32, name=f"gate_sb{r}") for r in range(2)]
         ident = keep.tile([P, P], F32, name="ident")
 
         def load_scale_rows(plane, rows):
@@ -71,8 +70,6 @@ def tile_moe_mhm_none_kernel(
             )
         nc.sync.dma_start(pos_sb[0][:], pos1)
         nc.sync.dma_start(pos_sb[1][:], pos2)
-        for r in range(2):
-            nc.sync.dma_start(gate_sb[r][:], gate[r])
         load_scale_rows(wms[:], wm_scales)
         nc.sync.dma_start(wmw[:].bitcast(I32), wm_words.rearrange("o p b -> p o b").bitcast(I32))
 
@@ -101,80 +98,99 @@ def tile_moe_mhm_none_kernel(
 
         for e in range(0, E, 4):
             gather_slots(xw_slots, xw, e, e + 4)
-        for e in range(0, E - 2, 2):
-            gather_slots(xs_slots, xs, e, e + 2)
-            experts(0, e, e + 2)
-            if e < E - 4:
-                experts(1, e, e + 2)
-        for e in range(E - 2, E):
-            gather_slots(xs_slots, xs, e, e + 1)
-            experts(0, e, e + 1)
-        for e in range(E - 4, E, 2):
+        gate_first = keep.tile([P, 2, 1024], F32, name="gate_first", tag="xw_then_gate", align_bytes=64)
+        for r in range(2):
+            nc.sync.dma_start(gate_first[:, r, :], gate[r, :, :1024])
+        gather_slots(xs_slots, xs, 0, 4)
+        for j in range(2):
+            experts(j, 0, 2)
+            experts(j, 2, 4)
+        gather_slots(xs_slots, xs, 4, 8)
+        experts(0, 4, 6)
+        experts(0, 6, 8)
+        gather_slots(xs_slots, xs, 8, 11)
+        experts(0, 8, 10)
+        experts(0, 10, 11)
+        gather_slots(xs_slots, xs, 11, 12)
+        experts(0, 11, 12)
+        for e in range(4, E, 2):
             experts(1, e, e + 2)
         for j in range(2, LT):
             for e in range(0, E, 2):
                 experts(j, e, e + 2)
 
-        gated = [[keep.tile([P, Z], F32, name=f"gated{r}_{j}") for j in range(LT)] for r in range(2)]
-        grouped = keep.tile([P, Z, 4], BF16, name="grouped", align_bytes=64)
+        gate_rest = keep.tile([P, 2, 512], F32, name="gate_rest", tag="xs_then_gate", align_bytes=64)
+        nc.sync.dma_start(gate_rest[:], gate[:, :, 1024:].rearrange("r p z -> p r z"))
+
+        rounded = keep.tile([P, Z // P, 2, P, 2], BF16, name="rounded")
         c_codes = keep.tile([P, Z], U32, name="c_codes", align_bytes=64)
         c_scales = keep.tile([P, Z], U8, name="c_scales", align_bytes=64)
+        out_v = out.rearrange("(h p) t -> p h t", p=P)
 
-        def fetch(j, z0, z1):
+        def any_bank():
+            return psum.tile([P, BANK], F32, name="bank")
+
+        def end_bank(tag):
+            return psum_end.tile([P, BANK], F32, name=tag)
+
+        def fetch(gated, j, z0, z1):
+            gates = gate_first[:, :, z0:z1] if z1 <= 1024 else gate_rest[:, :, z0 - 1024 : z1 - 1024]
             for r in range(2):
                 nc.vector.tensor_tensor(
-                    gated[r][j][:, z0:z1],
+                    gated[:, r, :],
                     y[j][:].indirect(pos_sb[r][:, z0 // PER_COL : z1 // PER_COL]),
-                    gate_sb[r][:, z0:z1],
+                    gates[:, r, :],
                     MULT,
                 )
 
-        rounded = keep.tile([P, Z // P, 2, P, 2], BF16, name="rounded")
+        def add_up(total, pairs):
+            steps = [(r, b) for r in range(2) for b in range(len(pairs))]
+            for i, (r, b) in enumerate(steps):
+                nc.tensor.matmul(
+                    total[:, P * b : P * (b + 1)],
+                    lhsT=pairs[b][:, r, :],
+                    rhs=ident[:],
+                    is_transpose=True,
+                    start=(i == 0),
+                    stop=(i == len(steps) - 1),
+                )
 
-        def add_up(j, z0, z1):
-            blocks = (z1 - z0) // P
-            total = psum.tile([P, BANK], F32, name="bank")
-            for r in range(2):
-                for b in range(blocks):
-                    nc.tensor.matmul(
-                        total[:, P * b : P * (b + 1)],
-                        lhsT=gated[r][j][:, z0 + P * b : z0 + P * (b + 1)],
-                        rhs=ident[:],
-                        is_transpose=True,
-                        start=(r == 0 and b == 0),
-                        stop=(r == 1 and b == blocks - 1),
-                    )
+        def add_up_blocks(total, gated, j, z0, first, z1):
+            add_up(total, [gated[:, :, z - first : z - first + P] for z in range(z0, z1, P)])
             nc.scalar.copy(
                 rounded[:, z0 // P : z1 // P, :, 32 * j : 32 * (j + 1), :].rearrange("z b u p e -> z u b p e"),
                 total[:, : z1 - z0].rearrange("z (b p u e) -> z u b p e", p=32, u=2, e=2),
             )
 
-        def turn_back(z0, z1):
-            blocks = (z1 - z0) // P
-            back = psum.tile([P, BANK], F32, name="bank")
-            for b in range(blocks):
+        def turn_back(grouped, first, z0, z1):
+            back = any_bank()
+            for b in range((z1 - z0) // P):
                 pairs = rounded[:, z0 // P + b].rearrange("z u p e -> z (u p e)").bitcast(F32)
                 for u in range(2):
                     nc.tensor.transpose(
                         back[:, P * (2 * b + u) : P * (2 * b + u + 1)], pairs[:, P * u : P * (u + 1)], ident[:]
                     )
+            words = grouped[:, z0 - first : z1 - first, :].rearrange("p z t -> p (z t)").bitcast(F32)
             nc.scalar.copy(
-                grouped[:, z0:z1, :].rearrange("p z t -> p (z t)").bitcast(F32).rearrange("p (b z u) -> p b z u", z=P, u=2),
+                words.rearrange("p (b z u) -> p b z u", z=P, u=2),
                 back[:, : 2 * (z1 - z0)].rearrange("p (b u z) -> p b z u", u=2, z=P),
             )
 
-        def quantize(z0, z1):
+        def turned(z0, z1):
+            grouped = keep.tile([P, z1 - z0, 4], BF16, name=f"grouped{z0}", align_bytes=64)
+            for z in range(z0, z1, 2 * P):
+                turn_back(grouped, z0, z, min(z + 2 * P, z1))
+            return grouped
+
+        def quantize(grouped, z0, z1):
             nc.vector.quantize_mx(
                 out=c_codes[:, z0:z1].bitcast(FP8X4),
                 scales=c_scales[:, z0:z1],
-                in_=grouped[:, z0:z1, :].rearrange("p z t -> p (z t)"),
+                in_=grouped[:].rearrange("p z t -> p (z t)"),
             )
 
-        out_v = out.rearrange("(h p) t -> p h t", p=P)
-
-        def merge(t0, t1, copy):
+        def merge(acc, t0, t1, copy):
             width = t1 - t0
-            acc = psum.tile([P, BANK], F32, name="bank")
             for h in range(N // P):
                 for t in range(t0, t1, P):
                     for o in range(D):
@@ -187,32 +203,80 @@ def tile_moe_mhm_none_kernel(
                             start=(o == 0),
                             stop=(o == D - 1),
                         )
-            staged = ring.tile([P, N // P, width], F32, name="staged")
+            staged = keep.tile([P, N // P, width], F32, name=f"staged{t0}")
             copy(staged[:].rearrange("p h t -> p (h t)"), acc[:, : (N // P) * width])
             nc.sync.dma_start(out_v[:, :, t0:t1], staged[:])
 
+        def merge_pass(acc, h, o, t, start, stop):
+            nc.tensor.matmul_mx(
+                out=acc,
+                lhsT=wmw[:, o, 2 * P * h : 2 * P * (h + 1)].bitcast(FP4X4),
+                lhsT_scale=wms[:, o, P * h : P * (h + 1)],
+                rhs=c_codes[:, o * T + t : o * T + t + P].bitcast(FP8X4),
+                rhs_scale=c_scales[:, o * T + t : o * T + t + P],
+                start=start,
+                stop=stop,
+            )
+
         for j in range(LT):
-            fetch(j, 0, 1024)
-            add_up(j, 0, 512)
-            add_up(j, 512, 1024)
-        for z in range(0, 1024, 256):
-            turn_back(z, z + 256)
+            gated = keep.tile([P, 2, 1024], F32, name=f"gated_first{j}")
+            fetch(gated, j, 0, 1024)
+            add_up_blocks(any_bank(), gated, j, 0, 0, 512)
+            add_up_blocks(any_bank(), gated, j, 512, 0, 1024)
+        g_a = turned(0, 256)
+        g_b = turned(768, 1024)
+        g_c = turned(256, 768)
+        gated_second = keep.tile([P, LT - 1, 2, 384], F32, name="gated_second", tag="xw_then_gate", align_bytes=64)
+        for j in range(LT - 1):
+            fetch(gated_second[:, j], j, 1024, 1408)
+            add_up_blocks(any_bank(), gated_second[:, j], j, 1024, 1024, 1408)
+        quantize(g_a, 0, 256)
+        quantize(g_b, 768, 1024)
+        merge(any_bank(), 0, 256, nc.scalar.copy)
+        gated = keep.tile([P, 2, 384], F32, name="gated_second_last", tag="grouped768", align_bytes=64)
+        fetch(gated, LT - 1, 1024, 1408)
+        add_up_blocks(end_bank("end_a"), gated, LT - 1, 1024, 1024, 1408)
+        quantize(g_c, 256, 768)
+        mid = [end_bank(f"mid{h}") for h in range(2)]
+        last = end_bank("last")
+        for h in range(2):
+            for t in range(256, 640, P):
+                merge_pass(mid[h][:, t - 256 : t - 256 + P], h, 0, t, t == 256, False)
+        for h in range(2):
+            merge_pass(last[:, P * h : P * (h + 1)], h, 0, 640, h == 0, False)
+        g_d = turned(1024, 1280)
+        g_e = turned(1280, 1408)
+        gated_third = keep.tile([P, LT, 2, P], F32, name="gated_third", tag="grouped256", align_bytes=64)
         for j in range(LT):
-            fetch(j, 1024, 1408)
-            add_up(j, 1024, 1408)
-            if j == 2:
-                quantize(0, 512)
-        quantize(512, 1024)
-        turn_back(1024, 1280)
-        turn_back(1280, 1408)
-        merge(0, 256, nc.scalar.copy)
-        for j in range(LT):
-            fetch(j, 1408, 1536)
-            add_up(j, 1408, 1536)
-        quantize(1024, 1280)
-        quantize(1280, 1408)
-        turn_back(1408, 1536)
-        merge(256, 512, nc.vector.tensor_copy)
-        merge(512, 640, nc.vector.tensor_copy)
-        quantize(1408, 1536)
-        merge(640, 768, nc.scalar.copy)
+            fetch(gated_third[:, j], j, 1408, 1536)
+        total = end_bank("end_a")
+        steps = [(j, r) for j in range(LT - 1) for r in range(2)]
+        for i, (j, r) in enumerate(steps):
+            nc.tensor.matmul(
+                total[:, P * j : P * (j + 1)],
+                lhsT=gated_third[:, j, r, :],
+                rhs=ident[:],
+                is_transpose=True,
+                start=(r == 0),
+                stop=(r == 1),
+            )
+        nc.scalar.copy(
+            rounded[:, 11, :, : 32 * (LT - 1), :],
+            total[:, : P * (LT - 1)].rearrange("z (p u e) -> z u p e", u=2, e=2),
+        )
+        add_up_blocks(any_bank(), gated_third[:, LT - 1], LT - 1, 1408, 1408, 1536)
+        quantize(g_d, 1024, 1280)
+        quantize(g_e, 1280, 1408)
+        g_f = turned(1408, 1536)
+        for h in range(2):
+            for t in range(256, 640, P):
+                merge_pass(mid[h][:, t - 256 : t - 256 + P], h, 1, t, False, t == 512)
+            staged_mid = keep.tile([P, 384], F32, name=f"staged_mid{h}")
+            nc.scalar.copy(staged_mid[:], mid[h][:, :384])
+            nc.sync.dma_start(out_v[:, h, 256:640], staged_mid[:])
+        quantize(g_f, 1408, 1536)
+        for h in range(2):
+            merge_pass(last[:, P * h : P * (h + 1)], h, 1, 640, False, h == 1)
+        staged_last = keep.tile([P, 2, P], F32, name="staged_last")
+        nc.vector.tensor_copy(staged_last[:].rearrange("p h t -> p (h t)"), last[:, : 2 * P])
+        nc.sync.dma_start(out_v[:, :, 640:768], staged_last[:])

@@ -36,8 +36,8 @@ def tile_moe_mhm_none_kernel(
 
         offs_sb = keep.tile([P, S // PER_COL], U16, name="offs_sb")
         pos_sb = [keep.tile([P, Z // PER_COL], U16, name=f"pos_sb{r}") for r in range(2)]
-        xw = keep.tile([P, Z], U32, name="xw", tag="xw_then_gate", align_bytes=64)
-        xs = keep.tile([P, Z], U8, name="xs", tag="xs_then_gate", align_bytes=64)
+        xw = keep.tile([P, Z], U32, name="xw", tag="xw_then_rest", align_bytes=64)
+        xs = keep.tile([P, Z], U8, name="xs", tag="xw_then_gate", align_bytes=64)
         ws = keep.tile([P, E, H], U8, name="ws", align_bytes=64)
         wms = keep.tile([P, D, N], U8, name="wms", align_bytes=64)
         ww = [keep.tile([P, W_LOAD, 2 * H], U8, name=f"ww{i}", align_bytes=64) for i in range(E // W_LOAD)]
@@ -57,19 +57,19 @@ def tile_moe_mhm_none_kernel(
         make_identity(nc, ident[:])
 
         nc.sync.dma_start(offs_sb[:], offs)
+        nc.sync.dma_start(pos_sb[0][:], pos1)
+        nc.sync.dma_start(pos_sb[1][:], pos2)
+        load_scale_rows(xs[:].rearrange("p (o t) -> p o t", o=D), x_scales)
         nc.sync.dma_start(
             xw[:].bitcast(I32).rearrange("p (o t) -> p o t", o=D),
             x_words.rearrange("o p t d -> p o (t d)").bitcast(I32),
         )
-        load_scale_rows(xs[:].rearrange("p (o t) -> p o t", o=D), x_scales)
         load_scale_rows(ws[:], w_scales[:, 0])
         for i in range(E // W_LOAD):
             nc.sync.dma_start(
                 ww[i][:].bitcast(I32),
                 w_words[W_LOAD * i : W_LOAD * (i + 1), 0].rearrange("e p b -> p e b").bitcast(I32),
             )
-        nc.sync.dma_start(pos_sb[0][:], pos1)
-        nc.sync.dma_start(pos_sb[1][:], pos2)
         load_scale_rows(wms[:], wm_scales)
         nc.sync.dma_start(wmw[:].bitcast(I32), wm_words.rearrange("o p b -> p o b").bitcast(I32))
 
@@ -97,21 +97,21 @@ def tile_moe_mhm_none_kernel(
             nc.scalar.copy(y[j][:, e0 * C : e1 * C], bank[:, : (e1 - e0) * C])
 
         for e in range(0, E, 4):
-            gather_slots(xw_slots, xw, e, e + 4)
+            gather_slots(xs_slots, xs, e, e + 4)
         gate_first = keep.tile([P, 2, 1024], F32, name="gate_first", tag="xw_then_gate", align_bytes=64)
         for r in range(2):
             nc.sync.dma_start(gate_first[:, r, :], gate[r, :, :1024])
-        gather_slots(xs_slots, xs, 0, 4)
+        gather_slots(xw_slots, xw, 0, 4)
         for j in range(2):
             experts(j, 0, 2)
             experts(j, 2, 4)
-        gather_slots(xs_slots, xs, 4, 8)
+        gather_slots(xw_slots, xw, 4, 8)
         experts(0, 4, 6)
         experts(0, 6, 8)
-        gather_slots(xs_slots, xs, 8, 11)
+        gather_slots(xw_slots, xw, 8, 11)
         experts(0, 8, 10)
         experts(0, 10, 11)
-        gather_slots(xs_slots, xs, 11, 12)
+        gather_slots(xw_slots, xw, 11, 12)
         experts(0, 11, 12)
         for e in range(4, E, 2):
             experts(1, e, e + 2)
@@ -119,7 +119,7 @@ def tile_moe_mhm_none_kernel(
             for e in range(0, E, 2):
                 experts(j, e, e + 2)
 
-        gate_rest = keep.tile([P, 2, 512], F32, name="gate_rest", tag="xs_then_gate", align_bytes=64)
+        gate_rest = keep.tile([P, 2, 512], F32, name="gate_rest", tag="xw_then_rest", align_bytes=64)
         nc.sync.dma_start(gate_rest[:], gate[:, :, 1024:].rearrange("r p z -> p r z"))
 
         rounded = keep.tile([P, Z // P, 2, P, 2], BF16, name="rounded")

@@ -23,6 +23,7 @@ LT = H // P
 BANK = 512
 PER_COL = 16
 W_LOAD = 4
+XS_COLS = 2048
 
 
 def tile_moe_mhm_none_kernel(
@@ -37,21 +38,22 @@ def tile_moe_mhm_none_kernel(
         offs_sb = keep.tile([P, S // PER_COL], U16, name="offs_sb")
         pos_sb = [keep.tile([P, Z // PER_COL], U16, name=f"pos_sb{r}") for r in range(2)]
         xw = keep.tile([P, Z], U32, name="xw", tag="xw_then_rest", align_bytes=64)
-        xs = keep.tile([P, Z], U8, name="xs", tag="xw_then_gate", align_bytes=64)
+        xs = keep.tile([P, XS_COLS], U8, name="xs", tag="xw_then_gate", align_bytes=64)
         ws = keep.tile([P, E, H], U8, name="ws", align_bytes=64)
         wms = keep.tile([P, D, N], U8, name="wms", align_bytes=64)
         ww = [keep.tile([P, W_LOAD, 2 * H], U8, name=f"ww{i}", align_bytes=64) for i in range(E // W_LOAD)]
         wmw = keep.tile([P, D, 2 * N], U8, name="wmw", align_bytes=64)
         ident = keep.tile([P, P], F32, name="ident")
 
-        def load_scale_rows(plane, rows):
+        def load_scale_rows(plane, rows, queues=(nc.sync,)):
             for q in range(4):
-                nc.sync.dma_start(
+                queues[q % len(queues)].dma_start(
                     plane[32 * q : 32 * q + 4].bitcast(I32),
                     rows[:, 4 * q : 4 * q + 4, :].rearrange("a r c -> r a c").bitcast(I32),
                 )
 
-        nc.vector.memset(xs[:].bitcast(I32), 0)
+        nc.vector.memset(xs[:, :Z].bitcast(I32), 0)
+        nc.vector.memset(xs[:, Z:].bitcast(I32), 0)
         nc.vector.memset(ws[:].rearrange("p e l -> p (e l)").bitcast(I32), 0)
         nc.vector.memset(wms[:].rearrange("p o n -> p (o n)").bitcast(I32), 0)
         make_identity(nc, ident[:])
@@ -59,7 +61,7 @@ def tile_moe_mhm_none_kernel(
         nc.sync.dma_start(offs_sb[:], offs)
         nc.sync.dma_start(pos_sb[0][:], pos1)
         nc.sync.dma_start(pos_sb[1][:], pos2)
-        load_scale_rows(xs[:].rearrange("p (o t) -> p o t", o=D), x_scales)
+        load_scale_rows(xs[:, :Z].rearrange("p (o t) -> p o t", o=D), x_scales, (nc.sync, nc.scalar))
         nc.sync.dma_start(
             xw[:].bitcast(I32).rearrange("p (o t) -> p o t", o=D),
             x_words.rearrange("o p t d -> p o (t d)").bitcast(I32),
@@ -82,22 +84,28 @@ def tile_moe_mhm_none_kernel(
 
         y = [keep.tile([P, S], F32, name=f"y{j}") for j in range(LT)]
 
-        def experts(j, e0, e1):
-            bank = psum.tile([P, BANK], F32, name="bank")
-            for e in range(e0, e1):
+        def multiply(bank, j, s0, s1):
+            step = min(C, s1 - s0)
+            for s in range(s0, s1, step):
+                e = s // C
                 nc.tensor.matmul_mx(
-                    out=bank[:, (e - e0) * C : (e - e0 + 1) * C],
+                    out=bank[:, s - s0 : s - s0 + step],
                     lhsT=ww[e // W_LOAD][:, e % W_LOAD, 2 * P * j : 2 * P * (j + 1)].bitcast(FP4X4),
                     lhsT_scale=ws[:, e, P * j : P * (j + 1)],
-                    rhs=xw_slots[:, e * C : (e + 1) * C].bitcast(FP8X4),
-                    rhs_scale=xs_slots[:, e * C : (e + 1) * C],
+                    rhs=xw_slots[:, s : s + step].bitcast(FP8X4),
+                    rhs_scale=xs_slots[:, s : s + step],
                     start=True,
                     stop=True,
                 )
-            nc.scalar.copy(y[j][:, e0 * C : e1 * C], bank[:, : (e1 - e0) * C])
+            return bank
 
-        for e in range(0, E, 4):
-            gather_slots(xs_slots, xs, e, e + 4)
+        def experts(j, e0, e1, copy=nc.scalar.copy):
+            s0, s1 = int(e0 * C), int(e1 * C)
+            bank = multiply(psum.tile([P, BANK], F32, name="bank"), j, s0, s1)
+            copy(y[j][:, s0:s1], bank[:, : s1 - s0])
+
+        for e in range(0, E, 6):
+            gather_slots(xs_slots, xs, e, e + 6)
         gate_first = keep.tile([P, 2, 1024], F32, name="gate_first", tag="xw_then_gate", align_bytes=64)
         for r in range(2):
             nc.sync.dma_start(gate_first[:, r, :], gate[r, :, :1024])
@@ -108,11 +116,13 @@ def tile_moe_mhm_none_kernel(
         gather_slots(xw_slots, xw, 4, 8)
         experts(0, 4, 6)
         experts(0, 6, 8)
-        gather_slots(xw_slots, xw, 8, 11)
+        gather_slots(xw_slots, xw, 8, 10)
         experts(0, 8, 10)
+        gather_slots(xw_slots, xw, 10, 11)
         experts(0, 10, 11)
         gather_slots(xw_slots, xw, 11, 12)
-        experts(0, 11, 12)
+        experts(0, 11, 11.5)
+        experts(0, 11.5, 12, nc.vector.tensor_copy)
         for e in range(4, E, 2):
             experts(1, e, e + 2)
         for j in range(2, LT):
@@ -122,7 +132,12 @@ def tile_moe_mhm_none_kernel(
         gate_rest = keep.tile([P, 2, 512], F32, name="gate_rest", tag="xw_then_rest", align_bytes=64)
         nc.sync.dma_start(gate_rest[:], gate[:, :, 1024:].rearrange("r p z -> p r z"))
 
-        rounded = keep.tile([P, Z // P, 2, P, 2], BF16, name="rounded")
+        rounded = keep.tile([P, Z // P - 1, 2, P, 2], BF16, name="rounded")
+        rounded_last = keep.tile([P, 1, 2, P, 2], BF16, name="rounded_last", tag="rounded_last", align_bytes=64)
+
+        def rounded_blocks(b0, b1):
+            return rounded[:, b0:b1] if b1 < Z // P else rounded_last[:, :]
+
         c_codes = keep.tile([P, Z], U32, name="c_codes", align_bytes=64)
         c_scales = keep.tile([P, Z], U8, name="c_scales", align_bytes=64)
         out_v = out.rearrange("(h p) t -> p h t", p=P)
@@ -158,14 +173,14 @@ def tile_moe_mhm_none_kernel(
         def add_up_blocks(total, gated, j, z0, first, z1):
             add_up(total, [gated[:, :, z - first : z - first + P] for z in range(z0, z1, P)])
             nc.scalar.copy(
-                rounded[:, z0 // P : z1 // P, :, 32 * j : 32 * (j + 1), :].rearrange("z b u p e -> z u b p e"),
+                rounded_blocks(z0 // P, z1 // P)[:, :, :, 32 * j : 32 * (j + 1), :].rearrange("z b u p e -> z u b p e"),
                 total[:, : z1 - z0].rearrange("z (b p u e) -> z u b p e", p=32, u=2, e=2),
             )
 
         def turn_back(grouped, first, z0, z1):
             back = any_bank()
             for b in range((z1 - z0) // P):
-                pairs = rounded[:, z0 // P + b].rearrange("z u p e -> z (u p e)").bitcast(F32)
+                pairs = rounded_blocks(z0 // P + b, z0 // P + b + 1)[:, 0].rearrange("z u p e -> z (u p e)").bitcast(F32)
                 for u in range(2):
                     nc.tensor.transpose(
                         back[:, P * (2 * b + u) : P * (2 * b + u + 1)], pairs[:, P * u : P * (u + 1)], ident[:]
@@ -182,9 +197,9 @@ def tile_moe_mhm_none_kernel(
                 turn_back(grouped, z0, z, min(z + 2 * P, z1))
             return grouped
 
-        def quantize(grouped, z0, z1):
+        def quantize(grouped, z0, z1, codes=c_codes, first=0):
             nc.vector.quantize_mx(
-                out=c_codes[:, z0:z1].bitcast(FP8X4),
+                out=codes[:, z0 - first : z1 - first].bitcast(FP8X4),
                 scales=c_scales[:, z0:z1],
                 in_=grouped[:].rearrange("p z t -> p (z t)"),
             )
@@ -207,12 +222,12 @@ def tile_moe_mhm_none_kernel(
             copy(staged[:].rearrange("p h t -> p (h t)"), acc[:, : (N // P) * width])
             nc.sync.dma_start(out_v[:, :, t0:t1], staged[:])
 
-        def merge_pass(acc, h, o, t, start, stop):
+        def merge_pass(acc, h, o, t, start, stop, codes=c_codes, first=0):
             nc.tensor.matmul_mx(
                 out=acc,
                 lhsT=wmw[:, o, 2 * P * h : 2 * P * (h + 1)].bitcast(FP4X4),
                 lhsT_scale=wms[:, o, P * h : P * (h + 1)],
-                rhs=c_codes[:, o * T + t : o * T + t + P].bitcast(FP8X4),
+                rhs=codes[:, o * T + t - first : o * T + t - first + P].bitcast(FP8X4),
                 rhs_scale=c_scales[:, o * T + t : o * T + t + P],
                 start=start,
                 stop=stop,
@@ -237,13 +252,15 @@ def tile_moe_mhm_none_kernel(
         fetch(gated, LT - 1, 1024, 1408)
         add_up_blocks(end_bank("end_a"), gated, LT - 1, 1024, 1024, 1408)
         quantize(g_c, 256, 768)
-        mid = [end_bank(f"mid{h}") for h in range(2)]
+        acc_d = end_bank("acc_d")
+        acc_e = end_bank("acc_e")
         last = end_bank("last")
         for h in range(2):
-            for t in range(256, 640, P):
-                merge_pass(mid[h][:, t - 256 : t - 256 + P], h, 0, t, t == 256, False)
+            for t in (256, 384):
+                merge_pass(acc_d[:, 256 * h + t - 256 : 256 * h + t - 256 + P], h, 0, t, h == 0 and t == 256, False)
         for h in range(2):
-            merge_pass(last[:, P * h : P * (h + 1)], h, 0, 640, h == 0, False)
+            merge_pass(acc_e[:, P * h : P * (h + 1)], h, 0, 512, h == 0, False)
+        merge_pass(last[:, :P], 0, 0, 640, True, False)
         g_d = turned(1024, 1280)
         g_e = turned(1280, 1408)
         gated_third = keep.tile([P, LT, 2, P], F32, name="gated_third", tag="grouped256", align_bytes=64)
@@ -261,22 +278,31 @@ def tile_moe_mhm_none_kernel(
                 stop=(r == 1),
             )
         nc.scalar.copy(
-            rounded[:, 11, :, : 32 * (LT - 1), :],
+            rounded_last[:, 0, :, : 32 * (LT - 1), :],
             total[:, : P * (LT - 1)].rearrange("z (p u e) -> z u p e", u=2, e=2),
         )
         add_up_blocks(any_bank(), gated_third[:, LT - 1], LT - 1, 1408, 1408, 1536)
         quantize(g_d, 1024, 1280)
-        quantize(g_e, 1280, 1408)
         g_f = turned(1408, 1536)
         for h in range(2):
-            for t in range(256, 640, P):
-                merge_pass(mid[h][:, t - 256 : t - 256 + P], h, 1, t, False, t == 512)
-            staged_mid = keep.tile([P, 384], F32, name=f"staged_mid{h}")
-            nc.scalar.copy(staged_mid[:], mid[h][:, :384])
-            nc.sync.dma_start(out_v[:, h, 256:640], staged_mid[:])
-        quantize(g_f, 1408, 1536)
+            for t in (256, 384):
+                merge_pass(acc_d[:, 256 * h + t - 256 : 256 * h + t - 256 + P], h, 1, t, False, h == 1 and t == 384)
+        staged_d = keep.tile([P, 2, 256], F32, name="staged_d")
+        nc.vector.tensor_copy(staged_d[:].rearrange("p h t -> p (h t)"), acc_d[:])
+        nc.sync.dma_start(out_v[:, :, 256:512], staged_d[:])
+        codes_e = keep.tile([P, P], U32, name="codes_e", tag="rounded_last", align_bytes=64)
+        quantize(g_e, 1280, 1408, codes_e, 1280)
+        last_b = end_bank("end_a")
+        merge_pass(last_b[:, :P], 1, 0, 640, True, False)
         for h in range(2):
-            merge_pass(last[:, P * h : P * (h + 1)], h, 1, 640, False, h == 1)
+            merge_pass(acc_e[:, P * h : P * (h + 1)], h, 1, 512, False, h == 1, codes_e, 1280)
+        quantize(g_f, 1408, 1536)
+        merge_pass(last[:, :P], 0, 1, 640, False, True)
+        merge_pass(last_b[:, :P], 1, 1, 640, False, True)
+        staged_e = keep.tile([P, 2, P], F32, name="staged_e")
+        nc.scalar.copy(staged_e[:].rearrange("p h t -> p (h t)"), acc_e[:, : 2 * P])
+        nc.sync.dma_start(out_v[:, :, 512:640], staged_e[:])
         staged_last = keep.tile([P, 2, P], F32, name="staged_last")
-        nc.vector.tensor_copy(staged_last[:].rearrange("p h t -> p (h t)"), last[:, : 2 * P])
+        nc.scalar.copy(staged_last[:, 0, :], last[:, :P])
+        nc.vector.tensor_copy(staged_last[:, 1, :], last_b[:, :P])
         nc.sync.dma_start(out_v[:, :, 640:768], staged_last[:])

@@ -32,22 +32,23 @@ def tile_moe_mhm_none_kernel(
     nc = tc.nc
     with ExitStack() as ctx:
         keep = ctx.enter_context(tc.tile_pool(name="keep", bufs=1))
+        shared = ctx.enter_context(tc.tile_pool(name="shared", bufs=1))
         psum = ctx.enter_context(tc.psum_pool(name="psum", bufs=4))
         psum_end = ctx.enter_context(tc.psum_pool(name="psum_end", bufs=1))
 
         offs_sb = keep.tile([P, S // PER_COL], U16, name="offs_sb")
         pos_sb = [keep.tile([P, Z // PER_COL], U16, name=f"pos_sb{r}") for r in range(2)]
         xw = keep.tile([P, Z], U32, name="xw", tag="xw_then_rest", align_bytes=64)
-        xs = keep.tile([P, XS_COLS], U8, name="xs", tag="xw_then_gate", align_bytes=64)
+        xs = shared.tile([P, XS_COLS], U8, name="xs", offset=8192)
         ws = keep.tile([P, E, H], U8, name="ws", align_bytes=64)
         wms = keep.tile([P, D, N], U8, name="wms", align_bytes=64)
         ww = [keep.tile([P, W_LOAD, 2 * H], U8, name=f"ww{i}", align_bytes=64) for i in range(E // W_LOAD)]
         wmw = keep.tile([P, D, 2 * N], U8, name="wmw", align_bytes=64)
         ident = keep.tile([P, P], F32, name="ident")
 
-        def load_scale_rows(plane, rows, queues=(nc.sync,)):
+        def load_scale_rows(plane, rows):
             for q in range(4):
-                queues[q % len(queues)].dma_start(
+                nc.sync.dma_start(
                     plane[32 * q : 32 * q + 4].bitcast(I32),
                     rows[:, 4 * q : 4 * q + 4, :].rearrange("a r c -> r a c").bitcast(I32),
                 )
@@ -61,7 +62,7 @@ def tile_moe_mhm_none_kernel(
         nc.sync.dma_start(offs_sb[:], offs)
         nc.sync.dma_start(pos_sb[0][:], pos1)
         nc.sync.dma_start(pos_sb[1][:], pos2)
-        load_scale_rows(xs[:, :Z].rearrange("p (o t) -> p o t", o=D), x_scales, (nc.sync, nc.scalar))
+        load_scale_rows(xs[:, :Z].rearrange("p (o t) -> p o t", o=D), x_scales)
         nc.sync.dma_start(
             xw[:].bitcast(I32).rearrange("p (o t) -> p o t", o=D),
             x_words.rearrange("o p t d -> p o (t d)").bitcast(I32),
@@ -106,9 +107,9 @@ def tile_moe_mhm_none_kernel(
 
         for e in range(0, E, 6):
             gather_slots(xs_slots, xs, e, e + 6)
-        gate_first = keep.tile([P, 2, 1024], F32, name="gate_first", tag="xw_then_gate", align_bytes=64)
+        gate_first = [shared.tile([P, 1024], F32, name=f"gate_first{r}", offset=5120 + 4096 * r) for r in range(2)]
         for r in range(2):
-            nc.sync.dma_start(gate_first[:, r, :], gate[r, :, :1024])
+            nc.sync.dma_start(gate_first[r][:], gate[r, :, :1024])
         gather_slots(xw_slots, xw, 0, 4)
         for j in range(2):
             experts(j, 0, 2)
@@ -132,11 +133,15 @@ def tile_moe_mhm_none_kernel(
         gate_rest = keep.tile([P, 2, 512], F32, name="gate_rest", tag="xw_then_rest", align_bytes=64)
         nc.sync.dma_start(gate_rest[:], gate[:, :, 1024:].rearrange("r p z -> p r z"))
 
-        rounded = keep.tile([P, Z // P - 1, 2, P, 2], BF16, name="rounded")
-        rounded_last = keep.tile([P, 1, 2, P, 2], BF16, name="rounded_last", tag="rounded_last", align_bytes=64)
+        cuts = (0, 4, 8, 11, 12)
+        rounded = [
+            keep.tile([P, b - a, 2, P, 2], BF16, name=f"rounded{a}", align_bytes=64) for a, b in zip(cuts, cuts[1:])
+        ]
+        rounded_last = rounded[-1]
 
         def rounded_blocks(b0, b1):
-            return rounded[:, b0:b1] if b1 < Z // P else rounded_last[:, :]
+            i = max(k for k in range(4) if cuts[k] <= b0)
+            return rounded[i][:, b0 - cuts[i] : b1 - cuts[i]]
 
         c_codes = keep.tile([P, Z], U32, name="c_codes", align_bytes=64)
         c_scales = keep.tile([P, Z], U8, name="c_scales", align_bytes=64)
@@ -149,12 +154,11 @@ def tile_moe_mhm_none_kernel(
             return psum_end.tile([P, BANK], F32, name=tag)
 
         def fetch(gated, j, z0, z1):
-            gates = gate_first[:, :, z0:z1] if z1 <= 1024 else gate_rest[:, :, z0 - 1024 : z1 - 1024]
             for r in range(2):
                 nc.vector.tensor_tensor(
                     gated[:, r, :],
                     y[j][:].indirect(pos_sb[r][:, z0 // PER_COL : z1 // PER_COL]),
-                    gates[:, r, :],
+                    gate_first[r][:, z0:z1] if z1 <= 1024 else gate_rest[:, r, z0 - 1024 : z1 - 1024],
                     MULT,
                 )
 
@@ -204,7 +208,7 @@ def tile_moe_mhm_none_kernel(
                 in_=grouped[:].rearrange("p z t -> p (z t)"),
             )
 
-        def merge(acc, t0, t1, copy):
+        def merge(acc, t0, t1, copy, codes):
             width = t1 - t0
             for h in range(N // P):
                 for t in range(t0, t1, P):
@@ -213,7 +217,7 @@ def tile_moe_mhm_none_kernel(
                             out=acc[:, h * width + t - t0 : h * width + t - t0 + P],
                             lhsT=wmw[:, o, 2 * P * h : 2 * P * (h + 1)].bitcast(FP4X4),
                             lhsT_scale=wms[:, o, P * h : P * (h + 1)],
-                            rhs=c_codes[:, o * T + t : o * T + t + P].bitcast(FP8X4),
+                            rhs=codes[:, o * 256 + t : o * 256 + t + P].bitcast(FP8X4),
                             rhs_scale=c_scales[:, o * T + t : o * T + t + P],
                             start=(o == 0),
                             stop=(o == D - 1),
@@ -241,14 +245,15 @@ def tile_moe_mhm_none_kernel(
         g_a = turned(0, 256)
         g_b = turned(768, 1024)
         g_c = turned(256, 768)
-        gated_second = keep.tile([P, LT - 1, 2, 384], F32, name="gated_second", tag="xw_then_gate", align_bytes=64)
+        gated_second = shared.tile([P, LT - 1, 2, 384], F32, name="gated_second", offset=0)
         for j in range(LT - 1):
             fetch(gated_second[:, j], j, 1024, 1408)
             add_up_blocks(any_bank(), gated_second[:, j], j, 1024, 1024, 1408)
-        quantize(g_a, 0, 256)
-        quantize(g_b, 768, 1024)
-        merge(any_bank(), 0, 256, nc.scalar.copy)
-        gated = keep.tile([P, 2, 384], F32, name="gated_second_last", tag="grouped768", align_bytes=64)
+        codes_ab = keep.tile([P, 512], U32, name="codes_ab", align_bytes=64)
+        quantize(g_a, 0, 256, codes_ab, 0)
+        quantize(g_b, 768, 1024, codes_ab, 512)
+        merge(any_bank(), 0, 256, nc.scalar.copy, codes_ab)
+        gated = keep.tile([P, 2, 384], F32, name="gated_second_last", tag="rounded4", align_bytes=64)
         fetch(gated, LT - 1, 1024, 1408)
         add_up_blocks(end_bank("end_a"), gated, LT - 1, 1024, 1024, 1408)
         quantize(g_c, 256, 768)
@@ -263,7 +268,7 @@ def tile_moe_mhm_none_kernel(
         merge_pass(last[:, :P], 0, 0, 640, True, False)
         g_d = turned(1024, 1280)
         g_e = turned(1280, 1408)
-        gated_third = keep.tile([P, LT, 2, P], F32, name="gated_third", tag="grouped256", align_bytes=64)
+        gated_third = keep.tile([P, LT, 2, P], F32, name="gated_third", tag="codes_ab", align_bytes=64)
         for j in range(LT):
             fetch(gated_third[:, j], j, 1408, 1536)
         total = end_bank("end_a")
@@ -290,7 +295,7 @@ def tile_moe_mhm_none_kernel(
         staged_d = keep.tile([P, 2, 256], F32, name="staged_d")
         nc.vector.tensor_copy(staged_d[:].rearrange("p h t -> p (h t)"), acc_d[:])
         nc.sync.dma_start(out_v[:, :, 256:512], staged_d[:])
-        codes_e = keep.tile([P, P], U32, name="codes_e", tag="rounded_last", align_bytes=64)
+        codes_e = keep.tile([P, P], U32, name="codes_e", tag="rounded11", align_bytes=64)
         quantize(g_e, 1280, 1408, codes_e, 1280)
         last_b = end_bank("end_a")
         merge_pass(last_b[:, :P], 1, 0, 640, True, False)

@@ -244,7 +244,8 @@ def tile_moe_mhm_none_kernel(
             add_up_blocks(any_bank(), gated, j, 512, 0, 1024)
         g_a = turned(0, 256)
         g_b = turned(768, 1024)
-        g_c = turned(256, 768)
+        g_c = turned(256, 512)
+        g_c2 = turned(512, 768)
         gated_second = shared.tile([P, LT - 1, 2, 384], F32, name="gated_second", offset=0)
         for j in range(LT - 1):
             fetch(gated_second[:, j], j, 1024, 1408)
@@ -256,16 +257,13 @@ def tile_moe_mhm_none_kernel(
         gated = keep.tile([P, 2, 384], F32, name="gated_second_last", tag="rounded4", align_bytes=64)
         fetch(gated, LT - 1, 1024, 1408)
         add_up_blocks(end_bank("end_a"), gated, LT - 1, 1024, 1024, 1408)
-        quantize(g_c, 256, 768)
+        quantize(g_c, 256, 512)
         acc_d = end_bank("acc_d")
         acc_e = end_bank("acc_e")
         last = end_bank("last")
         for h in range(2):
             for t in (256, 384):
                 merge_pass(acc_d[:, 256 * h + t - 256 : 256 * h + t - 256 + P], h, 0, t, h == 0 and t == 256, False)
-        for h in range(2):
-            merge_pass(acc_e[:, P * h : P * (h + 1)], h, 0, 512, h == 0, False)
-        merge_pass(last[:, :P], 0, 0, 640, True, False)
         g_d = turned(1024, 1280)
         g_e = turned(1280, 1408)
         gated_third = keep.tile([P, LT, 2, P], F32, name="gated_third", tag="codes_ab", align_bytes=64)
@@ -292,13 +290,18 @@ def tile_moe_mhm_none_kernel(
         for h in range(2):
             for t in (256, 384):
                 merge_pass(acc_d[:, 256 * h + t - 256 : 256 * h + t - 256 + P], h, 1, t, False, h == 1 and t == 384)
+        codes_c2 = keep.tile([P, 256], U32, name="codes_c2", tag="codes_ab", align_bytes=64)
+        quantize(g_c2, 512, 768, codes_c2, 512)
+        for h in range(2):
+            merge_pass(acc_e[:, P * h : P * (h + 1)], h, 0, 512, h == 0, False, codes_c2, 512)
+        merge_pass(last[:, :P], 0, 0, 640, True, False, codes_c2, 512)
         staged_d = keep.tile([P, 2, 256], F32, name="staged_d")
         nc.vector.tensor_copy(staged_d[:].rearrange("p h t -> p (h t)"), acc_d[:])
         nc.sync.dma_start(out_v[:, :, 256:512], staged_d[:])
         codes_e = keep.tile([P, P], U32, name="codes_e", tag="rounded11", align_bytes=64)
         quantize(g_e, 1280, 1408, codes_e, 1280)
         last_b = end_bank("end_a")
-        merge_pass(last_b[:, :P], 1, 0, 640, True, False)
+        merge_pass(last_b[:, :P], 1, 0, 640, True, False, codes_c2, 512)
         for h in range(2):
             merge_pass(acc_e[:, P * h : P * (h + 1)], h, 1, 512, False, h == 1, codes_e, 1280)
         quantize(g_f, 1408, 1536)

@@ -38,12 +38,10 @@ def tile_moe_mhm_none_kernel(
 
         offs_sb = keep.tile([P, S // PER_COL], U16, name="offs_sb")
         pos_sb = [keep.tile([P, Z // PER_COL], U16, name=f"pos_sb{r}") for r in range(2)]
-        xw = keep.tile([P, Z], U32, name="xw", tag="xw_then_rest", align_bytes=64)
+        xw = shared.tile([P, Z], U32, name="xw", offset=13312)
         xs = shared.tile([P, XS_COLS], U8, name="xs", offset=8192)
         ws = keep.tile([P, E, H], U8, name="ws", align_bytes=64)
-        wms = keep.tile([P, D, N], U8, name="wms", align_bytes=64)
         ww = [keep.tile([P, W_LOAD, 2 * H], U8, name=f"ww{i}", align_bytes=64) for i in range(E // W_LOAD)]
-        wmw = keep.tile([P, D, 2 * N], U8, name="wmw", align_bytes=64)
         ident = keep.tile([P, P], F32, name="ident")
 
         def load_scale_rows(plane, rows):
@@ -53,31 +51,34 @@ def tile_moe_mhm_none_kernel(
                     rows[:, 4 * q : 4 * q + 4, :].rearrange("a r c -> r a c").bitcast(I32),
                 )
 
-        nc.vector.memset(xs[:, :Z].bitcast(I32), 0)
+        nc.vector.memset(xs[:96, :Z].bitcast(I32), 0)
         nc.vector.memset(xs[:, Z:].bitcast(I32), 0)
         nc.vector.memset(ws[:].rearrange("p e l -> p (e l)").bitcast(I32), 0)
-        nc.vector.memset(wms[:].rearrange("p o n -> p (o n)").bitcast(I32), 0)
+        xs_slots = keep.tile([P, S], U8, name="xs_slots", align_bytes=64)
+        nc.gpsimd.memset(xs_slots[:].bitcast(I32), 0)
         make_identity(nc, ident[:])
 
+        for half in range(2):
+            nc.sync.dma_start(
+                xs[96 + 16 * half : 112 + 16 * half, :Z].bitcast(I32).rearrange("p (o t) -> p o t", o=D),
+                x_scales.rearrange("o b t -> b o t").bitcast(I32),
+            )
         nc.sync.dma_start(offs_sb[:], offs)
-        nc.sync.dma_start(pos_sb[0][:], pos1)
-        nc.sync.dma_start(pos_sb[1][:], pos2)
-        load_scale_rows(xs[:, :Z].rearrange("p (o t) -> p o t", o=D), x_scales)
         nc.sync.dma_start(
             xw[:].bitcast(I32).rearrange("p (o t) -> p o t", o=D),
             x_words.rearrange("o p t d -> p o (t d)").bitcast(I32),
         )
+        nc.sync.dma_start(pos_sb[0][:], pos1)
+        nc.sync.dma_start(pos_sb[1][:], pos2)
         load_scale_rows(ws[:], w_scales[:, 0])
         for i in range(E // W_LOAD):
             nc.sync.dma_start(
                 ww[i][:].bitcast(I32),
                 w_words[W_LOAD * i : W_LOAD * (i + 1), 0].rearrange("e p b -> p e b").bitcast(I32),
             )
-        load_scale_rows(wms[:], wm_scales)
-        nc.sync.dma_start(wmw[:].bitcast(I32), wm_words.rearrange("o p b -> p o b").bitcast(I32))
 
         xw_slots = keep.tile([P, S], U32, name="xw_slots", align_bytes=64)
-        xs_slots = keep.tile([P, S], U8, name="xs_slots", align_bytes=64)
+        xs_rows = keep.tile([P, S], U8, name="xs_rows", align_bytes=64)
 
         def gather_slots(dst, window, e0, e1):
             cols = slice(e0 * C // PER_COL, e1 * C // PER_COL)
@@ -106,7 +107,12 @@ def tile_moe_mhm_none_kernel(
             copy(y[j][:, s0:s1], bank[:, : s1 - s0])
 
         for e in range(0, E, 6):
-            gather_slots(xs_slots, xs, e, e + 6)
+            gather_slots(xs_rows, xs, e, e + 6)
+            for q in range(4):
+                nc.scalar.dma_start(
+                    xs_slots[32 * q : 32 * q + 4, e * C : (e + 6) * C].bitcast(I32),
+                    xs_rows[96 + 16 * (e // 6) + 4 * q : 100 + 16 * (e // 6) + 4 * q, e * C : (e + 6) * C].bitcast(I32),
+                )
         gate_first = [shared.tile([P, 1024], F32, name=f"gate_first{r}", offset=5120 + 4096 * r) for r in range(2)]
         for r in range(2):
             nc.sync.dma_start(gate_first[r][:], gate[r, :, :1024])
@@ -130,8 +136,13 @@ def tile_moe_mhm_none_kernel(
             for e in range(0, E, 2):
                 experts(j, e, e + 2)
 
-        gate_rest = keep.tile([P, 2, 512], F32, name="gate_rest", tag="xw_then_rest", align_bytes=64)
+        gate_rest = shared.tile([P, 2, 512], F32, name="gate_rest", offset=13312)
         nc.sync.dma_start(gate_rest[:], gate[:, :, 1024:].rearrange("r p z -> p r z"))
+        wmw = shared.tile([P, D, 2 * N], U8, name="wmw", offset=17408, align_bytes=64)
+        wms = shared.tile([P, D, N], U8, name="wms", offset=18432, align_bytes=64)
+        nc.gpsimd.memset(wms[:].rearrange("p o n -> p (o n)").bitcast(I32), 0)
+        nc.sync.dma_start(wmw[:].bitcast(I32), wm_words.rearrange("o p b -> p o b").bitcast(I32))
+        load_scale_rows(wms[:], wm_scales)
 
         cuts = (0, 4, 8, 11, 12)
         rounded = [

@@ -39,7 +39,7 @@ def tile_moe_mhm_none_kernel(
         offs_sb = keep.tile([P, S // PER_COL], U16, name="offs_sb")
         pos_sb = [keep.tile([P, Z // PER_COL], U16, name=f"pos_sb{r}") for r in range(2)]
         xw = shared.tile([P, Z], U32, name="xw", offset=13312)
-        xs = shared.tile([P, XS_COLS], U8, name="xs", offset=8192)
+        xs = keep.tile([P, XS_COLS], U8, name="xs", align_bytes=64)
         ws = keep.tile([P, E, H], U8, name="ws", align_bytes=64)
         ww = [keep.tile([P, W_LOAD, 2 * H], U8, name=f"ww{i}", align_bytes=64) for i in range(E // W_LOAD)]
         ident = keep.tile([P, P], F32, name="ident")
@@ -55,7 +55,7 @@ def tile_moe_mhm_none_kernel(
         nc.vector.memset(xs[:, Z:].bitcast(I32), 0)
         nc.vector.memset(ws[:].rearrange("p e l -> p (e l)").bitcast(I32), 0)
         xs_slots = keep.tile([P, S], U8, name="xs_slots", align_bytes=64)
-        nc.gpsimd.memset(xs_slots[:].bitcast(I32), 0)
+        nc.vector.memset(xs_slots[:].bitcast(I32), 0)
         make_identity(nc, ident[:])
 
         for half in range(2):
@@ -78,7 +78,7 @@ def tile_moe_mhm_none_kernel(
             )
 
         xw_slots = keep.tile([P, S], U32, name="xw_slots", align_bytes=64)
-        xs_rows = keep.tile([P, S], U8, name="xs_rows", align_bytes=64)
+        xs_rows = shared.tile([P, S], U8, name="xs_rows", offset=7680)
 
         def gather_slots(dst, window, e0, e1):
             cols = slice(e0 * C // PER_COL, e1 * C // PER_COL)

@@ -173,27 +173,40 @@ def tile_moe_mhm_none_kernel(
                     MULT,
                 )
 
-        def add_up(total, pairs):
-            steps = [(r, b) for r in range(2) for b in range(len(pairs))]
-            for i, (r, b) in enumerate(steps):
-                nc.tensor.matmul(
-                    total[:, P * b : P * (b + 1)],
-                    lhsT=pairs[b][:, r, :],
-                    rhs=ident[:],
-                    is_transpose=True,
-                    start=(i == 0),
-                    stop=(i == len(steps) - 1),
-                )
+        def warm_up(bank):
+            nc.tensor.matmul_mx(
+                out=bank[:],
+                lhsT=ww[0][:, 0, : 2 * P].bitcast(FP4X4),
+                lhsT_scale=ws[:, 0, :P],
+                rhs=xw_slots[:, :BANK].bitcast(FP8X4),
+                rhs_scale=xs_slots[:, :BANK],
+                start=True,
+                stop=True,
+            )
+            return bank
 
-        def add_up_blocks(total, gated, j, z0, first, z1):
-            add_up(total, [gated[:, :, z - first : z - first + P] for z in range(z0, z1, P)])
+        def add_up(total, pairs, lists):
+            for r in lists:
+                for b in range(len(pairs)):
+                    nc.tensor.matmul(
+                        total[:, P * b : P * (b + 1)],
+                        lhsT=pairs[b][:, r, :],
+                        rhs=ident[:],
+                        is_transpose=True,
+                        start=(r == 0 and b == 0),
+                        stop=(r == 1 and b == len(pairs) - 1),
+                    )
+
+        def add_up_blocks(total, gated, j, z0, first, z1, lists=(0, 1)):
+            add_up(total, [gated[:, :, z - first : z - first + P] for z in range(z0, z1, P)], lists)
+            if 1 not in lists:
+                return
             nc.scalar.copy(
                 rounded_blocks(z0 // P, z1 // P)[:, :, :, 32 * j : 32 * (j + 1), :].rearrange("z b u p e -> z u b p e"),
                 total[:, : z1 - z0].rearrange("z (b p u e) -> z u b p e", p=32, u=2, e=2),
             )
 
-        def turn_back(grouped, first, z0, z1):
-            back = any_bank()
+        def turn_back(grouped, first, z0, z1, back):
             for b in range((z1 - z0) // P):
                 pairs = rounded_blocks(z0 // P + b, z0 // P + b + 1)[:, 0].rearrange("z u p e -> z (u p e)").bitcast(F32)
                 for u in range(2):
@@ -206,10 +219,9 @@ def tile_moe_mhm_none_kernel(
                 back[:, : 2 * (z1 - z0)].rearrange("p (b u z) -> p b z u", u=2, z=P),
             )
 
-        def turned(z0, z1):
+        def turned(z0, z1, back):
             grouped = keep.tile([P, z1 - z0, 4], BF16, name=f"grouped{z0}", align_bytes=64)
-            for z in range(z0, z1, 2 * P):
-                turn_back(grouped, z0, z, min(z + 2 * P, z1))
+            turn_back(grouped, z0, z0, z1, back)
             return grouped
 
         def quantize(grouped, z0, z1, codes=c_codes, first=0):
@@ -248,19 +260,28 @@ def tile_moe_mhm_none_kernel(
                 stop=stop,
             )
 
-        for j in range(LT):
+        for j in range(LT - 1):
             gated = keep.tile([P, 2, 1024], F32, name=f"gated_first{j}")
             fetch(gated, j, 0, 1024)
             add_up_blocks(any_bank(), gated, j, 0, 0, 512)
             add_up_blocks(any_bank(), gated, j, 512, 0, 1024)
-        g_a = turned(0, 256)
-        g_b = turned(768, 1024)
-        g_c = turned(256, 512)
-        g_c2 = turned(512, 768)
+        gated = keep.tile([P, 2, 1024], F32, name="gated_first_last")
+        fetch(gated, LT - 1, 0, 1024)
+        sums = [any_bank(), any_bank()]
+        add_up_blocks(sums[0], gated, LT - 1, 0, 0, 512, (0,))
+        add_up_blocks(sums[1], gated, LT - 1, 512, 0, 1024, (0,))
+        back_a = warm_up(warm_up(any_bank()))
+        add_up_blocks(sums[0], gated, LT - 1, 0, 0, 512, (1,))
+        add_up_blocks(sums[1], gated, LT - 1, 512, 0, 1024, (1,))
+        g_a = turned(0, 256, back_a)
+        g_b = turned(768, 1024, any_bank())
+        g_c = turned(256, 512, warm_up(any_bank()))
+        g_c2 = turned(512, 768, any_bank())
         gated_second = shared.tile([P, LT - 1, 2, 384], F32, name="gated_second", offset=0)
         for j in range(LT - 1):
             fetch(gated_second[:, j], j, 1024, 1408)
-            add_up_blocks(any_bank(), gated_second[:, j], j, 1024, 1024, 1408)
+            bank = any_bank()
+            add_up_blocks(warm_up(bank) if j > 0 else bank, gated_second[:, j], j, 1024, 1024, 1408)
         codes_ab = keep.tile([P, 512], U32, name="codes_ab", align_bytes=64)
         quantize(g_a, 0, 256, codes_ab, 0)
         quantize(g_b, 768, 1024, codes_ab, 512)
@@ -275,8 +296,8 @@ def tile_moe_mhm_none_kernel(
         for h in range(2):
             for t in (256, 384):
                 merge_pass(acc_d[:, 256 * h + t - 256 : 256 * h + t - 256 + P], h, 0, t, h == 0 and t == 256, False)
-        g_d = turned(1024, 1280)
-        g_e = turned(1280, 1408)
+        g_d = turned(1024, 1280, warm_up(any_bank()))
+        g_e = turned(1280, 1408, any_bank())
         gated_third = keep.tile([P, LT, 2, P], F32, name="gated_third", tag="codes_ab", align_bytes=64)
         for j in range(LT):
             fetch(gated_third[:, j], j, 1408, 1536)
@@ -295,9 +316,9 @@ def tile_moe_mhm_none_kernel(
             rounded_last[:, 0, :, : 32 * (LT - 1), :],
             total[:, : P * (LT - 1)].rearrange("z (p u e) -> z u p e", u=2, e=2),
         )
-        add_up_blocks(any_bank(), gated_third[:, LT - 1], LT - 1, 1408, 1408, 1536)
+        add_up_blocks(warm_up(any_bank()), gated_third[:, LT - 1], LT - 1, 1408, 1408, 1536)
         quantize(g_d, 1024, 1280)
-        g_f = turned(1408, 1536)
+        g_f = turned(1408, 1536, any_bank())
         for h in range(2):
             for t in (256, 384):
                 merge_pass(acc_d[:, 256 * h + t - 256 : 256 * h + t - 256 + P], h, 1, t, False, h == 1 and t == 384)

@@ -117,9 +117,9 @@ def tile_moe_mhm_none_kernel(
         for r in range(2):
             nc.sync.dma_start(gate_first[r][:], gate[r, :, :1024])
         gather_slots(xw_slots, xw, 0, 4)
-        for j in range(2):
-            experts(j, 0, 2)
-            experts(j, 2, 4)
+        experts(0, 0, 2)
+        experts(0, 2, 4)
+        experts(1, 0, 2)
         gather_slots(xw_slots, xw, 4, 8)
         experts(0, 4, 6)
         experts(0, 6, 8)
@@ -128,9 +128,9 @@ def tile_moe_mhm_none_kernel(
         gather_slots(xw_slots, xw, 10, 11)
         experts(0, 10, 11)
         gather_slots(xw_slots, xw, 11, 12)
-        experts(0, 11, 11.5)
-        experts(0, 11.5, 12, nc.vector.tensor_copy)
-        for e in range(4, E, 2):
+        experts(0, 11, 11.5, nc.vector.tensor_copy)
+        experts(0, 11.5, 12)
+        for e in range(2, E, 2):
             experts(1, e, e + 2)
         for j in range(2, LT):
             for e in range(0, E, 2):
@@ -263,25 +263,26 @@ def tile_moe_mhm_none_kernel(
         for j in range(LT - 1):
             gated = keep.tile([P, 2, 1024], F32, name=f"gated_first{j}")
             fetch(gated, j, 0, 1024)
-            add_up_blocks(any_bank(), gated, j, 0, 0, 512)
-            add_up_blocks(any_bank(), gated, j, 512, 0, 1024)
+            sums = [any_bank(), any_bank()]
+            for r in range(2):
+                add_up_blocks(sums[0], gated, j, 0, 0, 512, (r,))
+                add_up_blocks(sums[1], gated, j, 512, 0, 1024, (r,))
         gated = keep.tile([P, 2, 1024], F32, name="gated_first_last")
         fetch(gated, LT - 1, 0, 1024)
-        sums = [any_bank(), any_bank()]
+        sums = [warm_up(warm_up(any_bank())), any_bank()]
         add_up_blocks(sums[0], gated, LT - 1, 0, 0, 512, (0,))
         add_up_blocks(sums[1], gated, LT - 1, 512, 0, 1024, (0,))
-        back_a = warm_up(warm_up(any_bank()))
+        back_a = warm_up(any_bank())
         add_up_blocks(sums[0], gated, LT - 1, 0, 0, 512, (1,))
         add_up_blocks(sums[1], gated, LT - 1, 512, 0, 1024, (1,))
         g_a = turned(0, 256, back_a)
         g_b = turned(768, 1024, any_bank())
-        g_c = turned(256, 512, warm_up(any_bank()))
+        g_c = turned(256, 512, any_bank())
         g_c2 = turned(512, 768, any_bank())
-        gated_second = shared.tile([P, LT - 1, 2, 384], F32, name="gated_second", offset=0)
+        gated_second = [shared.tile([P, 2, 384], F32, name=f"gated_second{j}", offset=2560 + 3072 * j) for j in range(LT - 1)]
         for j in range(LT - 1):
-            fetch(gated_second[:, j], j, 1024, 1408)
-            bank = any_bank()
-            add_up_blocks(warm_up(bank) if j > 0 else bank, gated_second[:, j], j, 1024, 1024, 1408)
+            fetch(gated_second[j], j, 1024, 1408)
+            add_up_blocks(any_bank(), gated_second[j], j, 1024, 1024, 1408)
         codes_ab = keep.tile([P, 512], U32, name="codes_ab", align_bytes=64)
         quantize(g_a, 0, 256, codes_ab, 0)
         quantize(g_b, 768, 1024, codes_ab, 512)
@@ -298,7 +299,7 @@ def tile_moe_mhm_none_kernel(
                 merge_pass(acc_d[:, 256 * h + t - 256 : 256 * h + t - 256 + P], h, 0, t, h == 0 and t == 256, False)
         g_d = turned(1024, 1280, warm_up(any_bank()))
         g_e = turned(1280, 1408, any_bank())
-        gated_third = keep.tile([P, LT, 2, P], F32, name="gated_third", tag="codes_ab", align_bytes=64)
+        gated_third = shared.tile([P, LT, 2, P], F32, name="gated_third", offset=4608)
         for j in range(LT):
             fetch(gated_third[:, j], j, 1408, 1536)
         total = end_bank("end_a")
@@ -318,20 +319,20 @@ def tile_moe_mhm_none_kernel(
         )
         add_up_blocks(warm_up(any_bank()), gated_third[:, LT - 1], LT - 1, 1408, 1408, 1536)
         quantize(g_d, 1024, 1280)
-        g_f = turned(1408, 1536, any_bank())
         for h in range(2):
             for t in (256, 384):
                 merge_pass(acc_d[:, 256 * h + t - 256 : 256 * h + t - 256 + P], h, 1, t, False, h == 1 and t == 384)
-        codes_c2 = keep.tile([P, 256], U32, name="codes_c2", tag="codes_ab", align_bytes=64)
+        g_f = turned(1408, 1536, any_bank())
+        codes_c2 = shared.tile([P, 256], U32, name="codes_c2", offset=4608, align_bytes=64)
         quantize(g_c2, 512, 768, codes_c2, 512)
         for h in range(2):
             merge_pass(acc_e[:, P * h : P * (h + 1)], h, 0, 512, h == 0, False, codes_c2, 512)
         merge_pass(last[:, :P], 0, 0, 640, True, False, codes_c2, 512)
+        codes_e = keep.tile([P, P], U32, name="codes_e", align_bytes=64)
+        quantize(g_e, 1280, 1408, codes_e, 1280)
         staged_d = keep.tile([P, 2, 256], F32, name="staged_d")
         nc.vector.tensor_copy(staged_d[:].rearrange("p h t -> p (h t)"), acc_d[:])
         nc.sync.dma_start(out_v[:, :, 256:512], staged_d[:])
-        codes_e = keep.tile([P, P], U32, name="codes_e", tag="rounded11", align_bytes=64)
-        quantize(g_e, 1280, 1408, codes_e, 1280)
         last_b = end_bank("end_a")
         merge_pass(last_b[:, :P], 1, 0, 640, True, False, codes_c2, 512)
         for h in range(2):

@@ -17,13 +17,19 @@ U8 = mybir.dt.uint8
 FP8X4 = mybir.dt.float8_e4m3fn_x4
 FP4X4 = mybir.dt.float4_e2m1fn_x4
 MULT = mybir.AluOpType.mult
+ADD = mybir.AluOpType.add
+COPY = mybir.ActivationFunctionType.Copy
 
 P = 128
 LT = H // P
 BANK = 512
 PER_COL = 16
-W_LOAD = 4
-XS_COLS = 2048
+W_CUTS = (0, 2, 4, 8, 12)
+WS_CUTS = (0, 4, 12)
+XW_FIRST = 4
+XS_FIRST = 2
+ZS = 640
+S_CUTS = (0, 3, 5)
 
 
 def tile_moe_mhm_none_kernel(
@@ -33,16 +39,31 @@ def tile_moe_mhm_none_kernel(
     with ExitStack() as ctx:
         keep = ctx.enter_context(tc.tile_pool(name="keep", bufs=1))
         shared = ctx.enter_context(tc.tile_pool(name="shared", bufs=1))
-        psum = ctx.enter_context(tc.psum_pool(name="psum", bufs=4))
-        psum_end = ctx.enter_context(tc.psum_pool(name="psum_end", bufs=1))
+        psum = ctx.enter_context(tc.psum_pool(name="psum", bufs=1))
 
         offs_sb = keep.tile([P, S // PER_COL], U16, name="offs_sb")
         pos_sb = [keep.tile([P, Z // PER_COL], U16, name=f"pos_sb{r}") for r in range(2)]
-        xw = shared.tile([P, Z], U32, name="xw", offset=13312)
-        xs = keep.tile([P, XS_COLS], U8, name="xs", align_bytes=64)
-        ws = keep.tile([P, E, H], U8, name="ws", align_bytes=64)
-        ww = [keep.tile([P, W_LOAD, 2 * H], U8, name=f"ww{i}", align_bytes=64) for i in range(E // W_LOAD)]
+        xw = keep.tile([P, Z], U32, name="xw")
+        xs = keep.tile([P, Z], U8, name="xs", align_bytes=64)
+        ws = [keep.tile([P, b - a, H], U8, name=f"ws{a}", align_bytes=64) for a, b in zip(WS_CUTS, WS_CUTS[1:])]
+        ww = [keep.tile([P, b - a, 2 * H], U8, name=f"ww{a}", align_bytes=64) for a, b in zip(W_CUTS, W_CUTS[1:])]
+        wmw = keep.tile([P, D, 2 * N], U8, name="wmw", align_bytes=64)
+        wms = keep.tile([P, D, N], U8, name="wms", align_bytes=64)
         ident = keep.tile([P, P], F32, name="ident")
+        ident16 = keep.tile([P, P], BF16, name="ident16")
+        gate_rows = keep.tile([P, P], F32, name="gate_rows")
+        ww_head = shared.tile([P, W_CUTS[1], 2 * P], U8, name="ww_head", offset=2304, align_bytes=64)
+        gate_cols = {
+            (0, 0): shared.tile([P, 3], F32, name="gate_cols00", offset=10752),
+            (0, 1): keep.tile([P, 2], F32, name="gate_cols01"),
+            (1, 0): keep.tile([P, 3], F32, name="gate_cols10"),
+            (1, 1): keep.tile([P, 2], F32, name="gate_cols11"),
+        }
+        gate_wide = keep.tile([P, 2, Z - ZS], F32, name="gate_wide")
+
+        def part(tiles, cuts, e):
+            i = max(k for k in range(len(tiles)) if cuts[k] <= e)
+            return tiles[i][:, e - cuts[i]]
 
         def load_scale_rows(plane, rows):
             for q in range(4):
@@ -51,299 +72,338 @@ def tile_moe_mhm_none_kernel(
                     rows[:, 4 * q : 4 * q + 4, :].rearrange("a r c -> r a c").bitcast(I32),
                 )
 
-        nc.vector.memset(xs[:96, :Z].bitcast(I32), 0)
-        nc.vector.memset(xs[:, Z:].bitcast(I32), 0)
-        nc.vector.memset(ws[:].rearrange("p e l -> p (e l)").bitcast(I32), 0)
-        xs_slots = keep.tile([P, S], U8, name="xs_slots", align_bytes=64)
-        nc.vector.memset(xs_slots[:].bitcast(I32), 0)
-        make_identity(nc, ident[:])
-
-        for half in range(2):
+        def load_words(i):
             nc.sync.dma_start(
-                xs[96 + 16 * half : 112 + 16 * half, :Z].bitcast(I32).rearrange("p (o t) -> p o t", o=D),
-                x_scales.rearrange("o b t -> b o t").bitcast(I32),
+                ww[i][:].bitcast(I32),
+                w_words[W_CUTS[i] : W_CUTS[i + 1], 0].rearrange("e p b -> p e b").bitcast(I32),
             )
+
+        nc.vector.memset(xs[:].bitcast(I32), 0)
+        for plane in ws:
+            nc.vector.memset(plane[:].rearrange("p e l -> p (e l)").bitcast(I32), 0)
+        nc.vector.memset(wms[:].rearrange("p o n -> p (o n)").bitcast(I32), 0)
+        nc.vector.memset(gate_rows[:], 0.0)
+        make_identity(nc, ident[:])
+        make_identity(nc, ident16[:])
+
         nc.sync.dma_start(offs_sb[:], offs)
+        head_words = w_words[: W_CUTS[1], 0].rearrange("e p b -> p e b")
+        nc.sync.dma_start(ww_head[:].bitcast(I32), head_words[:, :, : 2 * P].bitcast(I32))
+        nc.sync.dma_start(ww[0][:, :, 2 * P :].bitcast(I32), head_words[:, :, 2 * P :].bitcast(I32))
+        load_scale_rows(xs[:].rearrange("p (o t) -> p o t", o=D), x_scales)
         nc.sync.dma_start(
             xw[:].bitcast(I32).rearrange("p (o t) -> p o t", o=D),
             x_words.rearrange("o p t d -> p o (t d)").bitcast(I32),
         )
+        load_scale_rows(ws[0][:], w_scales[WS_CUTS[0] : WS_CUTS[1], 0])
+        load_words(1)
+        load_scale_rows(ws[1][:], w_scales[WS_CUTS[1] : WS_CUTS[2], 0])
+        load_words(2)
+        load_words(3)
         nc.sync.dma_start(pos_sb[0][:], pos1)
         nc.sync.dma_start(pos_sb[1][:], pos2)
-        load_scale_rows(ws[:], w_scales[:, 0])
-        for i in range(E // W_LOAD):
-            nc.sync.dma_start(
-                ww[i][:].bitcast(I32),
-                w_words[W_LOAD * i : W_LOAD * (i + 1), 0].rearrange("e p b -> p e b").bitcast(I32),
-            )
-
-        xw_slots = keep.tile([P, S], U32, name="xw_slots", align_bytes=64)
-        xs_rows = shared.tile([P, S], U8, name="xs_rows", offset=7680)
-
-        def gather_slots(dst, window, e0, e1):
-            cols = slice(e0 * C // PER_COL, e1 * C // PER_COL)
-            nc.vector.tensor_copy(dst[:, e0 * C : e1 * C], window[:].indirect(offs_sb[:, cols]))
-
-        y = [keep.tile([P, S], F32, name=f"y{j}") for j in range(LT)]
-
-        def multiply(bank, j, s0, s1):
-            step = min(C, s1 - s0)
-            for s in range(s0, s1, step):
-                e = s // C
-                nc.tensor.matmul_mx(
-                    out=bank[:, s - s0 : s - s0 + step],
-                    lhsT=ww[e // W_LOAD][:, e % W_LOAD, 2 * P * j : 2 * P * (j + 1)].bitcast(FP4X4),
-                    lhsT_scale=ws[:, e, P * j : P * (j + 1)],
-                    rhs=xw_slots[:, s : s + step].bitcast(FP8X4),
-                    rhs_scale=xs_slots[:, s : s + step],
-                    start=True,
-                    stop=True,
-                )
-            return bank
-
-        def experts(j, e0, e1, copy=nc.scalar.copy):
-            s0, s1 = int(e0 * C), int(e1 * C)
-            bank = multiply(psum.tile([P, BANK], F32, name="bank"), j, s0, s1)
-            copy(y[j][:, s0:s1], bank[:, : s1 - s0])
-
-        for e in range(0, E, 6):
-            gather_slots(xs_rows, xs, e, e + 6)
-            for q in range(4):
-                nc.scalar.dma_start(
-                    xs_slots[32 * q : 32 * q + 4, e * C : (e + 6) * C].bitcast(I32),
-                    xs_rows[96 + 16 * (e // 6) + 4 * q : 100 + 16 * (e // 6) + 4 * q, e * C : (e + 6) * C].bitcast(I32),
-                )
-        gate_first = [shared.tile([P, 1024], F32, name=f"gate_first{r}", offset=5120 + 4096 * r) for r in range(2)]
         for r in range(2):
-            nc.sync.dma_start(gate_first[r][:], gate[r, :, :1024])
-        gather_slots(xw_slots, xw, 0, 4)
-        experts(0, 0, 2)
-        experts(0, 2, 4)
-        experts(1, 0, 2)
-        gather_slots(xw_slots, xw, 4, 8)
-        experts(0, 4, 6)
-        experts(0, 6, 8)
-        gather_slots(xw_slots, xw, 8, 10)
-        experts(0, 8, 10)
-        gather_slots(xw_slots, xw, 10, 11)
-        experts(0, 10, 11)
-        gather_slots(xw_slots, xw, 11, 12)
-        experts(0, 11, 11.5, nc.vector.tensor_copy)
-        experts(0, 11.5, 12)
-        for e in range(2, E, 2):
-            experts(1, e, e + 2)
-        for j in range(2, LT):
-            for e in range(0, E, 2):
-                experts(j, e, e + 2)
-
-        gate_rest = shared.tile([P, 2, 512], F32, name="gate_rest", offset=13312)
-        nc.sync.dma_start(gate_rest[:], gate[:, :, 1024:].rearrange("r p z -> p r z"))
-        wmw = shared.tile([P, D, 2 * N], U8, name="wmw", offset=17408, align_bytes=64)
-        wms = shared.tile([P, D, N], U8, name="wms", offset=18432, align_bytes=64)
-        nc.gpsimd.memset(wms[:].rearrange("p o n -> p (o n)").bitcast(I32), 0)
+            nc.sync.dma_start(gate_rows[5 * r : 5 * r + 5, :], gate[r, 0, :ZS].rearrange("(b z) -> b z", z=P))
+        nc.sync.dma_start(gate_wide[:], gate[:, :, ZS:].rearrange("r p z -> p r z"))
         nc.sync.dma_start(wmw[:].bitcast(I32), wm_words.rearrange("o p b -> p o b").bitcast(I32))
         load_scale_rows(wms[:], wm_scales)
 
-        cuts = (0, 4, 8, 11, 12)
-        rounded = [
-            keep.tile([P, b - a, 2, P, 2], BF16, name=f"rounded{a}", align_bytes=64) for a, b in zip(cuts, cuts[1:])
-        ]
-        rounded_last = rounded[-1]
+        xw_slots = [keep.tile([P, XW_FIRST * C], U32, name="xw_first", align_bytes=64)]
+        xs_slots = [keep.tile([P, XS_FIRST * C], U8, name="xs_first", align_bytes=64)]
+        y = [keep.tile([P, S], F32, name=f"y{j}") for j in range(LT)]
 
-        def rounded_blocks(b0, b1):
-            i = max(k for k in range(4) if cuts[k] <= b0)
-            return rounded[i][:, b0 - cuts[i] : b1 - cuts[i]]
+        def bank(k):
+            return psum.tile([P, BANK], F32, name=f"bank{k}")
 
-        c_codes = keep.tile([P, Z], U32, name="c_codes", align_bytes=64)
-        c_scales = keep.tile([P, Z], U8, name="c_scales", align_bytes=64)
+        used = []
+
+        def next_bank():
+            used.append(len(used) % 8)
+            return bank(used[-1])
+
+        def slots(tiles, e0, e1):
+            first = tiles[0].shape[1] // C
+            if e0 < first:
+                return tiles[0][:, e0 * C : e1 * C]
+            return tiles[1][:, (e0 - first) * C : (e1 - first) * C]
+
+        def gather_slots(dst, window, e0, e1):
+            cols = slice(e0 * C // PER_COL, e1 * C // PER_COL)
+            nc.vector.tensor_copy(slots(dst, e0, e1), window[:].indirect(offs_sb[:, cols]))
+
+        def experts(j, e0, e1, copy=nc.scalar.copy):
+            acc = next_bank()
+            for e in range(e0, e1):
+                if j == 0 and e < W_CUTS[1]:
+                    words = ww_head[:, e]
+                else:
+                    words = part(ww, W_CUTS, e)[:, 2 * P * j : 2 * P * (j + 1)]
+                nc.tensor.matmul_mx(
+                    out=acc[:, (e - e0) * C : (e - e0 + 1) * C],
+                    lhsT=words.bitcast(FP4X4),
+                    lhsT_scale=part(ws, WS_CUTS, e)[:, P * j : P * (j + 1)],
+                    rhs=slots(xw_slots, e, e + 1).bitcast(FP8X4),
+                    rhs_scale=slots(xs_slots, e, e + 1),
+                    start=True,
+                    stop=True,
+                )
+            copy(y[j][:, e0 * C : e1 * C], acc[:, : (e1 - e0) * C])
+
+        xs_slots.append(shared.tile([P, (E - XS_FIRST) * C], U8, name="xs_rest", offset=0, align_bytes=64))
+        xw_slots.append(shared.tile([P, (E - XW_FIRST) * C], U32, name="xw_rest", offset=2560, align_bytes=64))
+        gather_slots(xs_slots, xs, 0, 2)
+        gather_slots(xw_slots, xw, 0, 2)
+        for j in range(LT):
+            experts(j, 0, 2)
+        gather_slots(xw_slots, xw, 2, 4)
+        for e in range(2, 8, 2):
+            gather_slots(xs_slots, xs, e, e + 2)
+            if e >= XW_FIRST:
+                gather_slots(xw_slots, xw, e, e + 2)
+            for j in range(LT):
+                experts(j, e, e + 2)
+        turned_gate = next_bank()
+        nc.tensor.transpose(turned_gate[:, :P], gate_rows[:], ident[:])
+        for r in range(2):
+            for c in range(2):
+                nc.scalar.copy(gate_cols[r, c][:], turned_gate[:, 5 * r + S_CUTS[c] : 5 * r + S_CUTS[c + 1]])
+        gather_slots(xs_slots, xs, 8, 10)
+        gather_slots(xw_slots, xw, 8, 10)
+        for j in range(LT - 1):
+            experts(j, 8, 10)
+        gather_slots(xs_slots, xs, 10, 12)
+        gather_slots(xw_slots, xw, 10, 11)
+        gather_slots(xw_slots, xw, 11, 12)
+        experts(0, 10, 11, nc.vector.tensor_copy)
+        experts(0, 11, 12, nc.vector.tensor_copy)
+        experts(1, 10, 12)
+        experts(2, 10, 12)
+        experts(3, 8, 10)
+        experts(3, 10, 12)
+
         out_v = out.rearrange("(h p) t -> p h t", p=P)
 
-        def any_bank():
-            return psum.tile([P, BANK], F32, name="bank")
+        def offsets(r, z0, z1):
+            return pos_sb[r][:, z0 // PER_COL : z1 // PER_COL]
 
-        def end_bank(tag):
-            return psum_end.tile([P, BANK], F32, name=tag)
+        def rounded_tile(z0, z1, offset=None):
+            pool = keep if offset is None else shared
+            return pool.tile([P, (z1 - z0) // P, 2, P, 2], BF16, name=f"rounded{z0}", align_bytes=64, offset=offset)
 
-        def fetch(gated, j, z0, z1):
+        def fetch_gated(j, z0, z1, gated):
             for r in range(2):
                 nc.vector.tensor_tensor(
-                    gated[:, r, :],
-                    y[j][:].indirect(pos_sb[r][:, z0 // PER_COL : z1 // PER_COL]),
-                    gate_first[r][:, z0:z1] if z1 <= 1024 else gate_rest[:, r, z0 - 1024 : z1 - 1024],
-                    MULT,
+                    gated[:, r, :], y[j][:].indirect(offsets(r, z0, z1)), gate_wide[:, r, z0 - ZS : z1 - ZS], MULT
+                )
+            return gated
+
+        def fetch_one(r, j, z0, z1, gated):
+            nc.vector.tensor_tensor(
+                gated, y[j][:].indirect(offsets(r, z0, z1)), gate_wide[:, r, z0 - ZS : z1 - ZS], MULT
+            )
+            return gated
+
+        def add_pair(total, one, other):
+            nc.vector.tensor_tensor(total, one, other, ADD)
+
+        def bank16(k):
+            return psum.tile([P, 2, H], BF16, name=f"bank{k}")
+
+        def turn16(banks, total, j):
+            for b in range(total.shape[1] // P):
+                nc.tensor.transpose(
+                    banks[b // 2][:, b % 2, P * j : P * (j + 1)], total[:, P * b : P * (b + 1)], ident16[:]
                 )
 
-        def warm_up(bank):
-            nc.tensor.matmul_mx(
-                out=bank[:],
-                lhsT=ww[0][:, 0, : 2 * P].bitcast(FP4X4),
-                lhsT_scale=ws[:, 0, :P],
-                rhs=xw_slots[:, :BANK].bitcast(FP8X4),
-                rhs_scale=xs_slots[:, :BANK],
-                start=True,
-                stop=True,
+        def regroup(turned, rounded, b0):
+            nc.scalar.copy(
+                rounded[:, b0 : b0 + 2].rearrange("z b u p e -> z (b u p e)").bitcast(F32).rearrange(
+                    "z (b u p) -> z b u p", b=2, u=2
+                ),
+                turned[:].rearrange("z b l -> z (b l)").bitcast(F32).rearrange("z (b p u) -> z b u p", b=2, u=2),
             )
-            return bank
 
-        def add_up(total, pairs, lists):
-            for r in lists:
-                for b in range(len(pairs)):
+        def add_up(gated, j, rounded, k):
+            blocks = rounded.shape[1]
+            total = bank(k)
+            for r in range(2):
+                for b in range(blocks):
                     nc.tensor.matmul(
                         total[:, P * b : P * (b + 1)],
-                        lhsT=pairs[b][:, r, :],
+                        lhsT=gated[:, r, P * b : P * (b + 1)],
                         rhs=ident[:],
                         is_transpose=True,
                         start=(r == 0 and b == 0),
-                        stop=(r == 1 and b == len(pairs) - 1),
+                        stop=(r == 1 and b == blocks - 1),
                     )
-
-        def add_up_blocks(total, gated, j, z0, first, z1, lists=(0, 1)):
-            add_up(total, [gated[:, :, z - first : z - first + P] for z in range(z0, z1, P)], lists)
-            if 1 not in lists:
-                return
             nc.scalar.copy(
-                rounded_blocks(z0 // P, z1 // P)[:, :, :, 32 * j : 32 * (j + 1), :].rearrange("z b u p e -> z u b p e"),
-                total[:, : z1 - z0].rearrange("z (b p u e) -> z u b p e", p=32, u=2, e=2),
+                rounded[:, :, :, 32 * j : 32 * (j + 1), :].rearrange("z b u p e -> z u b p e"),
+                total[:, : P * blocks].rearrange("z (b p u e) -> z u b p e", p=32, u=2, e=2),
             )
 
-        def turn_back(grouped, first, z0, z1, back):
-            for b in range((z1 - z0) // P):
-                pairs = rounded_blocks(z0 // P + b, z0 // P + b + 1)[:, 0].rearrange("z u p e -> z (u p e)").bitcast(F32)
+        def fetch_plain(r, j, z0, z1, plain):
+            nc.scalar.activation(plain, y[j][:].indirect(offsets(r, z0, z1)), COPY)
+            return plain
+
+        def turn(plains, b, k):
+            turned = bank(k)
+            for j in range(LT):
+                nc.tensor.transpose(turned[:, P * j : P * (j + 1)], plains[j][:, P * b : P * (b + 1)], ident[:])
+            return turned
+
+        def first_product(turned, block):
+            first = keep.tile([P, 2, P, 2], F32, name=f"first{block}")
+            nc.scalar.activation(
+                first[:],
+                turned[:].rearrange("z (p u e) -> z u p e", u=2, e=2),
+                COPY,
+                scale=gate_cols[0, block // 3][:, block % 3 : block % 3 + 1],
+            )
+            return first
+
+        def second_product(turned, first, block, rounded, b):
+            for u in range(2):
+                nc.vector.scalar_tensor_tensor(
+                    rounded[:, b, u],
+                    turned[:].rearrange("z (p u e) -> z u p e", u=2, e=2)[:, u],
+                    gate_cols[1, block // 3][:, block % 3 : block % 3 + 1],
+                    first[:, u],
+                    MULT,
+                    ADD,
+                )
+
+        def turn_back(grouped, rounded, b0, b1, k):
+            back = bank(k)
+            for b in range(b0, b1):
+                pairs = rounded[:, b].rearrange("z u p e -> z (u p e)").bitcast(F32)
                 for u in range(2):
-                    nc.tensor.transpose(
-                        back[:, P * (2 * b + u) : P * (2 * b + u + 1)], pairs[:, P * u : P * (u + 1)], ident[:]
-                    )
-            words = grouped[:, z0 - first : z1 - first, :].rearrange("p z t -> p (z t)").bitcast(F32)
+                    k = 2 * (b - b0) + u
+                    nc.tensor.transpose(back[:, P * k : P * (k + 1)], pairs[:, P * u : P * (u + 1)], ident[:])
+            words = grouped[:, P * b0 : P * b1, :].rearrange("p z t -> p (z t)").bitcast(F32)
             nc.scalar.copy(
                 words.rearrange("p (b z u) -> p b z u", z=P, u=2),
-                back[:, : 2 * (z1 - z0)].rearrange("p (b u z) -> p b z u", u=2, z=P),
+                back[:, : 2 * P * (b1 - b0)].rearrange("p (b u z) -> p b z u", u=2, z=P),
             )
 
-        def turned(z0, z1, back):
-            grouped = keep.tile([P, z1 - z0, 4], BF16, name=f"grouped{z0}", align_bytes=64)
-            turn_back(grouped, z0, z0, z1, back)
-            return grouped
+        def grouped_tile(z0, z1):
+            return keep.tile([P, z1 - z0, 4], BF16, name=f"grouped{z0}", align_bytes=64)
 
-        def quantize(grouped, z0, z1, codes=c_codes, first=0):
+        def quantize(grouped, z0):
+            width = grouped.shape[1]
+            codes = keep.tile([P, width], U32, name=f"codes{z0}", align_bytes=64)
+            scales = keep.tile([P, width], U8, name=f"scales{z0}", align_bytes=64)
             nc.vector.quantize_mx(
-                out=codes[:, z0 - first : z1 - first].bitcast(FP8X4),
-                scales=c_scales[:, z0:z1],
-                in_=grouped[:].rearrange("p z t -> p (z t)"),
+                out=codes[:].bitcast(FP8X4), scales=scales[:], in_=grouped[:].rearrange("p z t -> p (z t)")
             )
+            return codes, scales, z0
 
-        def merge(acc, t0, t1, copy, codes):
+        def merge(heads, t0, t1, copy, k):
             width = t1 - t0
+            acc = bank(k)
             for h in range(N // P):
-                for t in range(t0, t1, P):
-                    for o in range(D):
-                        nc.tensor.matmul_mx(
-                            out=acc[:, h * width + t - t0 : h * width + t - t0 + P],
-                            lhsT=wmw[:, o, 2 * P * h : 2 * P * (h + 1)].bitcast(FP4X4),
-                            lhsT_scale=wms[:, o, P * h : P * (h + 1)],
-                            rhs=codes[:, o * 256 + t : o * 256 + t + P].bitcast(FP8X4),
-                            rhs_scale=c_scales[:, o * T + t : o * T + t + P],
-                            start=(o == 0),
-                            stop=(o == D - 1),
-                        )
+                for o in range(D):
+                    codes, scales, z0 = heads[o]
+                    cols = slice(o * T + t0 - z0, o * T + t1 - z0)
+                    nc.tensor.matmul_mx(
+                        out=acc[:, h * width : (h + 1) * width],
+                        lhsT=wmw[:, o, 2 * P * h : 2 * P * (h + 1)].bitcast(FP4X4),
+                        lhsT_scale=wms[:, o, P * h : P * (h + 1)],
+                        rhs=codes[:, cols].bitcast(FP8X4),
+                        rhs_scale=scales[:, cols],
+                        start=(o == 0),
+                        stop=(o == D - 1),
+                    )
             staged = keep.tile([P, N // P, width], F32, name=f"staged{t0}")
             copy(staged[:].rearrange("p h t -> p (h t)"), acc[:, : (N // P) * width])
             nc.sync.dma_start(out_v[:, :, t0:t1], staged[:])
 
-        def merge_pass(acc, h, o, t, start, stop, codes=c_codes, first=0):
-            nc.tensor.matmul_mx(
-                out=acc,
-                lhsT=wmw[:, o, 2 * P * h : 2 * P * (h + 1)].bitcast(FP4X4),
-                lhsT_scale=wms[:, o, P * h : P * (h + 1)],
-                rhs=codes[:, o * T + t - first : o * T + t - first + P].bitcast(FP8X4),
-                rhs_scale=c_scales[:, o * T + t : o * T + t + P],
-                start=start,
-                stop=stop,
-            )
+        rx, ry = rounded_tile(640, 1152, 31232), rounded_tile(1152, 1408, 35328)
+        r0, r1 = rounded_tile(0, 384, 23040), rounded_tile(384, 640)
+        gx, gy, gz = grouped_tile(640, 1152), grouped_tile(1152, 1408), grouped_tile(1408, 1536)
+        g0, g1 = grouped_tile(0, 384), grouped_tile(384, 640)
 
+        xt = keep.tile([P, 2 * LT, 512], F32, name="xt")
+        cx = shared.tile([P, LT, 512], BF16, name="cx", offset=27136)
+        pt = keep.tile([P, 7, 384], F32, name="pt")
+        pt7 = shared.tile([P, 384], F32, name="pt7", offset=10784)
+        x_banks = [bank16(0), bank16(1)]
+        fetch_one(0, 0, 640, 1152, xt[:, 0])
         for j in range(LT - 1):
-            gated = keep.tile([P, 2, 1024], F32, name=f"gated_first{j}")
-            fetch(gated, j, 0, 1024)
-            sums = [any_bank(), any_bank()]
-            for r in range(2):
-                add_up_blocks(sums[0], gated, j, 0, 0, 512, (r,))
-                add_up_blocks(sums[1], gated, j, 512, 0, 1024, (r,))
-        gated = keep.tile([P, 2, 1024], F32, name="gated_first_last")
-        fetch(gated, LT - 1, 0, 1024)
-        sums = [warm_up(warm_up(any_bank())), any_bank()]
-        add_up_blocks(sums[0], gated, LT - 1, 0, 0, 512, (0,))
-        add_up_blocks(sums[1], gated, LT - 1, 512, 0, 1024, (0,))
-        back_a = warm_up(any_bank())
-        add_up_blocks(sums[0], gated, LT - 1, 0, 0, 512, (1,))
-        add_up_blocks(sums[1], gated, LT - 1, 512, 0, 1024, (1,))
-        g_a = turned(0, 256, back_a)
-        g_b = turned(768, 1024, any_bank())
-        g_c = turned(256, 512, any_bank())
-        g_c2 = turned(512, 768, any_bank())
-        gated_second = [shared.tile([P, 2, 384], F32, name=f"gated_second{j}", offset=2560 + 3072 * j) for j in range(LT - 1)]
+            fetch_one(1, j, 640, 1152, xt[:, 2 * j + 1])
+            fetch_one(0, j + 1, 640, 1152, xt[:, 2 * j + 2])
+            add_pair(cx[:, j], xt[:, 2 * j], xt[:, 2 * j + 1])
+            turn16(x_banks, cx[:, j], j)
+        fetch_one(1, 3, 640, 1152, xt[:, 7])
+        plains = [fetch_plain(0, j, 0, 384, pt[:, j]) for j in range(LT)]
+        turned = [turn(plains, b, 2 + b) for b in range(3)]
+        plains = [fetch_plain(1, j, 0, 384, pt[:, 4 + j] if j < 3 else pt7[:]) for j in range(LT)]
+        firsts = [first_product(turned[b], b) for b in range(3)]
+        turned = [turn(plains, b, 5 + b) for b in range(3)]
+        y00 = keep.tile([P, 256], F32, name="y00")
+        fetch_one(0, 0, 1152, 1408, y00[:])
+        add_pair(cx[:, 3], xt[:, 6], xt[:, 7])
+        turn16(x_banks, cx[:, 3], 3)
+        for b in range(3):
+            second_product(turned[b], firsts[b], b, r0, b)
+        pa = keep.tile([P, LT, 256], F32, name="pa")
+        plains = [fetch_plain(0, j, 384, 640, pa[:, j]) for j in range(LT)]
+        regroup(x_banks[0], rx, 0)
+        regroup(x_banks[1], rx, 2)
+        turned = [turn(plains, b, 2 + b) for b in range(2)]
+        pb = shared.tile([P, LT, 256], F32, name="pb", offset=27136)
+        plains = [fetch_plain(1, j, 384, 640, pb[:, j]) for j in range(2)]
+        turn_back(gx, rx, 0, 2, 4)
+        turn_back(gx, rx, 2, 4, 7)
+        turn_back(g0, r0, 0, 2, 0)
+        turn_back(g0, r0, 2, 3, 1)
+        plains.extend([fetch_plain(1, j, 384, 640, pb[:, j]) for j in range(2, LT)])
+        firsts = [first_product(turned[b], 3 + b) for b in range(2)]
+        turned = [turn(plains, b, 5 + b) for b in range(2)]
+        yt = shared.tile([P, 6, 256], F32, name="yt", offset=10752)
+        cy = keep.tile([P, LT, 256], BF16, name="cy")
+        y_banks = [bank16(0)]
+        yt3 = shared.tile([P, 2, 256], F32, name="yt3", offset=31232)
         for j in range(LT - 1):
-            fetch(gated_second[j], j, 1024, 1408)
-            add_up_blocks(any_bank(), gated_second[j], j, 1024, 1024, 1408)
-        codes_ab = keep.tile([P, 512], U32, name="codes_ab", align_bytes=64)
-        quantize(g_a, 0, 256, codes_ab, 0)
-        quantize(g_b, 768, 1024, codes_ab, 512)
-        merge(any_bank(), 0, 256, nc.scalar.copy, codes_ab)
-        gated = keep.tile([P, 2, 384], F32, name="gated_second_last", tag="rounded4", align_bytes=64)
-        fetch(gated, LT - 1, 1024, 1408)
-        add_up_blocks(end_bank("end_a"), gated, LT - 1, 1024, 1024, 1408)
-        quantize(g_c, 256, 512)
-        acc_d = end_bank("acc_d")
-        acc_e = end_bank("acc_e")
-        last = end_bank("last")
-        for h in range(2):
-            for t in (256, 384):
-                merge_pass(acc_d[:, 256 * h + t - 256 : 256 * h + t - 256 + P], h, 0, t, h == 0 and t == 256, False)
-        g_d = turned(1024, 1280, warm_up(any_bank()))
-        g_e = turned(1280, 1408, any_bank())
-        gated_third = shared.tile([P, LT, 2, P], F32, name="gated_third", offset=4608)
+            fetch_one(1, j, 1152, 1408, yt[:, 2 * j + 1])
+            fetch_one(0, j + 1, 1152, 1408, yt[:, 2 * j + 2] if j < 2 else yt3[:, 0])
+            add_pair(cy[:, j], yt[:, 2 * j] if j else y00[:], yt[:, 2 * j + 1])
+            turn16(y_banks, cy[:, j], j)
+        fetch_one(1, 3, 1152, 1408, yt3[:, 1])
+        qx = quantize(gx, 640)
+        add_pair(cy[:, 3], yt3[:, 0], yt3[:, 1])
+        turn16(y_banks, cy[:, 3], 3)
+        q0 = quantize(g0, 0)
+        merge((q0, qx), 0, 256, nc.scalar.copy, 4)
+        merge((q0, qx), 256, 384, nc.scalar.copy, 7)
+        regroup(y_banks[0], ry, 0)
+        turn_back(gy, ry, 0, 2, 1)
+        rz = rounded_tile(1408, 1536, 35328)
+        last = shared.tile([P, LT, 2, P], F32, name="last", offset=22016)
         for j in range(LT):
-            fetch(gated_third[:, j], j, 1408, 1536)
-        total = end_bank("end_a")
-        steps = [(j, r) for j in range(LT - 1) for r in range(2)]
-        for i, (j, r) in enumerate(steps):
-            nc.tensor.matmul(
-                total[:, P * j : P * (j + 1)],
-                lhsT=gated_third[:, j, r, :],
-                rhs=ident[:],
-                is_transpose=True,
-                start=(r == 0),
-                stop=(r == 1),
-            )
+            fetch_gated(j, 1408, 1536, last[:, j])
+        for b in range(2):
+            second_product(turned[b], firsts[b], 3 + b, r1, b)
+        total = bank(2)
+        for j in range(LT - 1):
+            for r in range(2):
+                nc.tensor.matmul(
+                    total[:, P * j : P * (j + 1)],
+                    lhsT=last[:, j, r, :],
+                    rhs=ident[:],
+                    is_transpose=True,
+                    start=(r == 0),
+                    stop=(r == 1),
+                )
         nc.scalar.copy(
-            rounded_last[:, 0, :, : 32 * (LT - 1), :],
+            rz[:, 0, :, : 32 * (LT - 1), :],
             total[:, : P * (LT - 1)].rearrange("z (p u e) -> z u p e", u=2, e=2),
         )
-        add_up_blocks(warm_up(any_bank()), gated_third[:, LT - 1], LT - 1, 1408, 1408, 1536)
-        quantize(g_d, 1024, 1280)
-        for h in range(2):
-            for t in (256, 384):
-                merge_pass(acc_d[:, 256 * h + t - 256 : 256 * h + t - 256 + P], h, 1, t, False, h == 1 and t == 384)
-        g_f = turned(1408, 1536, any_bank())
-        codes_c2 = shared.tile([P, 256], U32, name="codes_c2", offset=4608, align_bytes=64)
-        quantize(g_c2, 512, 768, codes_c2, 512)
-        for h in range(2):
-            merge_pass(acc_e[:, P * h : P * (h + 1)], h, 0, 512, h == 0, False, codes_c2, 512)
-        merge_pass(last[:, :P], 0, 0, 640, True, False, codes_c2, 512)
-        codes_e = keep.tile([P, P], U32, name="codes_e", align_bytes=64)
-        quantize(g_e, 1280, 1408, codes_e, 1280)
-        staged_d = keep.tile([P, 2, 256], F32, name="staged_d")
-        nc.vector.tensor_copy(staged_d[:].rearrange("p h t -> p (h t)"), acc_d[:])
-        nc.sync.dma_start(out_v[:, :, 256:512], staged_d[:])
-        last_b = end_bank("end_a")
-        merge_pass(last_b[:, :P], 1, 0, 640, True, False, codes_c2, 512)
-        for h in range(2):
-            merge_pass(acc_e[:, P * h : P * (h + 1)], h, 1, 512, False, h == 1, codes_e, 1280)
-        quantize(g_f, 1408, 1536)
-        merge_pass(last[:, :P], 0, 1, 640, False, True)
-        merge_pass(last_b[:, :P], 1, 1, 640, False, True)
-        staged_e = keep.tile([P, 2, P], F32, name="staged_e")
-        nc.scalar.copy(staged_e[:].rearrange("p h t -> p (h t)"), acc_e[:, : 2 * P])
-        nc.sync.dma_start(out_v[:, :, 512:640], staged_e[:])
-        staged_last = keep.tile([P, 2, P], F32, name="staged_last")
-        nc.scalar.copy(staged_last[:, 0, :], last[:, :P])
-        nc.vector.tensor_copy(staged_last[:, 1, :], last_b[:, :P])
-        nc.sync.dma_start(out_v[:, :, 640:768], staged_last[:])
+        add_up(last[:, LT - 1], LT - 1, rz, 3)
+        qy = quantize(gy, 1152)
+        turn_back(gz, rz, 0, 1, 0)
+        turn_back(g1, r1, 0, 2, 3)
+        qz = quantize(gz, 1408)
+        merge((qx, qz), 640, 768, nc.scalar.copy, 0)
+        q1 = quantize(g1, 384)
+        merge((q1, qy), 384, 512, nc.vector.tensor_copy, 5)
+        merge((q1, qy), 512, 640, nc.scalar.copy, 6)

@@ -79,22 +79,24 @@ def tile_moe_mhm_none_kernel(
             )
 
         nc.vector.memset(xs[:].bitcast(I32), 0)
-        for plane in ws:
-            nc.vector.memset(plane[:].rearrange("p e l -> p (e l)").bitcast(I32), 0)
+        nc.vector.memset(ws[0][:].rearrange("p e l -> p (e l)").bitcast(I32), 0)
+        nc.vector.memset(ident[:], 0.0)
+        nc.vector.memset(ident16[:], 0.0)
+        nc.vector.memset(ws[1][:].rearrange("p e l -> p (e l)").bitcast(I32), 0)
         nc.vector.memset(wms[:].rearrange("p o n -> p (o n)").bitcast(I32), 0)
         nc.vector.memset(gate_rows[:], 0.0)
-        make_identity(nc, ident[:])
-        make_identity(nc, ident16[:])
+        make_identity(nc, ident[:], nomemset=True)
+        make_identity(nc, ident16[:], nomemset=True)
 
         nc.sync.dma_start(offs_sb[:], offs)
         head_words = w_words[: W_CUTS[1], 0].rearrange("e p b -> p e b")
         nc.sync.dma_start(ww_head[:].bitcast(I32), head_words[:, :, : 2 * P].bitcast(I32))
-        nc.sync.dma_start(ww[0][:, :, 2 * P :].bitcast(I32), head_words[:, :, 2 * P :].bitcast(I32))
         load_scale_rows(xs[:].rearrange("p (o t) -> p o t", o=D), x_scales)
         nc.sync.dma_start(
             xw[:].bitcast(I32).rearrange("p (o t) -> p o t", o=D),
             x_words.rearrange("o p t d -> p o (t d)").bitcast(I32),
         )
+        nc.sync.dma_start(ww[0][:, :, 2 * P :].bitcast(I32), head_words[:, :, 2 * P :].bitcast(I32))
         load_scale_rows(ws[0][:], w_scales[WS_CUTS[0] : WS_CUTS[1], 0])
         load_words(1)
         load_scale_rows(ws[1][:], w_scales[WS_CUTS[1] : WS_CUTS[2], 0])
@@ -318,9 +320,9 @@ def tile_moe_mhm_none_kernel(
             nc.sync.dma_start(out_v[:, :, t0:t1], staged[:])
 
         rx, ry = rounded_tile(640, 1152, 31232), rounded_tile(1152, 1408, 35328)
-        r0, r1 = rounded_tile(0, 384, 23040), rounded_tile(384, 640)
+        r0, r3, r4 = rounded_tile(0, 384), rounded_tile(384, 512), rounded_tile(512, 640)
         gx, gy, gz = grouped_tile(640, 1152), grouped_tile(1152, 1408), grouped_tile(1408, 1536)
-        g0, g1 = grouped_tile(0, 384), grouped_tile(384, 640)
+        g0, g3, g4 = grouped_tile(0, 384), grouped_tile(384, 512), grouped_tile(512, 640)
 
         xt = keep.tile([P, 2 * LT, 512], F32, name="xt")
         cx = shared.tile([P, LT, 512], BF16, name="cx", offset=27136)
@@ -373,17 +375,18 @@ def tile_moe_mhm_none_kernel(
         add_pair(cy[:, 3], yt3[:, 0], yt3[:, 1])
         turn16(y_banks, cy[:, 3], 3)
         q0 = quantize(g0, 0)
-        merge((q0, qx), 0, 256, nc.scalar.copy, 4)
-        merge((q0, qx), 256, 384, nc.scalar.copy, 7)
+        second_product(turned[0], firsts[0], 3, r3, 0)
         regroup(y_banks[0], ry, 0)
+        merge((q0, qx), 0, 256, nc.scalar.copy, 4)
         turn_back(gy, ry, 0, 2, 1)
+        turn_back(g3, r3, 0, 1, 0)
+        merge((q0, qx), 256, 384, nc.scalar.copy, 0)
         rz = rounded_tile(1408, 1536, 35328)
-        last = shared.tile([P, LT, 2, P], F32, name="last", offset=22016)
+        last = shared.tile([P, LT, 2, P], F32, name="last", offset=27136)
         for j in range(LT):
             fetch_gated(j, 1408, 1536, last[:, j])
-        for b in range(2):
-            second_product(turned[b], firsts[b], 3 + b, r1, b)
-        total = bank(2)
+        second_product(turned[1], firsts[1], 4, r4, 0)
+        total = bank(4)
         for j in range(LT - 1):
             for r in range(2):
                 nc.tensor.matmul(
@@ -398,12 +401,13 @@ def tile_moe_mhm_none_kernel(
             rz[:, 0, :, : 32 * (LT - 1), :],
             total[:, : P * (LT - 1)].rearrange("z (p u e) -> z u p e", u=2, e=2),
         )
-        add_up(last[:, LT - 1], LT - 1, rz, 3)
+        add_up(last[:, LT - 1], LT - 1, rz, 1)
+        turn_back(g4, r4, 0, 1, 6)
+        turn_back(gz, rz, 0, 1, 2)
         qy = quantize(gy, 1152)
-        turn_back(gz, rz, 0, 1, 0)
-        turn_back(g1, r1, 0, 2, 3)
+        q3 = quantize(g3, 384)
+        q4 = quantize(g4, 512)
         qz = quantize(gz, 1408)
-        merge((qx, qz), 640, 768, nc.scalar.copy, 0)
-        q1 = quantize(g1, 384)
-        merge((q1, qy), 384, 512, nc.vector.tensor_copy, 5)
-        merge((q1, qy), 512, 640, nc.scalar.copy, 6)
+        merge((q3, qy), 384, 512, nc.vector.tensor_copy, 5)
+        merge((q4, qy), 512, 640, nc.scalar.copy, 6)
+        merge((qx, qz), 640, 768, nc.vector.tensor_copy, 2)

@@ -29,7 +29,7 @@ WS_CUTS = (0, 4, 12)
 XW_FIRST = 4
 XS_FIRST = 2
 ZS = 640
-S_CUTS = (0, 3, 5)
+S_CUTS = (0, 3, 4, 5)
 
 
 def tile_moe_mhm_none_kernel(
@@ -55,10 +55,10 @@ def tile_moe_mhm_none_kernel(
         ww_head = shared.tile([P, W_CUTS[1], 2 * P], U8, name="ww_head", offset=2304, align_bytes=64)
         gate_cols = {
             (0, 0): shared.tile([P, 3], F32, name="gate_cols00", offset=10752),
-            (0, 1): keep.tile([P, 2], F32, name="gate_cols01"),
-            (1, 0): keep.tile([P, 3], F32, name="gate_cols10"),
-            (1, 1): keep.tile([P, 2], F32, name="gate_cols11"),
+            (0, 1): shared.tile([P, 1], F32, name="gate_cols01", offset=27104),
+            (0, 2): keep.tile([P, 1], F32, name="gate_cols02"),
         }
+        gate_cols1 = keep.tile([P, ZS // P], F32, name="gate_cols1")
         gate_wide = keep.tile([P, 2, Z - ZS], F32, name="gate_wide")
 
         def part(tiles, cuts, e):
@@ -120,7 +120,7 @@ def tile_moe_mhm_none_kernel(
         used = []
 
         def next_bank():
-            used.append(len(used) % 8)
+            used.append((len(used) + 7) % 8)
             return bank(used[-1])
 
         def slots(tiles, e0, e1):
@@ -166,9 +166,9 @@ def tile_moe_mhm_none_kernel(
                 experts(j, e, e + 2)
         turned_gate = next_bank()
         nc.tensor.transpose(turned_gate[:, :P], gate_rows[:], ident[:])
-        for r in range(2):
-            for c in range(2):
-                nc.scalar.copy(gate_cols[r, c][:], turned_gate[:, 5 * r + S_CUTS[c] : 5 * r + S_CUTS[c + 1]])
+        for c in range(3):
+            nc.scalar.copy(gate_cols[0, c][:], turned_gate[:, S_CUTS[c] : S_CUTS[c + 1]])
+        nc.scalar.copy(gate_cols1[:], turned_gate[:, 5:10])
         gather_slots(xs_slots, xs, 8, 10)
         gather_slots(xw_slots, xw, 8, 10)
         for j in range(LT - 1):
@@ -178,7 +178,8 @@ def tile_moe_mhm_none_kernel(
         gather_slots(xw_slots, xw, 11, 12)
         experts(0, 10, 11, nc.vector.tensor_copy)
         experts(0, 11, 12, nc.vector.tensor_copy)
-        experts(1, 10, 12)
+        experts(1, 10, 11, nc.vector.tensor_copy)
+        experts(1, 11, 12)
         experts(2, 10, 12)
         experts(3, 8, 10)
         experts(3, 10, 12)
@@ -259,7 +260,7 @@ def tile_moe_mhm_none_kernel(
                 first[:],
                 turned[:].rearrange("z (p u e) -> z u p e", u=2, e=2),
                 COPY,
-                scale=gate_cols[0, block // 3][:, block % 3 : block % 3 + 1],
+                scale=gate_cols[0, 0][:, block : block + 1] if block < 3 else gate_cols[0, block - 2][:],
             )
             return first
 
@@ -268,7 +269,7 @@ def tile_moe_mhm_none_kernel(
                 nc.vector.scalar_tensor_tensor(
                     rounded[:, b, u],
                     turned[:].rearrange("z (p u e) -> z u p e", u=2, e=2)[:, u],
-                    gate_cols[1, block // 3][:, block % 3 : block % 3 + 1],
+                    gate_cols1[:, block : block + 1],
                     first[:, u],
                     MULT,
                     ADD,
@@ -299,7 +300,7 @@ def tile_moe_mhm_none_kernel(
             )
             return codes, scales, z0
 
-        def merge(heads, t0, t1, copy, k):
+        def merge(heads, t0, t1, k):
             width = t1 - t0
             acc = bank(k)
             for h in range(N // P):
@@ -315,12 +316,17 @@ def tile_moe_mhm_none_kernel(
                         start=(o == 0),
                         stop=(o == D - 1),
                     )
-            staged = keep.tile([P, N // P, width], F32, name=f"staged{t0}")
-            copy(staged[:].rearrange("p h t -> p (h t)"), acc[:, : (N // P) * width])
-            nc.sync.dma_start(out_v[:, :, t0:t1], staged[:])
+
+            def store(copy, offset=None):
+                pool = keep if offset is None else shared
+                staged = pool.tile([P, N // P, width], F32, name=f"staged{t0}", offset=offset)
+                copy(staged[:].rearrange("p h t -> p (h t)"), acc[:, : (N // P) * width])
+                nc.sync.dma_start(out_v[:, :, t0:t1], staged[:])
+
+            return store
 
         rx, ry = rounded_tile(640, 1152, 31232), rounded_tile(1152, 1408, 35328)
-        r0, r3, r4 = rounded_tile(0, 384), rounded_tile(384, 512), rounded_tile(512, 640)
+        r0, r3, r4 = rounded_tile(0, 384, 23040), rounded_tile(384, 512), rounded_tile(512, 640)
         gx, gy, gz = grouped_tile(640, 1152), grouped_tile(1152, 1408), grouped_tile(1408, 1536)
         g0, g3, g4 = grouped_tile(0, 384), grouped_tile(384, 512), grouped_tile(512, 640)
 
@@ -359,7 +365,7 @@ def tile_moe_mhm_none_kernel(
         turn_back(g0, r0, 0, 2, 0)
         turn_back(g0, r0, 2, 3, 1)
         plains.extend([fetch_plain(1, j, 384, 640, pb[:, j]) for j in range(2, LT)])
-        firsts = [first_product(turned[b], 3 + b) for b in range(2)]
+        first3, turned4 = first_product(turned[0], 3), turned[1]
         turned = [turn(plains, b, 5 + b) for b in range(2)]
         yt = shared.tile([P, 6, 256], F32, name="yt", offset=10752)
         cy = keep.tile([P, LT, 256], BF16, name="cy")
@@ -375,23 +381,24 @@ def tile_moe_mhm_none_kernel(
         add_pair(cy[:, 3], yt3[:, 0], yt3[:, 1])
         turn16(y_banks, cy[:, 3], 3)
         q0 = quantize(g0, 0)
-        second_product(turned[0], firsts[0], 3, r3, 0)
         regroup(y_banks[0], ry, 0)
-        merge((q0, qx), 0, 256, nc.scalar.copy, 4)
+        first4 = first_product(turned4, 4)
+        early = shared.tile([P, LT - 1, 2, P], F32, name="early", offset=23040)
+        for j in range(LT - 1):
+            fetch_gated(j, 1408, 1536, early[:, j])
+        second_product(turned[0], first3, 3, r3, 0)
+        last = shared.tile([P, 2, P], F32, name="last", offset=27104)
+        fetch_gated(LT - 1, 1408, 1536, last[:])
+        second_product(turned[1], first4, 4, r4, 0)
+        store_first = merge((q0, qx), 0, 256, 4)
         turn_back(gy, ry, 0, 2, 1)
-        turn_back(g3, r3, 0, 1, 0)
-        merge((q0, qx), 256, 384, nc.scalar.copy, 0)
         rz = rounded_tile(1408, 1536, 35328)
-        last = shared.tile([P, LT, 2, P], F32, name="last", offset=27136)
-        for j in range(LT):
-            fetch_gated(j, 1408, 1536, last[:, j])
-        second_product(turned[1], firsts[1], 4, r4, 0)
-        total = bank(4)
+        total = bank(0)
         for j in range(LT - 1):
             for r in range(2):
                 nc.tensor.matmul(
                     total[:, P * j : P * (j + 1)],
-                    lhsT=last[:, j, r, :],
+                    lhsT=early[:, j, r, :],
                     rhs=ident[:],
                     is_transpose=True,
                     start=(r == 0),
@@ -401,13 +408,17 @@ def tile_moe_mhm_none_kernel(
             rz[:, 0, :, : 32 * (LT - 1), :],
             total[:, : P * (LT - 1)].rearrange("z (p u e) -> z u p e", u=2, e=2),
         )
-        add_up(last[:, LT - 1], LT - 1, rz, 1)
+        turn_back(g3, r3, 0, 1, 5)
+        add_up(last[:], LT - 1, rz, 3)
         turn_back(g4, r4, 0, 1, 6)
+        store_second = merge((q0, qx), 256, 384, 0)
         turn_back(gz, rz, 0, 1, 2)
         qy = quantize(gy, 1152)
         q3 = quantize(g3, 384)
+        store_first(nc.vector.tensor_copy, 26112)
         q4 = quantize(g4, 512)
+        store_second(nc.vector.tensor_copy)
         qz = quantize(gz, 1408)
-        merge((q3, qy), 384, 512, nc.vector.tensor_copy, 5)
-        merge((q4, qy), 512, 640, nc.scalar.copy, 6)
-        merge((qx, qz), 640, 768, nc.vector.tensor_copy, 2)
+        merge((q3, qy), 384, 512, 5)(nc.vector.tensor_copy)
+        merge((q4, qy), 512, 640, 6)(nc.scalar.copy)
+        merge((qx, qz), 640, 768, 2)(nc.vector.tensor_copy)

@@ -27,7 +27,7 @@ PER_COL = 16
 W_CUTS = (0, 2, 4, 8, 12)
 WS_CUTS = (0, 4, 12)
 XW_FIRST = 4
-XS_FIRST = 2
+XS_FIRST = 3
 ZS = 640
 S_CUTS = (0, 3, 4, 5)
 
@@ -52,7 +52,7 @@ def tile_moe_mhm_none_kernel(
         ident = keep.tile([P, P], F32, name="ident")
         ident16 = keep.tile([P, P], BF16, name="ident16")
         gate_rows = keep.tile([P, P], F32, name="gate_rows")
-        ww_head = shared.tile([P, W_CUTS[1], 2 * P], U8, name="ww_head", offset=2304, align_bytes=64)
+        ww_head = shared.tile([P, W_CUTS[1], 2 * P], U8, name="ww_head", offset=2048, align_bytes=64)
         gate_cols = {
             (0, 0): shared.tile([P, 3], F32, name="gate_cols00", offset=10752),
             (0, 1): shared.tile([P, 1], F32, name="gate_cols01", offset=27104),
@@ -120,7 +120,7 @@ def tile_moe_mhm_none_kernel(
         used = []
 
         def next_bank():
-            used.append((len(used) + 7) % 8)
+            used.append(len(used) % 8)
             return bank(used[-1])
 
         def slots(tiles, e0, e1):
@@ -152,16 +152,14 @@ def tile_moe_mhm_none_kernel(
             copy(y[j][:, e0 * C : e1 * C], acc[:, : (e1 - e0) * C])
 
         xs_slots.append(shared.tile([P, (E - XS_FIRST) * C], U8, name="xs_rest", offset=0, align_bytes=64))
-        xw_slots.append(shared.tile([P, (E - XW_FIRST) * C], U32, name="xw_rest", offset=2560, align_bytes=64))
-        gather_slots(xs_slots, xs, 0, 2)
+        xw_slots.append(shared.tile([P, (E - XW_FIRST) * C], U32, name="xw_rest", offset=2304, align_bytes=64))
+        gather_slots(xs_slots, xs, 0, 3)
         gather_slots(xw_slots, xw, 0, 2)
         for j in range(LT):
             experts(j, 0, 2)
-        gather_slots(xw_slots, xw, 2, 4)
         for e in range(2, 8, 2):
-            gather_slots(xs_slots, xs, e, e + 2)
-            if e >= XW_FIRST:
-                gather_slots(xw_slots, xw, e, e + 2)
+            gather_slots(xw_slots, xw, e, e + 2)
+            gather_slots(xs_slots, xs, e + 1, e + 3)
             for j in range(LT):
                 experts(j, e, e + 2)
         turned_gate = next_bank()
@@ -169,17 +167,16 @@ def tile_moe_mhm_none_kernel(
         for c in range(3):
             nc.scalar.copy(gate_cols[0, c][:], turned_gate[:, S_CUTS[c] : S_CUTS[c + 1]])
         nc.scalar.copy(gate_cols1[:], turned_gate[:, 5:10])
-        gather_slots(xs_slots, xs, 8, 10)
         gather_slots(xw_slots, xw, 8, 10)
+        gather_slots(xs_slots, xs, 9, 11)
         for j in range(LT - 1):
             experts(j, 8, 10)
-        gather_slots(xs_slots, xs, 10, 12)
         gather_slots(xw_slots, xw, 10, 11)
+        gather_slots(xs_slots, xs, 11, 12)
         gather_slots(xw_slots, xw, 11, 12)
         experts(0, 10, 11, nc.vector.tensor_copy)
         experts(0, 11, 12, nc.vector.tensor_copy)
-        experts(1, 10, 11, nc.vector.tensor_copy)
-        experts(1, 11, 12)
+        experts(1, 10, 12, nc.vector.tensor_copy)
         experts(2, 10, 12)
         experts(3, 8, 10)
         experts(3, 10, 12)
@@ -349,7 +346,7 @@ def tile_moe_mhm_none_kernel(
         turned = [turn(plains, b, 5 + b) for b in range(3)]
         y00 = keep.tile([P, 256], F32, name="y00")
         fetch_one(0, 0, 1152, 1408, y00[:])
-        add_pair(cx[:, 3], xt[:, 6], xt[:, 7])
+        nc.gpsimd.tensor_tensor(cx[:, 3], xt[:, 6], xt[:, 7], ADD)
         turn16(x_banks, cx[:, 3], 3)
         for b in range(3):
             second_product(turned[b], firsts[b], b, r0, b)

@@ -23,13 +23,23 @@ COPY = mybir.ActivationFunctionType.Copy
 P = 128
 LT = H // P
 BANK = 512
+BANKS = 8
 PER_COL = 16
+
 W_CUTS = (0, 2, 4, 8, 12)
 WS_CUTS = (0, 4, 12)
 XW_FIRST = 4
 XS_FIRST = 3
-ZS = 640
-S_CUTS = (0, 3, 4, 5)
+S_MID, V_FIRST, V_MID, V_LAST = 384, 640, 1152, 1408
+S_BLOCKS = V_FIRST // P
+GATE_CUTS = (0, 2, 3, 4, 5)
+
+AT_XS_REST, AT_W_HEAD, AT_XW_REST = 0, 2048, 2304
+AT_MID_FETCH, AT_GATE_2, AT_PLAIN_END = 10752, 10752, 10784
+AT_MID_END, AT_ROUNDED_S, AT_LAST_EARLY = 22528, 23040, 23552
+AT_GATE_01, AT_SUM_END, AT_PLAIN_LATE = 27136, 27136, 27136
+AT_GATE_3, AT_LAST_END, AT_STAGED = 27104, 27104, 26112
+AT_ROUNDED_MID = 35328
 
 
 def tile_moe_mhm_none_kernel(
@@ -52,18 +62,19 @@ def tile_moe_mhm_none_kernel(
         ident = keep.tile([P, P], F32, name="ident")
         ident16 = keep.tile([P, P], BF16, name="ident16")
         gate_rows = keep.tile([P, P], F32, name="gate_rows")
-        ww_head = shared.tile([P, W_CUTS[1], 2 * P], U8, name="ww_head", offset=2048, align_bytes=64)
-        gate_cols = {
-            (0, 0): shared.tile([P, 3], F32, name="gate_cols00", offset=10752),
-            (0, 1): shared.tile([P, 1], F32, name="gate_cols01", offset=27104),
-            (0, 2): keep.tile([P, 1], F32, name="gate_cols02"),
-        }
-        gate_cols1 = keep.tile([P, ZS // P], F32, name="gate_cols1")
-        gate_wide = keep.tile([P, 2, Z - ZS], F32, name="gate_wide")
+        w_head = shared.tile([P, W_CUTS[1], 2 * P], U8, name="w_head", offset=AT_W_HEAD, align_bytes=64)
+        gate_first = [
+            shared.tile([P, 2], F32, name="gate_first01", offset=AT_GATE_01),
+            shared.tile([P, 1], F32, name="gate_first2", offset=AT_GATE_2),
+            shared.tile([P, 1], F32, name="gate_first3", offset=AT_GATE_3),
+            keep.tile([P, 1], F32, name="gate_first4"),
+        ]
+        gate_second = keep.tile([P, S_BLOCKS], F32, name="gate_second")
+        gate_wide = keep.tile([P, 2, Z - V_FIRST], F32, name="gate_wide")
 
-        def part(tiles, cuts, e):
-            i = max(k for k in range(len(tiles)) if cuts[k] <= e)
-            return tiles[i][:, e - cuts[i]]
+        def part(tiles, cuts, i):
+            tile = max(k for k in range(len(tiles)) if cuts[k] <= i)
+            return tiles[tile][:, i - cuts[tile]]
 
         def load_scale_rows(plane, rows):
             for q in range(4):
@@ -90,7 +101,7 @@ def tile_moe_mhm_none_kernel(
 
         nc.sync.dma_start(offs_sb[:], offs)
         head_words = w_words[: W_CUTS[1], 0].rearrange("e p b -> p e b")
-        nc.sync.dma_start(ww_head[:].bitcast(I32), head_words[:, :, : 2 * P].bitcast(I32))
+        nc.sync.dma_start(w_head[:].bitcast(I32), head_words[:, :, : 2 * P].bitcast(I32))
         load_scale_rows(xs[:].rearrange("p (o t) -> p o t", o=D), x_scales)
         nc.sync.dma_start(
             xw[:].bitcast(I32).rearrange("p (o t) -> p o t", o=D),
@@ -105,23 +116,31 @@ def tile_moe_mhm_none_kernel(
         nc.sync.dma_start(pos_sb[0][:], pos1)
         nc.sync.dma_start(pos_sb[1][:], pos2)
         for r in range(2):
-            nc.sync.dma_start(gate_rows[5 * r : 5 * r + 5, :], gate[r, 0, :ZS].rearrange("(b z) -> b z", z=P))
-        nc.sync.dma_start(gate_wide[:], gate[:, :, ZS:].rearrange("r p z -> p r z"))
+            nc.sync.dma_start(
+                gate_rows[S_BLOCKS * r : S_BLOCKS * (r + 1), :], gate[r, 0, :V_FIRST].rearrange("(b z) -> b z", z=P)
+            )
+        nc.sync.dma_start(gate_wide[:], gate[:, :, V_FIRST:].rearrange("r p z -> p r z"))
         nc.sync.dma_start(wmw[:].bitcast(I32), wm_words.rearrange("o p b -> p o b").bitcast(I32))
         load_scale_rows(wms[:], wm_scales)
 
-        xw_slots = [keep.tile([P, XW_FIRST * C], U32, name="xw_first", align_bytes=64)]
-        xs_slots = [keep.tile([P, XS_FIRST * C], U8, name="xs_first", align_bytes=64)]
+        xw_slots = [
+            keep.tile([P, XW_FIRST * C], U32, name="xw_first", align_bytes=64),
+            shared.tile([P, (E - XW_FIRST) * C], U32, name="xw_rest", offset=AT_XW_REST, align_bytes=64),
+        ]
+        xs_slots = [
+            keep.tile([P, XS_FIRST * C], U8, name="xs_first", align_bytes=64),
+            shared.tile([P, (E - XS_FIRST) * C], U8, name="xs_rest", offset=AT_XS_REST, align_bytes=64),
+        ]
         y = [keep.tile([P, S], F32, name=f"y{j}") for j in range(LT)]
 
         def bank(k):
             return psum.tile([P, BANK], F32, name=f"bank{k}")
 
-        used = []
+        taken = []
 
         def next_bank():
-            used.append(len(used) % 8)
-            return bank(used[-1])
+            taken.append(len(taken) % BANKS)
+            return bank(taken[-1])
 
         def slots(tiles, e0, e1):
             first = tiles[0].shape[1] // C
@@ -137,7 +156,7 @@ def tile_moe_mhm_none_kernel(
             acc = next_bank()
             for e in range(e0, e1):
                 if j == 0 and e < W_CUTS[1]:
-                    words = ww_head[:, e]
+                    words = w_head[:, e]
                 else:
                     words = part(ww, W_CUTS, e)[:, 2 * P * j : 2 * P * (j + 1)]
                 nc.tensor.matmul_mx(
@@ -151,101 +170,90 @@ def tile_moe_mhm_none_kernel(
                 )
             copy(y[j][:, e0 * C : e1 * C], acc[:, : (e1 - e0) * C])
 
-        xs_slots.append(shared.tile([P, (E - XS_FIRST) * C], U8, name="xs_rest", offset=0, align_bytes=64))
-        xw_slots.append(shared.tile([P, (E - XW_FIRST) * C], U32, name="xw_rest", offset=2304, align_bytes=64))
-        gather_slots(xs_slots, xs, 0, 3)
+        gather_slots(xs_slots, xs, 0, XS_FIRST)
         gather_slots(xw_slots, xw, 0, 2)
         for j in range(LT):
             experts(j, 0, 2)
-        for e in range(2, 8, 2):
+        for e in range(2, E - 4, 2):
             gather_slots(xw_slots, xw, e, e + 2)
             gather_slots(xs_slots, xs, e + 1, e + 3)
             for j in range(LT):
                 experts(j, e, e + 2)
         turned_gate = next_bank()
         nc.tensor.transpose(turned_gate[:, :P], gate_rows[:], ident[:])
-        for c in range(3):
-            nc.scalar.copy(gate_cols[0, c][:], turned_gate[:, S_CUTS[c] : S_CUTS[c + 1]])
-        nc.scalar.copy(gate_cols1[:], turned_gate[:, 5:10])
-        gather_slots(xw_slots, xw, 8, 10)
-        gather_slots(xs_slots, xs, 9, 11)
+        for i in range(len(gate_first)):
+            nc.scalar.copy(gate_first[i][:], turned_gate[:, GATE_CUTS[i] : GATE_CUTS[i + 1]])
+        nc.scalar.copy(gate_second[:], turned_gate[:, S_BLOCKS : 2 * S_BLOCKS])
+        gather_slots(xw_slots, xw, E - 4, E - 2)
+        gather_slots(xs_slots, xs, E - 3, E - 1)
         for j in range(LT - 1):
-            experts(j, 8, 10)
-        gather_slots(xw_slots, xw, 10, 11)
-        gather_slots(xs_slots, xs, 11, 12)
-        gather_slots(xw_slots, xw, 11, 12)
-        experts(0, 10, 11, nc.vector.tensor_copy)
-        experts(0, 11, 12, nc.vector.tensor_copy)
-        experts(1, 10, 12, nc.vector.tensor_copy)
-        experts(2, 10, 12)
-        experts(3, 8, 10)
-        experts(3, 10, 12)
+            experts(j, E - 4, E - 2)
+        gather_slots(xw_slots, xw, E - 2, E - 1)
+        gather_slots(xs_slots, xs, E - 1, E)
+        gather_slots(xw_slots, xw, E - 1, E)
+        experts(0, E - 2, E - 1, nc.vector.tensor_copy)
+        experts(0, E - 1, E, nc.vector.tensor_copy)
+        experts(1, E - 2, E, nc.vector.tensor_copy)
+        experts(2, E - 2, E)
+        experts(3, E - 4, E - 2)
+        experts(3, E - 2, E)
 
         out_v = out.rearrange("(h p) t -> p h t", p=P)
 
-        def offsets(r, z0, z1):
-            return pos_sb[r][:, z0 // PER_COL : z1 // PER_COL]
+        def looked_up(r, j, z0, z1):
+            return y[j][:].indirect(pos_sb[r][:, z0 // PER_COL : z1 // PER_COL])
+
+        def fetch_gated(r, j, z0, z1, dst):
+            nc.vector.tensor_tensor(dst, looked_up(r, j, z0, z1), gate_wide[:, r, z0 - V_FIRST : z1 - V_FIRST], MULT)
+
+        def fetch_plain(r, j, z0, z1, dst):
+            nc.scalar.activation(dst, looked_up(r, j, z0, z1), COPY)
+            return dst
 
         def rounded_tile(z0, z1, offset=None):
             pool = keep if offset is None else shared
             return pool.tile([P, (z1 - z0) // P, 2, P, 2], BF16, name=f"rounded{z0}", align_bytes=64, offset=offset)
 
-        def fetch_gated(j, z0, z1, gated):
-            for r in range(2):
-                nc.vector.tensor_tensor(
-                    gated[:, r, :], y[j][:].indirect(offsets(r, z0, z1)), gate_wide[:, r, z0 - ZS : z1 - ZS], MULT
-                )
-            return gated
-
-        def fetch_one(r, j, z0, z1, gated):
-            nc.vector.tensor_tensor(
-                gated, y[j][:].indirect(offsets(r, z0, z1)), gate_wide[:, r, z0 - ZS : z1 - ZS], MULT
-            )
-            return gated
-
-        def add_pair(total, one, other):
-            nc.vector.tensor_tensor(total, one, other, ADD)
+        def grouped_tile(z0, z1):
+            return keep.tile([P, z1 - z0, 4], BF16, name=f"grouped{z0}", align_bytes=64)
 
         def bank16(k):
             return psum.tile([P, 2, H], BF16, name=f"bank{k}")
 
-        def turn16(banks, total, j):
-            for b in range(total.shape[1] // P):
+        def turn_sums(banks, sums, j):
+            for b in range(sums.shape[1] // P):
                 nc.tensor.transpose(
-                    banks[b // 2][:, b % 2, P * j : P * (j + 1)], total[:, P * b : P * (b + 1)], ident16[:]
+                    banks[b // 2][:, b % 2, P * j : P * (j + 1)], sums[:, P * b : P * (b + 1)], ident16[:]
                 )
 
         def regroup(turned, rounded, b0):
             nc.scalar.copy(
-                rounded[:, b0 : b0 + 2].rearrange("z b u p e -> z (b u p e)").bitcast(F32).rearrange(
-                    "z (b u p) -> z b u p", b=2, u=2
-                ),
+                rounded[:, b0 : b0 + 2]
+                .rearrange("z b u p e -> z (b u p e)")
+                .bitcast(F32)
+                .rearrange("z (b u p) -> z b u p", b=2, u=2),
                 turned[:].rearrange("z b l -> z (b l)").bitcast(F32).rearrange("z (b p u) -> z b u p", b=2, u=2),
             )
 
-        def add_up(gated, j, rounded, k):
-            blocks = rounded.shape[1]
+        def add_up(gated, j0, rounded, k):
+            tiles = gated.shape[1]
             total = bank(k)
-            for r in range(2):
-                for b in range(blocks):
+            for j in range(tiles):
+                for r in range(2):
                     nc.tensor.matmul(
-                        total[:, P * b : P * (b + 1)],
-                        lhsT=gated[:, r, P * b : P * (b + 1)],
+                        total[:, P * j : P * (j + 1)],
+                        lhsT=gated[:, j, r, :],
                         rhs=ident[:],
                         is_transpose=True,
-                        start=(r == 0 and b == 0),
-                        stop=(r == 1 and b == blocks - 1),
+                        start=(r == 0),
+                        stop=(r == 1),
                     )
             nc.scalar.copy(
-                rounded[:, :, :, 32 * j : 32 * (j + 1), :].rearrange("z b u p e -> z u b p e"),
-                total[:, : P * blocks].rearrange("z (b p u e) -> z u b p e", p=32, u=2, e=2),
+                rounded[:, 0, :, 32 * j0 : 32 * (j0 + tiles), :],
+                total[:, : P * tiles].rearrange("z (p u e) -> z u p e", u=2, e=2),
             )
 
-        def fetch_plain(r, j, z0, z1, plain):
-            nc.scalar.activation(plain, y[j][:].indirect(offsets(r, z0, z1)), COPY)
-            return plain
-
-        def turn(plains, b, k):
+        def turn_plain(plains, b, k):
             turned = bank(k)
             for j in range(LT):
                 nc.tensor.transpose(turned[:, P * j : P * (j + 1)], plains[j][:, P * b : P * (b + 1)], ident[:])
@@ -253,11 +261,13 @@ def tile_moe_mhm_none_kernel(
 
         def first_product(turned, block):
             first = keep.tile([P, 2, P, 2], F32, name=f"first{block}")
+            tile = max(i for i in range(len(gate_first)) if GATE_CUTS[i] <= block)
+            column = block - GATE_CUTS[tile]
             nc.scalar.activation(
                 first[:],
                 turned[:].rearrange("z (p u e) -> z u p e", u=2, e=2),
                 COPY,
-                scale=gate_cols[0, 0][:, block : block + 1] if block < 3 else gate_cols[0, block - 2][:],
+                scale=gate_first[tile][:, column : column + 1],
             )
             return first
 
@@ -266,7 +276,7 @@ def tile_moe_mhm_none_kernel(
                 nc.vector.scalar_tensor_tensor(
                     rounded[:, b, u],
                     turned[:].rearrange("z (p u e) -> z u p e", u=2, e=2)[:, u],
-                    gate_cols1[:, block : block + 1],
+                    gate_second[:, block : block + 1],
                     first[:, u],
                     MULT,
                     ADD,
@@ -277,16 +287,13 @@ def tile_moe_mhm_none_kernel(
             for b in range(b0, b1):
                 pairs = rounded[:, b].rearrange("z u p e -> z (u p e)").bitcast(F32)
                 for u in range(2):
-                    k = 2 * (b - b0) + u
-                    nc.tensor.transpose(back[:, P * k : P * (k + 1)], pairs[:, P * u : P * (u + 1)], ident[:])
+                    at = P * (2 * (b - b0) + u)
+                    nc.tensor.transpose(back[:, at : at + P], pairs[:, P * u : P * (u + 1)], ident[:])
             words = grouped[:, P * b0 : P * b1, :].rearrange("p z t -> p (z t)").bitcast(F32)
             nc.scalar.copy(
                 words.rearrange("p (b z u) -> p b z u", z=P, u=2),
                 back[:, : 2 * P * (b1 - b0)].rearrange("p (b u z) -> p b z u", u=2, z=P),
             )
-
-        def grouped_tile(z0, z1):
-            return keep.tile([P, z1 - z0, 4], BF16, name=f"grouped{z0}", align_bytes=64)
 
         def quantize(grouped, z0):
             width = grouped.shape[1]
@@ -297,125 +304,132 @@ def tile_moe_mhm_none_kernel(
             )
             return codes, scales, z0
 
+        def merge_half(acc, heads, h, t0, t1):
+            for o, (codes, scales, z0) in enumerate(heads):
+                cols = slice(o * T + t0 - z0, o * T + t1 - z0)
+                nc.tensor.matmul_mx(
+                    out=acc,
+                    lhsT=wmw[:, o, 2 * P * h : 2 * P * (h + 1)].bitcast(FP4X4),
+                    lhsT_scale=wms[:, o, P * h : P * (h + 1)],
+                    rhs=codes[:, cols].bitcast(FP8X4),
+                    rhs_scale=scales[:, cols],
+                    start=(o == 0),
+                    stop=(o == D - 1),
+                )
+
         def merge(heads, t0, t1, k):
             width = t1 - t0
             acc = bank(k)
             for h in range(N // P):
-                for o in range(D):
-                    codes, scales, z0 = heads[o]
-                    cols = slice(o * T + t0 - z0, o * T + t1 - z0)
-                    nc.tensor.matmul_mx(
-                        out=acc[:, h * width : (h + 1) * width],
-                        lhsT=wmw[:, o, 2 * P * h : 2 * P * (h + 1)].bitcast(FP4X4),
-                        lhsT_scale=wms[:, o, P * h : P * (h + 1)],
-                        rhs=codes[:, cols].bitcast(FP8X4),
-                        rhs_scale=scales[:, cols],
-                        start=(o == 0),
-                        stop=(o == D - 1),
-                    )
+                merge_half(acc[:, h * width : (h + 1) * width], heads, h, t0, t1)
+            return acc
 
-            def store(copy, offset=None):
-                pool = keep if offset is None else shared
-                staged = pool.tile([P, N // P, width], F32, name=f"staged{t0}", offset=offset)
-                copy(staged[:].rearrange("p h t -> p (h t)"), acc[:, : (N // P) * width])
-                nc.sync.dma_start(out_v[:, :, t0:t1], staged[:])
+        def store(acc, t0, t1, copy, offset=None):
+            width = t1 - t0
+            pool = keep if offset is None else shared
+            staged = pool.tile([P, N // P, width], F32, name=f"staged{t0}", offset=offset)
+            copy(staged[:].rearrange("p h t -> p (h t)"), acc[:, : (N // P) * width])
+            nc.sync.dma_start(out_v[:, :, t0:t1], staged[:])
 
-            return store
+        rounded_first, rounded_mid = rounded_tile(V_FIRST, V_MID), rounded_tile(V_MID, V_LAST, AT_ROUNDED_MID)
+        rounded_s = rounded_tile(0, S_MID, AT_ROUNDED_S)
+        rounded_3, rounded_4 = rounded_tile(S_MID, S_MID + P), rounded_tile(S_MID + P, V_FIRST)
+        grouped_first, grouped_mid = grouped_tile(V_FIRST, V_MID), grouped_tile(V_MID, V_LAST)
+        grouped_last, grouped_s = grouped_tile(V_LAST, Z), grouped_tile(0, S_MID)
+        grouped_3, grouped_4 = grouped_tile(S_MID, S_MID + P), grouped_tile(S_MID + P, V_FIRST)
 
-        rx, ry = rounded_tile(640, 1152, 31232), rounded_tile(1152, 1408, 35328)
-        r0, r3, r4 = rounded_tile(0, 384, 23040), rounded_tile(384, 512), rounded_tile(512, 640)
-        gx, gy, gz = grouped_tile(640, 1152), grouped_tile(1152, 1408), grouped_tile(1408, 1536)
-        g0, g3, g4 = grouped_tile(0, 384), grouped_tile(384, 512), grouped_tile(512, 640)
-
-        xt = keep.tile([P, 2 * LT, 512], F32, name="xt")
-        cx = shared.tile([P, LT, 512], BF16, name="cx", offset=27136)
-        pt = keep.tile([P, 7, 384], F32, name="pt")
-        pt7 = shared.tile([P, 384], F32, name="pt7", offset=10784)
-        x_banks = [bank16(0), bank16(1)]
-        fetch_one(0, 0, 640, 1152, xt[:, 0])
+        wide, mid, narrow = V_MID - V_FIRST, V_LAST - V_MID, V_FIRST - S_MID
+        fetched = keep.tile([P, 2 * LT, wide], F32, name="fetched")
+        sums = keep.tile([P, LT - 1, wide], BF16, name="sums")
+        plain = keep.tile([P, 2 * LT - 1, S_MID], F32, name="plain")
+        plain_end = shared.tile([P, S_MID], F32, name="plain_end", offset=AT_PLAIN_END)
+        fetch_gated(0, 0, V_FIRST, V_MID, fetched[:, 0])
         for j in range(LT - 1):
-            fetch_one(1, j, 640, 1152, xt[:, 2 * j + 1])
-            fetch_one(0, j + 1, 640, 1152, xt[:, 2 * j + 2])
-            add_pair(cx[:, j], xt[:, 2 * j], xt[:, 2 * j + 1])
-            turn16(x_banks, cx[:, j], j)
-        fetch_one(1, 3, 640, 1152, xt[:, 7])
-        plains = [fetch_plain(0, j, 0, 384, pt[:, j]) for j in range(LT)]
-        turned = [turn(plains, b, 2 + b) for b in range(3)]
-        plains = [fetch_plain(1, j, 0, 384, pt[:, 4 + j] if j < 3 else pt7[:]) for j in range(LT)]
-        firsts = [first_product(turned[b], b) for b in range(3)]
-        turned = [turn(plains, b, 5 + b) for b in range(3)]
-        y00 = keep.tile([P, 256], F32, name="y00")
-        fetch_one(0, 0, 1152, 1408, y00[:])
-        nc.gpsimd.tensor_tensor(cx[:, 3], xt[:, 6], xt[:, 7], ADD)
-        turn16(x_banks, cx[:, 3], 3)
+            fetch_gated(1, j, V_FIRST, V_MID, fetched[:, 2 * j + 1])
+            fetch_gated(0, j + 1, V_FIRST, V_MID, fetched[:, 2 * j + 2])
+            nc.vector.tensor_tensor(sums[:, j], fetched[:, 2 * j], fetched[:, 2 * j + 1], ADD)
+        fetch_gated(1, LT - 1, V_FIRST, V_MID, fetched[:, 2 * LT - 1])
+        plains = [fetch_plain(0, j, 0, S_MID, plain[:, j]) for j in range(LT)]
+        turned_1 = [turn_plain(plains, b, 2 + b) for b in range(3)]
+        plains = [fetch_plain(1, j, 0, S_MID, plain[:, LT + j] if j < LT - 1 else plain_end[:]) for j in range(LT)]
+        firsts = [first_product(turned_1[b], b) for b in range(3)]
+        turned_2 = [turn_plain(plains, b, 5 + b) for b in range(3)]
+        mid_start = keep.tile([P, mid], F32, name="mid_start")
+        fetch_gated(0, 0, V_MID, V_LAST, mid_start[:])
+        sum_end = shared.tile([P, wide], BF16, name="sum_end", offset=AT_SUM_END)
+        nc.gpsimd.tensor_tensor(sum_end[:], fetched[:, 2 * LT - 2], fetched[:, 2 * LT - 1], ADD)
+        first_banks = [bank16(2), bank16(3)]
+        for j in range(LT):
+            turn_sums(first_banks, sums[:, j] if j < LT - 1 else sum_end[:], j)
         for b in range(3):
-            second_product(turned[b], firsts[b], b, r0, b)
-        pa = keep.tile([P, LT, 256], F32, name="pa")
-        plains = [fetch_plain(0, j, 384, 640, pa[:, j]) for j in range(LT)]
-        regroup(x_banks[0], rx, 0)
-        regroup(x_banks[1], rx, 2)
-        turned = [turn(plains, b, 2 + b) for b in range(2)]
-        pb = shared.tile([P, LT, 256], F32, name="pb", offset=27136)
-        plains = [fetch_plain(1, j, 384, 640, pb[:, j]) for j in range(2)]
-        turn_back(gx, rx, 0, 2, 4)
-        turn_back(gx, rx, 2, 4, 7)
-        turn_back(g0, r0, 0, 2, 0)
-        turn_back(g0, r0, 2, 3, 1)
-        plains.extend([fetch_plain(1, j, 384, 640, pb[:, j]) for j in range(2, LT)])
-        first3, turned4 = first_product(turned[0], 3), turned[1]
-        turned = [turn(plains, b, 5 + b) for b in range(2)]
-        yt = shared.tile([P, 6, 256], F32, name="yt", offset=10752)
-        cy = keep.tile([P, LT, 256], BF16, name="cy")
-        y_banks = [bank16(0)]
-        yt3 = shared.tile([P, 2, 256], F32, name="yt3", offset=31232)
+            second_product(turned_2[b], firsts[b], b, rounded_s, b)
+
+        plain_a = keep.tile([P, LT, narrow], F32, name="plain_a")
+        plains = [fetch_plain(0, j, S_MID, V_FIRST, plain_a[:, j]) for j in range(LT)]
+        regroup(first_banks[0], rounded_first, 0)
+        regroup(first_banks[1], rounded_first, 2)
+        turned_1 = [turn_plain(plains, b, b) for b in range(2)]
+        plain_b = keep.tile([P, narrow], F32, name="plain_b")
+        plain_late = shared.tile([P, LT - 1, narrow], F32, name="plain_late", offset=AT_PLAIN_LATE)
+        plains = [fetch_plain(1, 0, S_MID, V_FIRST, plain_b[:]), fetch_plain(1, 1, S_MID, V_FIRST, plain_late[:, 0])]
+        turn_back(grouped_first, rounded_first, 0, 2, 4)
+        turn_back(grouped_first, rounded_first, 2, 4, 7)
+        turn_back(grouped_s, rounded_s, 0, 2, 2)
+        turn_back(grouped_s, rounded_s, 2, 3, 3)
+        plains.extend([fetch_plain(1, j, S_MID, V_FIRST, plain_late[:, j - 1]) for j in range(2, LT)])
+        first_3 = first_product(turned_1[0], 3)
+        turned_2 = [turn_plain(plains, b, 5 + b) for b in range(2)]
+
+        mid_fetched = shared.tile([P, 2 * LT - 1, mid], F32, name="mid_fetched", offset=AT_MID_FETCH)
+        mid_sums = keep.tile([P, LT, mid], BF16, name="mid_sums")
+        mid_banks = [bank16(2)]
+        mid_end = shared.tile([P, mid], F32, name="mid_end", offset=AT_MID_END)
         for j in range(LT - 1):
-            fetch_one(1, j, 1152, 1408, yt[:, 2 * j + 1])
-            fetch_one(0, j + 1, 1152, 1408, yt[:, 2 * j + 2] if j < 2 else yt3[:, 0])
-            add_pair(cy[:, j], yt[:, 2 * j] if j else y00[:], yt[:, 2 * j + 1])
-            turn16(y_banks, cy[:, j], j)
-        fetch_one(1, 3, 1152, 1408, yt3[:, 1])
-        qx = quantize(gx, 640)
-        add_pair(cy[:, 3], yt3[:, 0], yt3[:, 1])
-        turn16(y_banks, cy[:, 3], 3)
-        q0 = quantize(g0, 0)
-        regroup(y_banks[0], ry, 0)
-        first4 = first_product(turned4, 4)
-        early = shared.tile([P, LT - 1, 2, P], F32, name="early", offset=23040)
-        for j in range(LT - 1):
-            fetch_gated(j, 1408, 1536, early[:, j])
-        second_product(turned[0], first3, 3, r3, 0)
-        last = shared.tile([P, 2, P], F32, name="last", offset=27104)
-        fetch_gated(LT - 1, 1408, 1536, last[:])
-        second_product(turned[1], first4, 4, r4, 0)
-        store_first = merge((q0, qx), 0, 256, 4)
-        turn_back(gy, ry, 0, 2, 1)
-        rz = rounded_tile(1408, 1536, 35328)
-        total = bank(0)
+            fetch_gated(1, j, V_MID, V_LAST, mid_fetched[:, 2 * j + 1])
+            fetch_gated(0, j + 1, V_MID, V_LAST, mid_fetched[:, 2 * j + 2])
+            nc.vector.tensor_tensor(
+                mid_sums[:, j], mid_fetched[:, 2 * j] if j else mid_start[:], mid_fetched[:, 2 * j + 1], ADD
+            )
+            turn_sums(mid_banks, mid_sums[:, j], j)
+        fetch_gated(1, LT - 1, V_MID, V_LAST, mid_end[:])
+        codes_first = quantize(grouped_first, V_FIRST)
+        nc.vector.tensor_tensor(mid_sums[:, LT - 1], mid_fetched[:, 2 * LT - 2], mid_end[:], ADD)
+        turn_sums(mid_banks, mid_sums[:, LT - 1], LT - 1)
+        codes_s = quantize(grouped_s, 0)
+        regroup(mid_banks[0], rounded_mid, 0)
+        first_4 = first_product(turned_1[1], 4)
+
+        last_early = shared.tile([P, LT - 1, 2, P], F32, name="last_early", offset=AT_LAST_EARLY)
         for j in range(LT - 1):
             for r in range(2):
-                nc.tensor.matmul(
-                    total[:, P * j : P * (j + 1)],
-                    lhsT=early[:, j, r, :],
-                    rhs=ident[:],
-                    is_transpose=True,
-                    start=(r == 0),
-                    stop=(r == 1),
-                )
-        nc.scalar.copy(
-            rz[:, 0, :, : 32 * (LT - 1), :],
-            total[:, : P * (LT - 1)].rearrange("z (p u e) -> z u p e", u=2, e=2),
-        )
-        turn_back(g3, r3, 0, 1, 5)
-        add_up(last[:], LT - 1, rz, 3)
-        turn_back(g4, r4, 0, 1, 6)
-        store_second = merge((q0, qx), 256, 384, 0)
-        turn_back(gz, rz, 0, 1, 2)
-        qy = quantize(gy, 1152)
-        q3 = quantize(g3, 384)
-        store_first(nc.vector.tensor_copy, 26112)
-        q4 = quantize(g4, 512)
-        store_second(nc.vector.tensor_copy)
-        qz = quantize(gz, 1408)
-        merge((q3, qy), 384, 512, 5)(nc.vector.tensor_copy)
-        merge((q4, qy), 512, 640, 6)(nc.scalar.copy)
-        merge((qx, qz), 640, 768, 2)(nc.vector.tensor_copy)
+                fetch_gated(r, j, V_LAST, Z, last_early[:, j, r, :])
+        second_product(turned_2[0], first_3, 3, rounded_3, 0)
+        last_end = shared.tile([P, 1, 2, P], F32, name="last_end", offset=AT_LAST_END)
+        for r in range(2):
+            fetch_gated(r, LT - 1, V_LAST, Z, last_end[:, 0, r, :])
+        second_product(turned_2[1], first_4, 4, rounded_4, 0)
+
+        acc_a = merge((codes_s, codes_first), 0, 2 * P, 4)
+        turn_back(grouped_mid, rounded_mid, 0, 2, 3)
+        rounded_last = rounded_tile(V_LAST, Z, AT_ROUNDED_MID)
+        add_up(last_early, 0, rounded_last, 2)
+        turn_back(grouped_3, rounded_3, 0, 1, 5)
+        add_up(last_end, LT - 1, rounded_last, 1)
+        turn_back(grouped_4, rounded_4, 0, 1, 6)
+        acc_b = merge((codes_s, codes_first), 2 * P, 3 * P, 2)
+        turn_back(grouped_last, rounded_last, 0, 1, 0)
+        codes_mid = quantize(grouped_mid, V_MID)
+        codes_3 = quantize(grouped_3, S_MID)
+        store(acc_a, 0, 2 * P, nc.vector.tensor_copy, AT_STAGED)
+        codes_4 = quantize(grouped_4, S_MID + P)
+        store(acc_b, 2 * P, 3 * P, nc.vector.tensor_copy)
+        codes_last = quantize(grouped_last, V_LAST)
+        store(merge((codes_3, codes_mid), 3 * P, 4 * P, 5), 3 * P, 4 * P, nc.vector.tensor_copy)
+        store(merge((codes_4, codes_mid), 4 * P, 5 * P, 6), 4 * P, 5 * P, nc.scalar.copy)
+        staged_last = keep.tile([P, N // P, P], F32, name="staged_last")
+        halves = [bank(0), bank(7)]
+        for h in range(N // P):
+            merge_half(halves[h][:, :P], (codes_first, codes_last), h, 5 * P, T)
+        nc.vector.tensor_copy(staged_last[:, 0], halves[0][:, :P])
+        nc.scalar.copy(staged_last[:, 1], halves[1][:, :P])
+        nc.sync.dma_start(out_v[:, :, 5 * P : T], staged_last[:])

@@ -26,20 +26,14 @@ BANK = 512
 BANKS = 8
 PER_COL = 16
 
-W_CUTS = (0, 2, 4, 8, 12)
-WS_CUTS = (0, 4, 12)
-XW_FIRST = 4
+W_CUTS = (0, 1, 3, 7, 12)
+WS_CUTS = (0, 5, 12)
+XW_FIRST = 5
 XS_FIRST = 3
 S_MID, V_FIRST, V_MID, V_LAST = 384, 640, 1152, 1408
 S_BLOCKS = V_FIRST // P
-GATE_CUTS = (0, 2, 3, 4, 5)
 
-AT_XS_REST, AT_W_HEAD, AT_XW_REST = 0, 2048, 2304
-AT_MID_FETCH, AT_GATE_2, AT_PLAIN_END = 10752, 10752, 10784
-AT_MID_END, AT_ROUNDED_S, AT_LAST_EARLY = 22528, 23040, 23552
-AT_GATE_01, AT_SUM_END, AT_PLAIN_LATE = 27136, 27136, 27136
-AT_GATE_3, AT_LAST_END, AT_STAGED = 27104, 27104, 26112
-AT_ROUNDED_MID = 35328
+AT_XS_REST, AT_W_FIRST, AT_XW_REST = 0, 2048, 2304
 
 
 def tile_moe_mhm_none_kernel(
@@ -48,26 +42,28 @@ def tile_moe_mhm_none_kernel(
     nc = tc.nc
     with ExitStack() as ctx:
         keep = ctx.enter_context(tc.tile_pool(name="keep", bufs=1))
-        shared = ctx.enter_context(tc.tile_pool(name="shared", bufs=1))
+        head = ctx.enter_context(tc.tile_pool(name="head", bufs=1))
+        slot = ctx.enter_context(tc.tile_pool(name="slot", bufs=1))
         psum = ctx.enter_context(tc.psum_pool(name="psum", bufs=1))
+
+        def in_slot(tag, shape, dtype, name):
+            return slot.tile(shape, dtype, name=name, tag=tag, align_bytes=64)
 
         offs_sb = keep.tile([P, S // PER_COL], U16, name="offs_sb")
         pos_sb = [keep.tile([P, Z // PER_COL], U16, name=f"pos_sb{r}") for r in range(2)]
         xw = keep.tile([P, Z], U32, name="xw")
         xs = keep.tile([P, Z], U8, name="xs", align_bytes=64)
         ws = [keep.tile([P, b - a, H], U8, name=f"ws{a}", align_bytes=64) for a, b in zip(WS_CUTS, WS_CUTS[1:])]
-        ww = [keep.tile([P, b - a, 2 * H], U8, name=f"ww{a}", align_bytes=64) for a, b in zip(W_CUTS, W_CUTS[1:])]
+        ww = [head.tile([P, W_CUTS[1], 2 * H], U8, name="ww0", offset=AT_W_FIRST, align_bytes=64)]
+        ww.extend(
+            [keep.tile([P, b - a, 2 * H], U8, name=f"ww{a}", align_bytes=64) for a, b in zip(W_CUTS[1:], W_CUTS[2:])]
+        )
         wmw = keep.tile([P, D, 2 * N], U8, name="wmw", align_bytes=64)
         wms = keep.tile([P, D, N], U8, name="wms", align_bytes=64)
         ident = keep.tile([P, P], F32, name="ident")
-        ident16 = keep.tile([P, P], BF16, name="ident16")
-        gate_rows = keep.tile([P, P], F32, name="gate_rows")
-        w_head = shared.tile([P, W_CUTS[1], 2 * P], U8, name="w_head", offset=AT_W_HEAD, align_bytes=64)
         gate_first = [
-            shared.tile([P, 2], F32, name="gate_first01", offset=AT_GATE_01),
-            shared.tile([P, 1], F32, name="gate_first2", offset=AT_GATE_2),
-            shared.tile([P, 1], F32, name="gate_first3", offset=AT_GATE_3),
-            keep.tile([P, 1], F32, name="gate_first4"),
+            in_slot("after_first_products", [P, S_MID // P], F32, "gate_first_a"),
+            keep.tile([P, (V_FIRST - S_MID) // P], F32, name="gate_first_b"),
         ]
         gate_second = keep.tile([P, S_BLOCKS], F32, name="gate_second")
         gate_wide = keep.tile([P, 2, Z - V_FIRST], F32, name="gate_wide")
@@ -89,47 +85,45 @@ def tile_moe_mhm_none_kernel(
                 w_words[W_CUTS[i] : W_CUTS[i + 1], 0].rearrange("e p b -> p e b").bitcast(I32),
             )
 
+        def load_gate_columns(dst, r, z0, z1):
+            with nc.allow_non_contiguous_dma(reason="one gate value a partition and block"):
+                nc.sync.dma_start(dst[:], gate[r, 0, z0:z1].rearrange("(b z) -> z b", z=P))
+
         nc.vector.memset(xs[:].bitcast(I32), 0)
         nc.vector.memset(ws[0][:].rearrange("p e l -> p (e l)").bitcast(I32), 0)
         nc.vector.memset(ident[:], 0.0)
-        nc.vector.memset(ident16[:], 0.0)
         nc.vector.memset(ws[1][:].rearrange("p e l -> p (e l)").bitcast(I32), 0)
         nc.vector.memset(wms[:].rearrange("p o n -> p (o n)").bitcast(I32), 0)
-        nc.vector.memset(gate_rows[:], 0.0)
         make_identity(nc, ident[:], nomemset=True)
-        make_identity(nc, ident16[:], nomemset=True)
 
         nc.sync.dma_start(offs_sb[:], offs)
-        head_words = w_words[: W_CUTS[1], 0].rearrange("e p b -> p e b")
-        nc.sync.dma_start(w_head[:].bitcast(I32), head_words[:, :, : 2 * P].bitcast(I32))
+        load_words(0)
         load_scale_rows(xs[:].rearrange("p (o t) -> p o t", o=D), x_scales)
         nc.sync.dma_start(
             xw[:].bitcast(I32).rearrange("p (o t) -> p o t", o=D),
             x_words.rearrange("o p t d -> p o (t d)").bitcast(I32),
         )
-        nc.sync.dma_start(ww[0][:, :, 2 * P :].bitcast(I32), head_words[:, :, 2 * P :].bitcast(I32))
-        load_scale_rows(ws[0][:], w_scales[WS_CUTS[0] : WS_CUTS[1], 0])
         load_words(1)
-        load_scale_rows(ws[1][:], w_scales[WS_CUTS[1] : WS_CUTS[2], 0])
+        load_scale_rows(ws[0][:], w_scales[WS_CUTS[0] : WS_CUTS[1], 0])
         load_words(2)
+        load_scale_rows(ws[1][:], w_scales[WS_CUTS[1] : WS_CUTS[2], 0])
         load_words(3)
         nc.sync.dma_start(pos_sb[0][:], pos1)
         nc.sync.dma_start(pos_sb[1][:], pos2)
-        for r in range(2):
-            nc.sync.dma_start(
-                gate_rows[S_BLOCKS * r : S_BLOCKS * (r + 1), :], gate[r, 0, :V_FIRST].rearrange("(b z) -> b z", z=P)
-            )
         nc.sync.dma_start(gate_wide[:], gate[:, :, V_FIRST:].rearrange("r p z -> p r z"))
+        load_gate_columns(gate_first[0], 0, 0, S_MID)
+        load_gate_columns(gate_first[1], 0, S_MID, V_FIRST)
+        load_gate_columns(gate_second, 1, 0, V_FIRST)
         nc.sync.dma_start(wmw[:].bitcast(I32), wm_words.rearrange("o p b -> p o b").bitcast(I32))
         load_scale_rows(wms[:], wm_scales)
 
         xw_slots = [
             keep.tile([P, XW_FIRST * C], U32, name="xw_first", align_bytes=64),
-            shared.tile([P, (E - XW_FIRST) * C], U32, name="xw_rest", offset=AT_XW_REST, align_bytes=64),
+            head.tile([P, (E - XW_FIRST) * C], U32, name="xw_rest", offset=AT_XW_REST, align_bytes=64),
         ]
         xs_slots = [
             keep.tile([P, XS_FIRST * C], U8, name="xs_first", align_bytes=64),
-            shared.tile([P, (E - XS_FIRST) * C], U8, name="xs_rest", offset=AT_XS_REST, align_bytes=64),
+            head.tile([P, (E - XS_FIRST) * C], U8, name="xs_rest", offset=AT_XS_REST, align_bytes=64),
         ]
         y = [keep.tile([P, S], F32, name=f"y{j}") for j in range(LT)]
 
@@ -152,51 +146,48 @@ def tile_moe_mhm_none_kernel(
             cols = slice(e0 * C // PER_COL, e1 * C // PER_COL)
             nc.vector.tensor_copy(slots(dst, e0, e1), window[:].indirect(offs_sb[:, cols]))
 
+        def expert(acc, j, e):
+            nc.tensor.matmul_mx(
+                out=acc,
+                lhsT=part(ww, W_CUTS, e)[:, 2 * P * j : 2 * P * (j + 1)].bitcast(FP4X4),
+                lhsT_scale=part(ws, WS_CUTS, e)[:, P * j : P * (j + 1)],
+                rhs=slots(xw_slots, e, e + 1).bitcast(FP8X4),
+                rhs_scale=slots(xs_slots, e, e + 1),
+                start=True,
+                stop=True,
+            )
+
         def experts(j, e0, e1, copy=nc.scalar.copy):
             acc = next_bank()
             for e in range(e0, e1):
-                if j == 0 and e < W_CUTS[1]:
-                    words = w_head[:, e]
-                else:
-                    words = part(ww, W_CUTS, e)[:, 2 * P * j : 2 * P * (j + 1)]
-                nc.tensor.matmul_mx(
-                    out=acc[:, (e - e0) * C : (e - e0 + 1) * C],
-                    lhsT=words.bitcast(FP4X4),
-                    lhsT_scale=part(ws, WS_CUTS, e)[:, P * j : P * (j + 1)],
-                    rhs=slots(xw_slots, e, e + 1).bitcast(FP8X4),
-                    rhs_scale=slots(xs_slots, e, e + 1),
-                    start=True,
-                    stop=True,
-                )
+                expert(acc[:, (e - e0) * C : (e - e0 + 1) * C], j, e)
             copy(y[j][:, e0 * C : e1 * C], acc[:, : (e1 - e0) * C])
 
+        def last_expert(j0, copy):
+            acc = next_bank()
+            for i in range(2):
+                expert(acc[:, i * C : (i + 1) * C], j0 + i, E - 1)
+            for i in range(2):
+                copy(y[j0 + i][:, (E - 1) * C :], acc[:, i * C : (i + 1) * C])
+
         gather_slots(xs_slots, xs, 0, XS_FIRST)
-        gather_slots(xw_slots, xw, 0, 2)
+        gather_slots(xw_slots, xw, 0, 1)
         for j in range(LT):
-            experts(j, 0, 2)
-        for e in range(2, E - 4, 2):
+            experts(j, 0, 1)
+        gather_slots(xw_slots, xw, 1, 3)
+        for j in range(LT):
+            experts(j, 1, 3)
+        for e in range(3, E - 1, 2):
             gather_slots(xw_slots, xw, e, e + 2)
-            gather_slots(xs_slots, xs, e + 1, e + 3)
+            gather_slots(xs_slots, xs, e, e + 2)
             for j in range(LT):
-                experts(j, e, e + 2)
-        turned_gate = next_bank()
-        nc.tensor.transpose(turned_gate[:, :P], gate_rows[:], ident[:])
-        for i in range(len(gate_first)):
-            nc.scalar.copy(gate_first[i][:], turned_gate[:, GATE_CUTS[i] : GATE_CUTS[i + 1]])
-        nc.scalar.copy(gate_second[:], turned_gate[:, S_BLOCKS : 2 * S_BLOCKS])
-        gather_slots(xw_slots, xw, E - 4, E - 2)
-        gather_slots(xs_slots, xs, E - 3, E - 1)
-        for j in range(LT - 1):
-            experts(j, E - 4, E - 2)
-        gather_slots(xw_slots, xw, E - 2, E - 1)
-        gather_slots(xs_slots, xs, E - 1, E)
-        gather_slots(xw_slots, xw, E - 1, E)
-        experts(0, E - 2, E - 1, nc.vector.tensor_copy)
-        experts(0, E - 1, E, nc.vector.tensor_copy)
-        experts(1, E - 2, E, nc.vector.tensor_copy)
-        experts(2, E - 2, E)
-        experts(3, E - 4, E - 2)
-        experts(3, E - 2, E)
+                last = e == E - 3 and j == LT - 1
+                if last:
+                    gather_slots(xs_slots, xs, E - 1, E)
+                    gather_slots(xw_slots, xw, E - 1, E)
+                experts(j, e, e + 2, nc.vector.tensor_copy if last else nc.scalar.copy)
+        last_expert(0, nc.vector.tensor_copy)
+        last_expert(2, nc.scalar.copy)
 
         out_v = out.rearrange("(h p) t -> p h t", p=P)
 
@@ -206,68 +197,55 @@ def tile_moe_mhm_none_kernel(
         def fetch_gated(r, j, z0, z1, dst):
             nc.vector.tensor_tensor(dst, looked_up(r, j, z0, z1), gate_wide[:, r, z0 - V_FIRST : z1 - V_FIRST], MULT)
 
-        def fetch_plain(r, j, z0, z1, dst):
-            nc.scalar.activation(dst, looked_up(r, j, z0, z1), COPY)
-            return dst
+        def add_turned(total, at, fetched, first, last):
+            blocks = fetched.shape[1] // P
+            step = BANK // blocks
+            for b in range(blocks):
+                nc.tensor.matmul(
+                    total[:, at + step * b : at + step * b + P],
+                    lhsT=fetched[:, P * b : P * (b + 1)],
+                    rhs=ident[:],
+                    is_transpose=True,
+                    start=(first and b == 0),
+                    stop=(last and b == blocks - 1),
+                )
 
-        def rounded_tile(z0, z1, offset=None):
-            pool = keep if offset is None else shared
-            return pool.tile([P, (z1 - z0) // P, 2, P, 2], BF16, name=f"rounded{z0}", align_bytes=64, offset=offset)
+        def gated_step(r, j, z0, z1, dst, total, at, first, last):
+            fetch_gated(r, j, z0, z1, dst)
+            add_turned(total, at, dst, first, last)
+
+        def round_sums(total, rounded, j0, tiles):
+            blocks = rounded.shape[1]
+            nc.scalar.copy(
+                rounded[:, :, :, 32 * j0 : 32 * (j0 + tiles), :],
+                total[:]
+                .rearrange("z (b l) -> z b l", b=blocks)[:, :, : P * tiles]
+                .rearrange("z b (p u e) -> z b u p e", u=2, e=2),
+            )
+
+        def plain_step(r, j, z0, z1, dst, turned, on_vector=False):
+            if on_vector:
+                nc.vector.tensor_copy(dst, looked_up(r, j, z0, z1))
+            else:
+                nc.scalar.activation(dst, looked_up(r, j, z0, z1), COPY)
+            for b in range(len(turned)):
+                nc.tensor.transpose(turned[b][:, P * j : P * (j + 1)], dst[:, P * b : P * (b + 1)], ident[:])
+
+        def rounded_tile(z0, z1):
+            return in_slot(f"rounded{z0}", [P, (z1 - z0) // P, 2, P, 2], BF16, f"rounded{z0}")
 
         def grouped_tile(z0, z1):
             return keep.tile([P, z1 - z0, 4], BF16, name=f"grouped{z0}", align_bytes=64)
 
-        def bank16(k):
-            return psum.tile([P, 2, H], BF16, name=f"bank{k}")
-
-        def turn_sums(banks, sums, j):
-            for b in range(sums.shape[1] // P):
-                nc.tensor.transpose(
-                    banks[b // 2][:, b % 2, P * j : P * (j + 1)], sums[:, P * b : P * (b + 1)], ident16[:]
-                )
-
-        def regroup(turned, rounded, b0):
-            nc.scalar.copy(
-                rounded[:, b0 : b0 + 2]
-                .rearrange("z b u p e -> z (b u p e)")
-                .bitcast(F32)
-                .rearrange("z (b u p) -> z b u p", b=2, u=2),
-                turned[:].rearrange("z b l -> z (b l)").bitcast(F32).rearrange("z (b p u) -> z b u p", b=2, u=2),
-            )
-
-        def add_up(gated, j0, rounded, k):
-            tiles = gated.shape[1]
-            total = bank(k)
-            for j in range(tiles):
-                for r in range(2):
-                    nc.tensor.matmul(
-                        total[:, P * j : P * (j + 1)],
-                        lhsT=gated[:, j, r, :],
-                        rhs=ident[:],
-                        is_transpose=True,
-                        start=(r == 0),
-                        stop=(r == 1),
-                    )
-            nc.scalar.copy(
-                rounded[:, 0, :, 32 * j0 : 32 * (j0 + tiles), :],
-                total[:, : P * tiles].rearrange("z (p u e) -> z u p e", u=2, e=2),
-            )
-
-        def turn_plain(plains, b, k):
-            turned = bank(k)
-            for j in range(LT):
-                nc.tensor.transpose(turned[:, P * j : P * (j + 1)], plains[j][:, P * b : P * (b + 1)], ident[:])
-            return turned
-
         def first_product(turned, block):
-            first = keep.tile([P, 2, P, 2], F32, name=f"first{block}")
-            tile = max(i for i in range(len(gate_first)) if GATE_CUTS[i] <= block)
-            column = block - GATE_CUTS[tile]
+            first = in_slot(f"first{block}", [P, 2, P, 2], F32, f"first{block}")
+            chunk = 0 if block < S_MID // P else 1
+            column = block - chunk * (S_MID // P)
             nc.scalar.activation(
                 first[:],
                 turned[:].rearrange("z (p u e) -> z u p e", u=2, e=2),
                 COPY,
-                scale=gate_first[tile][:, column : column + 1],
+                scale=gate_first[chunk][:, column : column + 1],
             )
             return first
 
@@ -324,110 +302,115 @@ def tile_moe_mhm_none_kernel(
                 merge_half(acc[:, h * width : (h + 1) * width], heads, h, t0, t1)
             return acc
 
-        def store(acc, t0, t1, copy, offset=None):
+        def store(acc, t0, t1, copy, tag):
             width = t1 - t0
-            pool = keep if offset is None else shared
-            staged = pool.tile([P, N // P, width], F32, name=f"staged{t0}", offset=offset)
+            staged = in_slot(tag, [P, N // P, width], F32, f"staged{t0}")
             copy(staged[:].rearrange("p h t -> p (h t)"), acc[:, : (N // P) * width])
             nc.sync.dma_start(out_v[:, :, t0:t1], staged[:])
 
-        rounded_first, rounded_mid = rounded_tile(V_FIRST, V_MID), rounded_tile(V_MID, V_LAST, AT_ROUNDED_MID)
-        rounded_s = rounded_tile(0, S_MID, AT_ROUNDED_S)
+        rounded_s, rounded_first = rounded_tile(0, S_MID), rounded_tile(V_FIRST, V_MID)
+        rounded_mid, rounded_last = rounded_tile(V_MID, V_LAST), rounded_tile(V_LAST, Z)
         rounded_3, rounded_4 = rounded_tile(S_MID, S_MID + P), rounded_tile(S_MID + P, V_FIRST)
         grouped_first, grouped_mid = grouped_tile(V_FIRST, V_MID), grouped_tile(V_MID, V_LAST)
         grouped_last, grouped_s = grouped_tile(V_LAST, Z), grouped_tile(0, S_MID)
         grouped_3, grouped_4 = grouped_tile(S_MID, S_MID + P), grouped_tile(S_MID + P, V_FIRST)
-
         wide, mid, narrow = V_MID - V_FIRST, V_LAST - V_MID, V_FIRST - S_MID
-        fetched = keep.tile([P, 2 * LT, wide], F32, name="fetched")
-        sums = keep.tile([P, LT - 1, wide], BF16, name="sums")
-        plain = keep.tile([P, 2 * LT - 1, S_MID], F32, name="plain")
-        plain_end = shared.tile([P, S_MID], F32, name="plain_end", offset=AT_PLAIN_END)
-        fetch_gated(0, 0, V_FIRST, V_MID, fetched[:, 0])
-        for j in range(LT - 1):
-            fetch_gated(1, j, V_FIRST, V_MID, fetched[:, 2 * j + 1])
-            fetch_gated(0, j + 1, V_FIRST, V_MID, fetched[:, 2 * j + 2])
-            nc.vector.tensor_tensor(sums[:, j], fetched[:, 2 * j], fetched[:, 2 * j + 1], ADD)
-        fetch_gated(1, LT - 1, V_FIRST, V_MID, fetched[:, 2 * LT - 1])
-        plains = [fetch_plain(0, j, 0, S_MID, plain[:, j]) for j in range(LT)]
-        turned_1 = [turn_plain(plains, b, 2 + b) for b in range(3)]
-        plains = [fetch_plain(1, j, 0, S_MID, plain[:, LT + j] if j < LT - 1 else plain_end[:]) for j in range(LT)]
-        firsts = [first_product(turned_1[b], b) for b in range(3)]
-        turned_2 = [turn_plain(plains, b, 5 + b) for b in range(3)]
-        mid_start = keep.tile([P, mid], F32, name="mid_start")
-        fetch_gated(0, 0, V_MID, V_LAST, mid_start[:])
-        sum_end = shared.tile([P, wide], BF16, name="sum_end", offset=AT_SUM_END)
-        nc.gpsimd.tensor_tensor(sum_end[:], fetched[:, 2 * LT - 2], fetched[:, 2 * LT - 1], ADD)
-        first_banks = [bank16(2), bank16(3)]
+
+        fetched = keep.tile([P, LT, 2, wide], F32, name="fetched")
+        plain = [[in_slot(f"plain{r}{j}", [P, S_MID], F32, f"plain{r}{j}") for j in range(LT)] for r in range(2)]
+        turned_1 = [bank(2 + b) for b in range(3)]
+        turned_2 = [bank(5 + b) for b in range(3)]
+
+        def wide_pair(j, k):
+            total = bank(k)
+            for r in range(2):
+                gated_step(r, j, V_FIRST, V_MID, fetched[:, j, r], total, 0, r == 0, r == 1)
+            return total
+
+        def plain_first(r, j):
+            plain_step(r, j, 0, S_MID, plain[r][j][:], turned_2 if r else turned_1)
+
+        total_0 = wide_pair(0, 0)
         for j in range(LT):
-            turn_sums(first_banks, sums[:, j] if j < LT - 1 else sum_end[:], j)
+            plain_first(0, j)
+        total_1 = wide_pair(1, 1)
+        round_sums(total_0, rounded_first, 0, 1)
+        plain_first(1, 0)
+        round_sums(total_1, rounded_first, 1, 1)
+        plain_first(1, 1)
+        plain_first(1, 2)
+        total_2 = wide_pair(2, 0)
+        round_sums(total_2, rounded_first, 2, 1)
+        plain_first(1, 3)
+        total_3 = wide_pair(3, 0)
+        firsts = [first_product(turned_1[b], b) for b in range(3)]
+        round_sums(total_3, rounded_first, 3, 1)
+
+        mid_early = in_slot("plain03", [P, 3, mid], F32, "mid_early")
+        mid_late = in_slot("after_first_products", [P, 6, mid], F32, "mid_late")
+        mid_a, mid_b = bank(2), bank(3)
+        gated_step(0, 0, V_MID, V_LAST, mid_early[:, 0], mid_a, 0, True, False)
+        gated_step(1, 0, V_MID, V_LAST, mid_early[:, 1], mid_a, 0, False, False)
+        gated_step(0, 1, V_MID, V_LAST, mid_early[:, 2], mid_a, P, False, False)
         for b in range(3):
             second_product(turned_2[b], firsts[b], b, rounded_s, b)
 
-        plain_a = keep.tile([P, LT, narrow], F32, name="plain_a")
-        plains = [fetch_plain(0, j, S_MID, V_FIRST, plain_a[:, j]) for j in range(LT)]
-        regroup(first_banks[0], rounded_first, 0)
-        regroup(first_banks[1], rounded_first, 2)
-        turned_1 = [turn_plain(plains, b, b) for b in range(2)]
-        plain_b = keep.tile([P, narrow], F32, name="plain_b")
-        plain_late = shared.tile([P, LT - 1, narrow], F32, name="plain_late", offset=AT_PLAIN_LATE)
-        plains = [fetch_plain(1, 0, S_MID, V_FIRST, plain_b[:]), fetch_plain(1, 1, S_MID, V_FIRST, plain_late[:, 0])]
-        turn_back(grouped_first, rounded_first, 0, 2, 4)
-        turn_back(grouped_first, rounded_first, 2, 4, 7)
-        turn_back(grouped_s, rounded_s, 0, 2, 2)
-        turn_back(grouped_s, rounded_s, 2, 3, 3)
-        plains.extend([fetch_plain(1, j, S_MID, V_FIRST, plain_late[:, j - 1]) for j in range(2, LT)])
-        first_3 = first_product(turned_1[0], 3)
-        turned_2 = [turn_plain(plains, b, 5 + b) for b in range(2)]
-
-        mid_fetched = shared.tile([P, 2 * LT - 1, mid], F32, name="mid_fetched", offset=AT_MID_FETCH)
-        mid_sums = keep.tile([P, LT, mid], BF16, name="mid_sums")
-        mid_banks = [bank16(2)]
-        mid_end = shared.tile([P, mid], F32, name="mid_end", offset=AT_MID_END)
-        for j in range(LT - 1):
-            fetch_gated(1, j, V_MID, V_LAST, mid_fetched[:, 2 * j + 1])
-            fetch_gated(0, j + 1, V_MID, V_LAST, mid_fetched[:, 2 * j + 2])
-            nc.vector.tensor_tensor(
-                mid_sums[:, j], mid_fetched[:, 2 * j] if j else mid_start[:], mid_fetched[:, 2 * j + 1], ADD
-            )
-            turn_sums(mid_banks, mid_sums[:, j], j)
-        fetch_gated(1, LT - 1, V_MID, V_LAST, mid_end[:])
+        late = keep.tile([P, 2 * LT - 1, narrow], F32, name="late")
+        turned_1 = [bank(4), bank(5)]
+        plain_step(0, 0, S_MID, V_FIRST, late[:, 0], turned_1)
+        plain_step(0, 1, S_MID, V_FIRST, late[:, 1], turned_1)
+        turn_back(grouped_first, rounded_first, 0, 2, 0)
+        turn_back(grouped_first, rounded_first, 2, 4, 1)
+        turn_back(grouped_s, rounded_s, 0, 2, 6)
+        turn_back(grouped_s, rounded_s, 2, 3, 7)
+        gated_step(1, 1, V_MID, V_LAST, mid_late[:, 0], mid_a, P, False, True)
+        gated_step(0, 2, V_MID, V_LAST, mid_late[:, 1], mid_b, 0, True, False)
+        gated_step(1, 2, V_MID, V_LAST, mid_late[:, 2], mid_b, 0, False, False)
         codes_first = quantize(grouped_first, V_FIRST)
-        nc.vector.tensor_tensor(mid_sums[:, LT - 1], mid_fetched[:, 2 * LT - 2], mid_end[:], ADD)
-        turn_sums(mid_banks, mid_sums[:, LT - 1], LT - 1)
+        gated_step(0, 3, V_MID, V_LAST, mid_late[:, 3], mid_b, P, False, False)
+        gated_step(1, 3, V_MID, V_LAST, mid_late[:, 4], mid_b, P, False, True)
+        plain_step(0, 2, S_MID, V_FIRST, late[:, 2], turned_1)
+        plain_step(0, 3, S_MID, V_FIRST, mid_late[:, 5], turned_1, on_vector=True)
         codes_s = quantize(grouped_s, 0)
-        regroup(mid_banks[0], rounded_mid, 0)
+        round_sums(mid_a, rounded_mid, 0, 2)
+        turned_2 = [bank(6), bank(7)]
+        plain_step(1, 0, S_MID, V_FIRST, late[:, 3], turned_2)
+        plain_step(1, 1, S_MID, V_FIRST, late[:, 4], turned_2)
+        acc_a = merge((codes_s, codes_first), 0, 2 * P, 0)
+        acc_b = merge((codes_s, codes_first), 2 * P, 3 * P, 1)
+        round_sums(mid_b, rounded_mid, 2, 2)
+        plain_step(1, 2, S_MID, V_FIRST, late[:, 5], turned_2)
+        plain_step(1, 3, S_MID, V_FIRST, late[:, 6], turned_2)
+        first_3 = first_product(turned_1[0], 3)
         first_4 = first_product(turned_1[1], 4)
+        turn_back(grouped_mid, rounded_mid, 0, 2, 2)
 
-        last_early = shared.tile([P, LT - 1, 2, P], F32, name="last_early", offset=AT_LAST_EARLY)
-        for j in range(LT - 1):
+        last = in_slot("rounded0", [P, LT, 2, P], F32, "last")
+        last_a, last_b = bank(3), bank(4)
+        for j in range(LT):
             for r in range(2):
-                fetch_gated(r, j, V_LAST, Z, last_early[:, j, r, :])
+                if j < LT - 1:
+                    gated_step(r, j, V_LAST, Z, last[:, j, r], last_a, P * j, j + r == 0, j + r == LT - 1)
+                else:
+                    gated_step(r, j, V_LAST, Z, last[:, j, r], last_b, 0, r == 0, r == 1)
         second_product(turned_2[0], first_3, 3, rounded_3, 0)
-        last_end = shared.tile([P, 1, 2, P], F32, name="last_end", offset=AT_LAST_END)
-        for r in range(2):
-            fetch_gated(r, LT - 1, V_LAST, Z, last_end[:, 0, r, :])
         second_product(turned_2[1], first_4, 4, rounded_4, 0)
+        round_sums(last_a, rounded_last, 0, LT - 1)
+        round_sums(last_b, rounded_last, LT - 1, 1)
 
-        acc_a = merge((codes_s, codes_first), 0, 2 * P, 4)
-        turn_back(grouped_mid, rounded_mid, 0, 2, 3)
-        rounded_last = rounded_tile(V_LAST, Z, AT_ROUNDED_MID)
-        add_up(last_early, 0, rounded_last, 2)
         turn_back(grouped_3, rounded_3, 0, 1, 5)
-        add_up(last_end, LT - 1, rounded_last, 1)
         turn_back(grouped_4, rounded_4, 0, 1, 6)
-        acc_b = merge((codes_s, codes_first), 2 * P, 3 * P, 2)
-        turn_back(grouped_last, rounded_last, 0, 1, 0)
+        turn_back(grouped_last, rounded_last, 0, 1, 3)
         codes_mid = quantize(grouped_mid, V_MID)
+        store(acc_a, 0, 2 * P, nc.vector.tensor_copy, "first3")
         codes_3 = quantize(grouped_3, S_MID)
-        store(acc_a, 0, 2 * P, nc.vector.tensor_copy, AT_STAGED)
         codes_4 = quantize(grouped_4, S_MID + P)
-        store(acc_b, 2 * P, 3 * P, nc.vector.tensor_copy)
         codes_last = quantize(grouped_last, V_LAST)
-        store(merge((codes_3, codes_mid), 3 * P, 4 * P, 5), 3 * P, 4 * P, nc.vector.tensor_copy)
-        store(merge((codes_4, codes_mid), 4 * P, 5 * P, 6), 4 * P, 5 * P, nc.scalar.copy)
+        store(acc_b, 2 * P, 3 * P, nc.scalar.copy, "staged2")
+        store(merge((codes_3, codes_mid), 3 * P, 4 * P, 5), 3 * P, 4 * P, nc.vector.tensor_copy, "staged3")
+        store(merge((codes_4, codes_mid), 4 * P, 5 * P, 6), 4 * P, 5 * P, nc.scalar.copy, "staged4")
         staged_last = keep.tile([P, N // P, P], F32, name="staged_last")
-        halves = [bank(0), bank(7)]
+        halves = [bank(4), bank(7)]
         for h in range(N // P):
             merge_half(halves[h][:, :P], (codes_first, codes_last), h, 5 * P, T)
         nc.vector.tensor_copy(staged_last[:, 0], halves[0][:, :P])

@@ -32,6 +32,7 @@ XW_FIRST = 5
 XS_FIRST = 3
 S_MID, V_FIRST, V_MID, V_LAST = 384, 640, 1152, 1408
 S_BLOCKS = V_FIRST // P
+RING = 5
 
 AT_XS_REST, AT_W_FIRST, AT_XW_REST = 0, 2048, 2304
 
@@ -163,12 +164,14 @@ def tile_moe_mhm_none_kernel(
                 expert(acc[:, (e - e0) * C : (e - e0 + 1) * C], j, e)
             copy(y[j][:, e0 * C : e1 * C], acc[:, : (e1 - e0) * C])
 
-        def last_expert(j0, copy):
+        def last_expert(j0):
             acc = next_bank()
             for i in range(2):
                 expert(acc[:, i * C : (i + 1) * C], j0 + i, E - 1)
-            for i in range(2):
-                copy(y[j0 + i][:, (E - 1) * C :], acc[:, i * C : (i + 1) * C])
+            return acc
+
+        def empty_last(acc, j, copy):
+            copy(y[j][:, (E - 1) * C :], acc[:, j % 2 * C : (j % 2 + 1) * C])
 
         gather_slots(xs_slots, xs, 0, XS_FIRST)
         gather_slots(xw_slots, xw, 0, 1)
@@ -186,8 +189,11 @@ def tile_moe_mhm_none_kernel(
                     gather_slots(xs_slots, xs, E - 1, E)
                     gather_slots(xw_slots, xw, E - 1, E)
                 experts(j, e, e + 2, nc.vector.tensor_copy if last else nc.scalar.copy)
-        last_expert(0, nc.vector.tensor_copy)
-        last_expert(2, nc.scalar.copy)
+        last_01 = last_expert(0)
+        empty_last(last_01, 0, nc.vector.tensor_copy)
+        empty_last(last_01, 1, nc.vector.tensor_copy)
+        last_23 = last_expert(2)
+        empty_last(last_23, 2, nc.scalar.copy)
 
         out_v = out.rearrange("(h p) t -> p h t", p=P)
 
@@ -210,10 +216,6 @@ def tile_moe_mhm_none_kernel(
                     stop=(last and b == blocks - 1),
                 )
 
-        def gated_step(r, j, z0, z1, dst, total, at, first, last):
-            fetch_gated(r, j, z0, z1, dst)
-            add_turned(total, at, dst, first, last)
-
         def round_sums(total, rounded, j0, tiles):
             blocks = rounded.shape[1]
             nc.scalar.copy(
@@ -223,13 +225,12 @@ def tile_moe_mhm_none_kernel(
                 .rearrange("z b (p u e) -> z b u p e", u=2, e=2),
             )
 
-        def plain_step(r, j, z0, z1, dst, turned, on_vector=False):
-            if on_vector:
-                nc.vector.tensor_copy(dst, looked_up(r, j, z0, z1))
-            else:
-                nc.scalar.activation(dst, looked_up(r, j, z0, z1), COPY)
+        def fetch_plain(r, j, z0, z1, dst):
+            nc.scalar.activation(dst, looked_up(r, j, z0, z1), COPY)
+
+        def turn_plain(turned, j, fetched):
             for b in range(len(turned)):
-                nc.tensor.transpose(turned[b][:, P * j : P * (j + 1)], dst[:, P * b : P * (b + 1)], ident[:])
+                nc.tensor.transpose(turned[b][:, P * j : P * (j + 1)], fetched[:, P * b : P * (b + 1)], ident[:])
 
         def rounded_tile(z0, z1):
             return in_slot(f"rounded{z0}", [P, (z1 - z0) // P, 2, P, 2], BF16, f"rounded{z0}")
@@ -237,12 +238,14 @@ def tile_moe_mhm_none_kernel(
         def grouped_tile(z0, z1):
             return keep.tile([P, z1 - z0, 4], BF16, name=f"grouped{z0}", align_bytes=64)
 
-        def first_product(turned, block):
-            first = in_slot(f"first{block}", [P, 2, P, 2], F32, f"first{block}")
+        def first_tile(block):
+            return in_slot(f"first{block}", [P, 2, P, 2], F32, f"first{block}")
+
+        def first_product(turned, block, first):
             chunk = 0 if block < S_MID // P else 1
             column = block - chunk * (S_MID // P)
             nc.scalar.activation(
-                first[:],
+                first,
                 turned[:].rearrange("z (p u e) -> z u p e", u=2, e=2),
                 COPY,
                 scale=gate_first[chunk][:, column : column + 1],
@@ -260,13 +263,16 @@ def tile_moe_mhm_none_kernel(
                     ADD,
                 )
 
-        def turn_back(grouped, rounded, b0, b1, k):
+        def turn_back(rounded, b0, b1, k):
             back = bank(k)
             for b in range(b0, b1):
                 pairs = rounded[:, b].rearrange("z u p e -> z (u p e)").bitcast(F32)
                 for u in range(2):
                     at = P * (2 * (b - b0) + u)
                     nc.tensor.transpose(back[:, at : at + P], pairs[:, P * u : P * (u + 1)], ident[:])
+            return back
+
+        def group(grouped, b0, b1, back):
             words = grouped[:, P * b0 : P * b1, :].rearrange("p z t -> p (z t)").bitcast(F32)
             nc.scalar.copy(
                 words.rearrange("p (b z u) -> p b z u", z=P, u=2),
@@ -282,25 +288,25 @@ def tile_moe_mhm_none_kernel(
             )
             return codes, scales, z0
 
-        def merge_half(acc, heads, h, t0, t1):
-            for o, (codes, scales, z0) in enumerate(heads):
-                cols = slice(o * T + t0 - z0, o * T + t1 - z0)
-                nc.tensor.matmul_mx(
-                    out=acc,
-                    lhsT=wmw[:, o, 2 * P * h : 2 * P * (h + 1)].bitcast(FP4X4),
-                    lhsT_scale=wms[:, o, P * h : P * (h + 1)],
-                    rhs=codes[:, cols].bitcast(FP8X4),
-                    rhs_scale=scales[:, cols],
-                    start=(o == 0),
-                    stop=(o == D - 1),
-                )
+        def merge_pass(acc, quantized, h, t0, t1, start, stop):
+            codes, scales, z0 = quantized
+            o = 0 if z0 <= t0 < z0 + codes.shape[1] else 1
+            cols = slice(o * T + t0 - z0, o * T + t1 - z0)
+            nc.tensor.matmul_mx(
+                out=acc,
+                lhsT=wmw[:, o, 2 * P * h : 2 * P * (h + 1)].bitcast(FP4X4),
+                lhsT_scale=wms[:, o, P * h : P * (h + 1)],
+                rhs=codes[:, cols].bitcast(FP8X4),
+                rhs_scale=scales[:, cols],
+                start=start,
+                stop=stop,
+            )
 
-        def merge(heads, t0, t1, k):
+        def merge_head(acc, quantized, t0, t1, first):
             width = t1 - t0
-            acc = bank(k)
             for h in range(N // P):
-                merge_half(acc[:, h * width : (h + 1) * width], heads, h, t0, t1)
-            return acc
+                start, stop = first and h == 0, not first and h == N // P - 1
+                merge_pass(acc[:, h * width : (h + 1) * width], quantized, h, t0, t1, start, stop)
 
         def store(acc, t0, t1, copy, tag):
             width = t1 - t0
@@ -316,103 +322,127 @@ def tile_moe_mhm_none_kernel(
         grouped_3, grouped_4 = grouped_tile(S_MID, S_MID + P), grouped_tile(S_MID + P, V_FIRST)
         wide, mid, narrow = V_MID - V_FIRST, V_LAST - V_MID, V_FIRST - S_MID
 
-        fetched = keep.tile([P, LT, 2, wide], F32, name="fetched")
-        plain = [[in_slot(f"plain{r}{j}", [P, S_MID], F32, f"plain{r}{j}") for j in range(LT)] for r in range(2)]
         turned_1 = [bank(2 + b) for b in range(3)]
         turned_2 = [bank(5 + b) for b in range(3)]
+        totals = []
+        for i in range(2 * LT):
+            plain = in_slot(f"ring{2 * i % RING}", [P, S_MID], F32, f"plain{i}")
+            fetch_plain(i // LT, i % LT, 0, S_MID, plain[:])
+            turn_plain(turned_1 if i < LT else turned_2, i % LT, plain)
+            if i == 0:
+                empty_last(last_23, LT - 1, nc.scalar.copy)
+            if i % 2 == 0:
+                if i >= LT:
+                    round_sums(totals[-2], rounded_first, i // 2 - 2, 1)
+                totals.append(bank(1 - i // 2 % 2))
+            gated = in_slot(f"ring{(2 * i + 1) % RING}", [P, wide], F32, f"gated{i}")
+            fetch_gated(i % 2, i // 2, V_FIRST, V_MID, gated[:])
+            add_turned(totals[-1], 0, gated, i % 2 == 0, i % 2 == 1)
+        round_sums(totals[-2], rounded_first, LT - 2, 1)
+        firsts = [first_product(turned_1[b], b, first_tile(b)[:]) for b in range(3)]
+        round_sums(totals[-1], rounded_first, LT - 1, 1)
 
-        def wide_pair(j, k):
-            total = bank(k)
-            for r in range(2):
-                gated_step(r, j, V_FIRST, V_MID, fetched[:, j, r], total, 0, r == 0, r == 1)
-            return total
+        def fetch_mid(i, dst):
+            fetch_gated(i % 2, i // 2, V_MID, V_LAST, dst)
+            return dst
 
-        def plain_first(r, j):
-            plain_step(r, j, 0, S_MID, plain[r][j][:], turned_2 if r else turned_1)
+        def add_mid(i, total, fetched):
+            add_turned(total, P * (i // 2 % 2), fetched, i % 4 == 0, i % 4 == 3)
 
-        total_0 = wide_pair(0, 0)
-        for j in range(LT):
-            plain_first(0, j)
-        total_1 = wide_pair(1, 1)
-        round_sums(total_0, rounded_first, 0, 1)
-        plain_first(1, 0)
-        round_sums(total_1, rounded_first, 1, 1)
-        plain_first(1, 1)
-        plain_first(1, 2)
-        total_2 = wide_pair(2, 0)
-        round_sums(total_2, rounded_first, 2, 1)
-        plain_first(1, 3)
-        total_3 = wide_pair(3, 0)
-        firsts = [first_product(turned_1[b], b) for b in range(3)]
-        round_sums(total_3, rounded_first, 3, 1)
+        def fetch_late(i, dst):
+            fetch_plain(i // LT, i % LT, S_MID, V_FIRST, dst)
+            return dst
 
-        mid_early = in_slot("plain03", [P, 3, mid], F32, "mid_early")
-        mid_late = in_slot("after_first_products", [P, 6, mid], F32, "mid_late")
-        mid_a, mid_b = bank(2), bank(3)
-        gated_step(0, 0, V_MID, V_LAST, mid_early[:, 0], mid_a, 0, True, False)
-        gated_step(1, 0, V_MID, V_LAST, mid_early[:, 1], mid_a, 0, False, False)
-        gated_step(0, 1, V_MID, V_LAST, mid_early[:, 2], mid_a, P, False, False)
+        mid_01 = in_slot(f"ring{(4 * LT - 4) % RING}", [P, 2, mid], F32, "mid_01")
+        late_01 = in_slot(f"ring{(4 * LT - 1) % RING}", [P, 2, narrow], F32, "late_01")
+        mid_23 = in_slot("after_first_products", [P, 2, mid], F32, "mid_23")
+        mid_a = bank(2)
+        for i in range(2):
+            add_mid(i, mid_a, fetch_mid(i, mid_01[:, i]))
         for b in range(3):
             second_product(turned_2[b], firsts[b], b, rounded_s, b)
-
-        late = keep.tile([P, 2 * LT - 1, narrow], F32, name="late")
-        turned_1 = [bank(4), bank(5)]
-        plain_step(0, 0, S_MID, V_FIRST, late[:, 0], turned_1)
-        plain_step(0, 1, S_MID, V_FIRST, late[:, 1], turned_1)
-        turn_back(grouped_first, rounded_first, 0, 2, 0)
-        turn_back(grouped_first, rounded_first, 2, 4, 1)
-        turn_back(grouped_s, rounded_s, 0, 2, 6)
-        turn_back(grouped_s, rounded_s, 2, 3, 7)
-        gated_step(1, 1, V_MID, V_LAST, mid_late[:, 0], mid_a, P, False, True)
-        gated_step(0, 2, V_MID, V_LAST, mid_late[:, 1], mid_b, 0, True, False)
-        gated_step(1, 2, V_MID, V_LAST, mid_late[:, 2], mid_b, 0, False, False)
-        codes_first = quantize(grouped_first, V_FIRST)
-        gated_step(0, 3, V_MID, V_LAST, mid_late[:, 3], mid_b, P, False, False)
-        gated_step(1, 3, V_MID, V_LAST, mid_late[:, 4], mid_b, P, False, True)
-        plain_step(0, 2, S_MID, V_FIRST, late[:, 2], turned_1)
-        plain_step(0, 3, S_MID, V_FIRST, mid_late[:, 5], turned_1, on_vector=True)
-        codes_s = quantize(grouped_s, 0)
+        late = [fetch_late(i, late_01[:, i]) for i in range(2)]
+        group(grouped_first, 0, 2, turn_back(rounded_first, 0, 2, 1))
+        group(grouped_first, 2, 4, turn_back(rounded_first, 2, 4, 5))
+        late.append(fetch_late(2, in_slot(f"rounded{V_FIRST}", [P, narrow], F32, "late_2")[:]))
+        group(grouped_s, 0, 2, turn_back(rounded_s, 0, 2, 0))
+        group(grouped_s, 2, 3, turn_back(rounded_s, 2, 3, 7))
+        for i in range(2, 4):
+            add_mid(i, mid_a, fetch_mid(i, mid_23[:, i - 2]))
         round_sums(mid_a, rounded_mid, 0, 2)
-        turned_2 = [bank(6), bank(7)]
-        plain_step(1, 0, S_MID, V_FIRST, late[:, 3], turned_2)
-        plain_step(1, 1, S_MID, V_FIRST, late[:, 4], turned_2)
-        acc_a = merge((codes_s, codes_first), 0, 2 * P, 0)
-        acc_b = merge((codes_s, codes_first), 2 * P, 3 * P, 1)
+        mid_4 = in_slot("first1", [P, mid], F32, "mid_4")
+        mid_5 = in_slot("first2", [P, mid], F32, "mid_5")
+        mid_b = bank(5)
+        add_mid(4, mid_b, fetch_mid(4, mid_4[:]))
+        add_mid(5, mid_b, fetch_mid(5, mid_5[:]))
+        turned_1 = [bank(0), bank(7)]
+        for j in range(LT - 1):
+            turn_plain(turned_1, j, late[j])
+        codes_first = quantize(grouped_first, V_FIRST)
+        mid_67 = in_slot("first1", [P, 3, mid], F32, "mid_67")
+        last = in_slot("first2", [P, 2 * LT * P], F32, "last")
+        late_456 = in_slot("after_first_products", [P, 3, narrow], F32, "late_456")
+        late_end = in_slot("first1", [P, narrow + H], F32, "late_end")
+        turned_2 = [bank(3), bank(4)]
+        nc.vector.tensor_copy(mid_67[:, 2], looked_up(0, LT - 1, S_MID, V_FIRST))
+        turn_plain(turned_1, LT - 1, mid_67[:, 2])
+        for i in range(6, 8):
+            add_mid(i, mid_b, fetch_mid(i, mid_67[:, i - 6]))
+        codes_s = quantize(grouped_s, 0)
+        for j in range(LT - 1):
+            fetch_late(LT + j, late_456[:, j])
+        acc_a = bank(1)
+        merge_head(acc_a, codes_s, 0, 2 * P, True)
+        merge_head(acc_a, codes_first, 0, 2 * P, False)
+        for j in range(2):
+            turn_plain(turned_2, j, late_456[:, j])
+        turn_plain(turned_2, 2, late_456[:, 2])
+        first_3 = first_product(turned_1[0], 3, first_tile(3)[:])
         round_sums(mid_b, rounded_mid, 2, 2)
-        plain_step(1, 2, S_MID, V_FIRST, late[:, 5], turned_2)
-        plain_step(1, 3, S_MID, V_FIRST, late[:, 6], turned_2)
-        first_3 = first_product(turned_1[0], 3)
-        first_4 = first_product(turned_1[1], 4)
-        turn_back(grouped_mid, rounded_mid, 0, 2, 2)
+        turn_plain(turned_2, 3, fetch_late(LT + 3, late_end[:, :narrow]))
+        back_mid = turn_back(rounded_mid, 0, 2, 2)
+        first_4 = first_product(turned_1[1], 4, late_end[:, narrow:].rearrange("z (u p e) -> z u p e", u=2, e=2))
+        group(grouped_mid, 0, 2, back_mid)
 
-        last = in_slot("rounded0", [P, LT, 2, P], F32, "last")
-        last_a, last_b = bank(3), bank(4)
+        last_a, last_b = bank(5), bank(7)
         for j in range(LT):
             for r in range(2):
+                fetched = last[:, P * (2 * j + r) : P * (2 * j + r + 1)]
+                fetch_gated(r, j, V_LAST, Z, fetched)
                 if j < LT - 1:
-                    gated_step(r, j, V_LAST, Z, last[:, j, r], last_a, P * j, j + r == 0, j + r == LT - 1)
+                    add_turned(last_a, P * j, fetched, j + r == 0, j + r == LT - 1)
                 else:
-                    gated_step(r, j, V_LAST, Z, last[:, j, r], last_b, 0, r == 0, r == 1)
+                    add_turned(last_b, 0, fetched, r == 0, r == 1)
         second_product(turned_2[0], first_3, 3, rounded_3, 0)
         second_product(turned_2[1], first_4, 4, rounded_4, 0)
         round_sums(last_a, rounded_last, 0, LT - 1)
         round_sums(last_b, rounded_last, LT - 1, 1)
 
-        turn_back(grouped_3, rounded_3, 0, 1, 5)
-        turn_back(grouped_4, rounded_4, 0, 1, 6)
-        turn_back(grouped_last, rounded_last, 0, 1, 3)
+        group(grouped_3, 0, 1, turn_back(rounded_3, 0, 1, 0))
+        acc_b = bank(3)
+        merge_head(acc_b, codes_s, 2 * P, 3 * P, True)
+        merge_head(acc_b, codes_first, 2 * P, 3 * P, False)
+        group(grouped_4, 0, 1, turn_back(rounded_4, 0, 1, 6))
+        group(grouped_last, 0, 1, turn_back(rounded_last, 0, 1, 5))
         codes_mid = quantize(grouped_mid, V_MID)
+        halves = [bank(7), bank(4)]
+        for h in range(N // P):
+            merge_pass(halves[h][:, :P], codes_first, h, 5 * P, T, True, False)
+        acc_3, acc_4 = bank(2), bank(0)
+        merge_head(acc_3, codes_mid, 3 * P, 4 * P, True)
+        merge_head(acc_4, codes_mid, 4 * P, 5 * P, True)
         store(acc_a, 0, 2 * P, nc.vector.tensor_copy, "first3")
         codes_3 = quantize(grouped_3, S_MID)
         codes_4 = quantize(grouped_4, S_MID + P)
         codes_last = quantize(grouped_last, V_LAST)
-        store(acc_b, 2 * P, 3 * P, nc.scalar.copy, "staged2")
-        store(merge((codes_3, codes_mid), 3 * P, 4 * P, 5), 3 * P, 4 * P, nc.vector.tensor_copy, "staged3")
-        store(merge((codes_4, codes_mid), 4 * P, 5 * P, 6), 4 * P, 5 * P, nc.scalar.copy, "staged4")
-        staged_last = keep.tile([P, N // P, P], F32, name="staged_last")
-        halves = [bank(4), bank(7)]
+        store(acc_b, 2 * P, 3 * P, nc.scalar.copy, f"rounded{V_LAST}")
+        merge_head(acc_3, codes_3, 3 * P, 4 * P, False)
+        merge_head(acc_4, codes_4, 4 * P, 5 * P, False)
         for h in range(N // P):
-            merge_half(halves[h][:, :P], (codes_first, codes_last), h, 5 * P, T)
+            merge_pass(halves[h][:, :P], codes_last, h, 5 * P, T, False, True)
+        store(acc_3, 3 * P, 4 * P, nc.vector.tensor_copy, "staged3")
+        store(acc_4, 4 * P, 5 * P, nc.scalar.copy, "staged4")
+        staged_last = keep.tile([P, N // P, P], F32, name="staged_last")
         nc.vector.tensor_copy(staged_last[:, 0], halves[0][:, :P])
         nc.scalar.copy(staged_last[:, 1], halves[1][:, :P])
         nc.sync.dma_start(out_v[:, :, 5 * P : T], staged_last[:])

@@ -27,14 +27,14 @@ BANKS = 8
 PER_COL = 16
 
 W_CUTS = (0, 1, 3, 7, 12)
-WS_CUTS = (0, 5, 12)
-XW_FIRST = 5
+WS_CUTS = (0, 3, 7, 12)
+XW_FIRST = 4
 XS_FIRST = 3
 S_MID, V_FIRST, V_MID, V_LAST = 384, 640, 1152, 1408
 S_BLOCKS = V_FIRST // P
 RING = 5
 
-AT_XS_REST, AT_W_FIRST, AT_XW_REST = 0, 2048, 2304
+AT_XS_REST, AT_W_HEAD, AT_XW_REST = 0, 2176, 2304
 
 
 def tile_moe_mhm_none_kernel(
@@ -55,10 +55,8 @@ def tile_moe_mhm_none_kernel(
         xw = keep.tile([P, Z], U32, name="xw")
         xs = keep.tile([P, Z], U8, name="xs", align_bytes=64)
         ws = [keep.tile([P, b - a, H], U8, name=f"ws{a}", align_bytes=64) for a, b in zip(WS_CUTS, WS_CUTS[1:])]
-        ww = [head.tile([P, W_CUTS[1], 2 * H], U8, name="ww0", offset=AT_W_FIRST, align_bytes=64)]
-        ww.extend(
-            [keep.tile([P, b - a, 2 * H], U8, name=f"ww{a}", align_bytes=64) for a, b in zip(W_CUTS[1:], W_CUTS[2:])]
-        )
+        ww = [keep.tile([P, b - a, 2 * H], U8, name=f"ww{a}", align_bytes=64) for a, b in zip(W_CUTS, W_CUTS[1:])]
+        w_head = head.tile([P, 2 * P], U8, name="w_head", offset=AT_W_HEAD, align_bytes=64)
         wmw = keep.tile([P, D, 2 * N], U8, name="wmw", align_bytes=64)
         wms = keep.tile([P, D, N], U8, name="wms", align_bytes=64)
         ident = keep.tile([P, P], F32, name="ident")
@@ -94,21 +92,21 @@ def tile_moe_mhm_none_kernel(
         nc.vector.memset(ws[0][:].rearrange("p e l -> p (e l)").bitcast(I32), 0)
         nc.vector.memset(ident[:], 0.0)
         nc.vector.memset(ws[1][:].rearrange("p e l -> p (e l)").bitcast(I32), 0)
+        nc.vector.memset(ws[2][:].rearrange("p e l -> p (e l)").bitcast(I32), 0)
         nc.vector.memset(wms[:].rearrange("p o n -> p (o n)").bitcast(I32), 0)
         make_identity(nc, ident[:], nomemset=True)
 
         nc.sync.dma_start(offs_sb[:], offs)
-        load_words(0)
+        nc.sync.dma_start(w_head[:].bitcast(I32), w_words[0, 0, :, : 2 * P].bitcast(I32))
         load_scale_rows(xs[:].rearrange("p (o t) -> p o t", o=D), x_scales)
         nc.sync.dma_start(
             xw[:].bitcast(I32).rearrange("p (o t) -> p o t", o=D),
             x_words.rearrange("o p t d -> p o (t d)").bitcast(I32),
         )
-        load_words(1)
-        load_scale_rows(ws[0][:], w_scales[WS_CUTS[0] : WS_CUTS[1], 0])
-        load_words(2)
-        load_scale_rows(ws[1][:], w_scales[WS_CUTS[1] : WS_CUTS[2], 0])
-        load_words(3)
+        nc.sync.dma_start(ww[0][:, 0, 2 * P :].bitcast(I32), w_words[0, 0, :, 2 * P :].bitcast(I32))
+        for i in range(len(ws)):
+            load_scale_rows(ws[i][:], w_scales[WS_CUTS[i] : WS_CUTS[i + 1], 0])
+            load_words(i + 1)
         nc.sync.dma_start(pos_sb[0][:], pos1)
         nc.sync.dma_start(pos_sb[1][:], pos2)
         nc.sync.dma_start(gate_wide[:], gate[:, :, V_FIRST:].rearrange("r p z -> p r z"))
@@ -148,9 +146,10 @@ def tile_moe_mhm_none_kernel(
             nc.vector.tensor_copy(slots(dst, e0, e1), window[:].indirect(offs_sb[:, cols]))
 
         def expert(acc, j, e):
+            words = w_head[:] if e == 0 and j == 0 else part(ww, W_CUTS, e)[:, 2 * P * j : 2 * P * (j + 1)]
             nc.tensor.matmul_mx(
                 out=acc,
-                lhsT=part(ww, W_CUTS, e)[:, 2 * P * j : 2 * P * (j + 1)].bitcast(FP4X4),
+                lhsT=words.bitcast(FP4X4),
                 lhsT_scale=part(ws, WS_CUTS, e)[:, P * j : P * (j + 1)],
                 rhs=slots(xw_slots, e, e + 1).bitcast(FP8X4),
                 rhs_scale=slots(xs_slots, e, e + 1),
@@ -158,42 +157,44 @@ def tile_moe_mhm_none_kernel(
                 stop=True,
             )
 
-        def experts(j, e0, e1, copy=nc.scalar.copy):
-            acc = next_bank()
-            for e in range(e0, e1):
-                expert(acc[:, (e - e0) * C : (e - e0 + 1) * C], j, e)
-            copy(y[j][:, e0 * C : e1 * C], acc[:, : (e1 - e0) * C])
-
-        def last_expert(j0):
+        def two_tiles(e, j0):
             acc = next_bank()
             for i in range(2):
-                expert(acc[:, i * C : (i + 1) * C], j0 + i, E - 1)
+                expert(acc[:, i * C : (i + 1) * C], j0 + i, e)
             return acc
 
-        def empty_last(acc, j, copy):
-            copy(y[j][:, (E - 1) * C :], acc[:, j % 2 * C : (j % 2 + 1) * C])
+        def empty(acc, e, j, copy):
+            copy(y[j][:, e * C : (e + 1) * C], acc[:, j % 2 * C : (j % 2 + 1) * C])
+
+        def half_expert(e, j0, copy=nc.scalar.copy):
+            acc = two_tiles(e, j0)
+            for j in range(j0, j0 + 2):
+                empty(acc, e, j, copy)
+
+        def expert_tiles(e):
+            half_expert(e, 0)
+            half_expert(e, 2)
 
         gather_slots(xs_slots, xs, 0, XS_FIRST)
         gather_slots(xw_slots, xw, 0, 1)
         for j in range(LT):
-            experts(j, 0, 1)
-        gather_slots(xw_slots, xw, 1, 3)
-        for j in range(LT):
-            experts(j, 1, 3)
-        for e in range(3, E - 1, 2):
-            gather_slots(xw_slots, xw, e, e + 2)
-            gather_slots(xs_slots, xs, e, e + 2)
-            for j in range(LT):
-                last = e == E - 3 and j == LT - 1
-                if last:
-                    gather_slots(xs_slots, xs, E - 1, E)
-                    gather_slots(xw_slots, xw, E - 1, E)
-                experts(j, e, e + 2, nc.vector.tensor_copy if last else nc.scalar.copy)
-        last_01 = last_expert(0)
-        empty_last(last_01, 0, nc.vector.tensor_copy)
-        empty_last(last_01, 1, nc.vector.tensor_copy)
-        last_23 = last_expert(2)
-        empty_last(last_23, 2, nc.scalar.copy)
+            acc = next_bank()[:, :C]
+            expert(acc, j, 0)
+            nc.scalar.copy(y[j][:, :C], acc)
+        gather_slots(xw_slots, xw, 1, 2)
+        expert_tiles(1)
+        for e in range(2, E - 3):
+            gather_slots(*((xw_slots, xw) if e % 2 == 0 else (xs_slots, xs)), e, e + 2)
+            expert_tiles(e)
+        gather_slots(xs_slots, xs, E - 3, E - 1)
+        gather_slots(xw_slots, xw, E - 2, E)
+        gather_slots(xs_slots, xs, E - 1, E)
+        half_expert(E - 3, 0)
+        half_expert(E - 3, 2, nc.vector.tensor_copy)
+        expert_tiles(E - 2)
+        half_expert(E - 1, 0, nc.vector.tensor_copy)
+        last_23 = two_tiles(E - 1, 2)
+        empty(last_23, E - 1, 2, nc.scalar.copy)
 
         out_v = out.rearrange("(h p) t -> p h t", p=P)
 
@@ -330,7 +331,7 @@ def tile_moe_mhm_none_kernel(
             fetch_plain(i // LT, i % LT, 0, S_MID, plain[:])
             turn_plain(turned_1 if i < LT else turned_2, i % LT, plain)
             if i == 0:
-                empty_last(last_23, LT - 1, nc.scalar.copy)
+                empty(last_23, E - 1, LT - 1, nc.scalar.copy)
             if i % 2 == 0:
                 if i >= LT:
                     round_sums(totals[-2], rounded_first, i // 2 - 2, 1)

@@ -26,13 +26,21 @@ BANK = 512
 BANKS = 8
 PER_COL = 16
 
-W_CUTS = (0, 1, 3, 7, 12)
-WS_CUTS = (0, 3, 7, 12)
+W_CUTS = (0, 1, 3, 6, 12)
+WS_CUTS = (0, 3, 6, 12)
 XW_FIRST = 4
 XS_FIRST = 3
 S_MID, V_FIRST, V_MID, V_LAST = 384, 640, 1152, 1408
 S_BLOCKS = V_FIRST // P
 RING = 5
+SLOT = 5120
+AT_RING = 1024
+AT_MID_01, AT_FIRST_2 = AT_RING + SLOT - 1024, AT_RING + SLOT + 1024
+AT_MID_5 = AT_FIRST_2 + 1024
+AT_LAST = AT_RING + 1024
+AT_FIRST_0, AT_FIRST_1 = AT_RING + 2 * SLOT - 1280, AT_RING + 2 * SLOT + 768
+AT_MID_4 = AT_FIRST_1 + 1024
+AT_MID_67 = AT_RING - 1024
 
 AT_XS_REST, AT_W_HEAD, AT_XW_REST = 0, 2176, 2304
 
@@ -45,10 +53,17 @@ def tile_moe_mhm_none_kernel(
         keep = ctx.enter_context(tc.tile_pool(name="keep", bufs=1))
         head = ctx.enter_context(tc.tile_pool(name="head", bufs=1))
         slot = ctx.enter_context(tc.tile_pool(name="slot", bufs=1))
+        ring = ctx.enter_context(tc.tile_pool(name="ring", bufs=1))
         psum = ctx.enter_context(tc.psum_pool(name="psum", bufs=1))
 
         def in_slot(tag, shape, dtype, name):
             return slot.tile(shape, dtype, name=name, tag=tag, align_bytes=64)
+
+        def at(offset, shape, name):
+            return ring.tile(shape, F32, name=name, offset=offset)
+
+        def in_ring(n, shape, name):
+            return at(AT_RING + n % RING * SLOT, shape, name)
 
         offs_sb = keep.tile([P, S // PER_COL], U16, name="offs_sb")
         pos_sb = [keep.tile([P, Z // PER_COL], U16, name=f"pos_sb{r}") for r in range(2)]
@@ -103,9 +118,10 @@ def tile_moe_mhm_none_kernel(
             xw[:].bitcast(I32).rearrange("p (o t) -> p o t", o=D),
             x_words.rearrange("o p t d -> p o (t d)").bitcast(I32),
         )
-        nc.sync.dma_start(ww[0][:, 0, 2 * P :].bitcast(I32), w_words[0, 0, :, 2 * P :].bitcast(I32))
         for i in range(len(ws)):
             load_scale_rows(ws[i][:], w_scales[WS_CUTS[i] : WS_CUTS[i + 1], 0])
+            if i == 0:
+                nc.sync.dma_start(ww[0][:, 0, 2 * P :].bitcast(I32), w_words[0, 0, :, 2 * P :].bitcast(I32))
             load_words(i + 1)
         nc.sync.dma_start(pos_sb[0][:], pos1)
         nc.sync.dma_start(pos_sb[1][:], pos2)
@@ -204,12 +220,12 @@ def tile_moe_mhm_none_kernel(
         def fetch_gated(r, j, z0, z1, dst):
             nc.vector.tensor_tensor(dst, looked_up(r, j, z0, z1), gate_wide[:, r, z0 - V_FIRST : z1 - V_FIRST], MULT)
 
-        def add_turned(total, at, fetched, first, last):
+        def add_turned(total, col, fetched, first, last):
             blocks = fetched.shape[1] // P
             step = BANK // blocks
             for b in range(blocks):
                 nc.tensor.matmul(
-                    total[:, at + step * b : at + step * b + P],
+                    total[:, col + step * b : col + step * b + P],
                     lhsT=fetched[:, P * b : P * (b + 1)],
                     rhs=ident[:],
                     is_transpose=True,
@@ -269,8 +285,8 @@ def tile_moe_mhm_none_kernel(
             for b in range(b0, b1):
                 pairs = rounded[:, b].rearrange("z u p e -> z (u p e)").bitcast(F32)
                 for u in range(2):
-                    at = P * (2 * (b - b0) + u)
-                    nc.tensor.transpose(back[:, at : at + P], pairs[:, P * u : P * (u + 1)], ident[:])
+                    col = P * (2 * (b - b0) + u)
+                    nc.tensor.transpose(back[:, col : col + P], pairs[:, P * u : P * (u + 1)], ident[:])
             return back
 
         def group(grouped, b0, b1, back):
@@ -327,7 +343,7 @@ def tile_moe_mhm_none_kernel(
         turned_2 = [bank(5 + b) for b in range(3)]
         totals = []
         for i in range(2 * LT):
-            plain = in_slot(f"ring{2 * i % RING}", [P, S_MID], F32, f"plain{i}")
+            plain = in_ring(2 * i, [P, S_MID], f"plain{i}")
             fetch_plain(i // LT, i % LT, 0, S_MID, plain[:])
             turn_plain(turned_1 if i < LT else turned_2, i % LT, plain)
             if i == 0:
@@ -336,11 +352,14 @@ def tile_moe_mhm_none_kernel(
                 if i >= LT:
                     round_sums(totals[-2], rounded_first, i // 2 - 2, 1)
                 totals.append(bank(1 - i // 2 % 2))
-            gated = in_slot(f"ring{(2 * i + 1) % RING}", [P, wide], F32, f"gated{i}")
+            gated = in_ring(2 * i + 1, [P, wide], f"gated{i}")
             fetch_gated(i % 2, i // 2, V_FIRST, V_MID, gated[:])
             add_turned(totals[-1], 0, gated, i % 2 == 0, i % 2 == 1)
         round_sums(totals[-2], rounded_first, LT - 2, 1)
-        firsts = [first_product(turned_1[b], b, first_tile(b)[:]) for b in range(3)]
+        firsts = [
+            first_product(turned_1[b], b, at(offset, [P, 2, P, 2], f"first{b}")[:])
+            for b, offset in enumerate((AT_FIRST_0, AT_FIRST_1, AT_FIRST_2))
+        ]
         round_sums(totals[-1], rounded_first, LT - 1, 1)
 
         def fetch_mid(i, dst):
@@ -354,15 +373,15 @@ def tile_moe_mhm_none_kernel(
             fetch_plain(i // LT, i % LT, S_MID, V_FIRST, dst)
             return dst
 
-        mid_01 = in_slot(f"ring{(4 * LT - 4) % RING}", [P, 2, mid], F32, "mid_01")
-        late_01 = in_slot(f"ring{(4 * LT - 1) % RING}", [P, 2, narrow], F32, "late_01")
+        mid_01 = at(AT_MID_01, [P, 2, mid], "mid_01")
+        late_01 = [at(AT_RING + 4 * narrow * i, [P, narrow], f"late_{i}") for i in range(2)]
         mid_23 = in_slot("after_first_products", [P, 2, mid], F32, "mid_23")
         mid_a = bank(2)
         for i in range(2):
             add_mid(i, mid_a, fetch_mid(i, mid_01[:, i]))
         for b in range(3):
             second_product(turned_2[b], firsts[b], b, rounded_s, b)
-        late = [fetch_late(i, late_01[:, i]) for i in range(2)]
+        late = [fetch_late(i, late_01[i][:]) for i in range(2)]
         group(grouped_first, 0, 2, turn_back(rounded_first, 0, 2, 1))
         group(grouped_first, 2, 4, turn_back(rounded_first, 2, 4, 5))
         late.append(fetch_late(2, in_slot(f"rounded{V_FIRST}", [P, narrow], F32, "late_2")[:]))
@@ -371,8 +390,8 @@ def tile_moe_mhm_none_kernel(
         for i in range(2, 4):
             add_mid(i, mid_a, fetch_mid(i, mid_23[:, i - 2]))
         round_sums(mid_a, rounded_mid, 0, 2)
-        mid_4 = in_slot("first1", [P, mid], F32, "mid_4")
-        mid_5 = in_slot("first2", [P, mid], F32, "mid_5")
+        mid_4 = at(AT_MID_4, [P, mid], "mid_4")
+        mid_5 = at(AT_MID_5, [P, mid], "mid_5")
         mid_b = bank(5)
         add_mid(4, mid_b, fetch_mid(4, mid_4[:]))
         add_mid(5, mid_b, fetch_mid(5, mid_5[:]))
@@ -380,63 +399,60 @@ def tile_moe_mhm_none_kernel(
         for j in range(LT - 1):
             turn_plain(turned_1, j, late[j])
         codes_first = quantize(grouped_first, V_FIRST)
-        mid_67 = in_slot("first1", [P, 3, mid], F32, "mid_67")
-        last = in_slot("first2", [P, 2 * LT * P], F32, "last")
-        late_456 = in_slot("after_first_products", [P, 3, narrow], F32, "late_456")
-        late_end = in_slot("first1", [P, narrow + H], F32, "late_end")
+        late_3 = at(AT_MID_4, [P, narrow], "late_3")
+        mid_67 = at(AT_MID_67, [P, 2, mid], "mid_67")
+        last = at(AT_LAST, [P, 2 * LT * P], "last")
+        late_second = in_slot("after_first_products", [P, LT, narrow], F32, "late_second")
         turned_2 = [bank(3), bank(4)]
-        nc.vector.tensor_copy(mid_67[:, 2], looked_up(0, LT - 1, S_MID, V_FIRST))
-        turn_plain(turned_1, LT - 1, mid_67[:, 2])
-        for i in range(6, 8):
-            add_mid(i, mid_b, fetch_mid(i, mid_67[:, i - 6]))
+        nc.vector.tensor_copy(late_3[:], looked_up(0, LT - 1, S_MID, V_FIRST))
+        turn_plain(turned_1, LT - 1, late_3)
         codes_s = quantize(grouped_s, 0)
-        for j in range(LT - 1):
-            fetch_late(LT + j, late_456[:, j])
         acc_a = bank(1)
         merge_head(acc_a, codes_s, 0, 2 * P, True)
         merge_head(acc_a, codes_first, 0, 2 * P, False)
-        for j in range(2):
-            turn_plain(turned_2, j, late_456[:, j])
-        turn_plain(turned_2, 2, late_456[:, 2])
+        for i in range(6, 8):
+            add_mid(i, mid_b, fetch_mid(i, mid_67[:, i - 6]))
+        for j in range(LT - 1):
+            turn_plain(turned_2, j, fetch_late(LT + j, late_second[:, j]))
         first_3 = first_product(turned_1[0], 3, first_tile(3)[:])
+        turn_plain(turned_2, LT - 1, fetch_late(2 * LT - 1, late_second[:, LT - 1]))
+        acc_b = bank(0)
+        merge_head(acc_b, codes_s, 2 * P, 3 * P, True)
+        merge_head(acc_b, codes_first, 2 * P, 3 * P, False)
         round_sums(mid_b, rounded_mid, 2, 2)
-        turn_plain(turned_2, 3, fetch_late(LT + 3, late_end[:, :narrow]))
         back_mid = turn_back(rounded_mid, 0, 2, 2)
-        first_4 = first_product(turned_1[1], 4, late_end[:, narrow:].rearrange("z (u p e) -> z u p e", u=2, e=2))
+        first_4 = first_product(turned_1[1], 4, at(AT_MID_67, [P, 2, P, 2], "first4")[:])
+        store(acc_b, 2 * P, 3 * P, nc.scalar.copy, "staged2")
         group(grouped_mid, 0, 2, back_mid)
 
-        last_a, last_b = bank(5), bank(7)
-        for j in range(LT):
-            for r in range(2):
-                fetched = last[:, P * (2 * j + r) : P * (2 * j + r + 1)]
-                fetch_gated(r, j, V_LAST, Z, fetched)
-                if j < LT - 1:
-                    add_turned(last_a, P * j, fetched, j + r == 0, j + r == LT - 1)
-                else:
-                    add_turned(last_b, 0, fetched, r == 0, r == 1)
+        last_a, last_b = bank(6), bank(7)
+        for i in range(2 * LT):
+            fetched = last[:, P * i : P * (i + 1)]
+            fetch_gated(i % 2, i // 2, V_LAST, Z, fetched)
+            if i < 2 * LT - 2:
+                add_turned(last_a, P * (i // 2), fetched, i == 0, i == 2 * LT - 3)
+            else:
+                add_turned(last_b, 0, fetched, i % 2 == 0, i % 2 == 1)
+        half_0 = bank(0)
+        merge_pass(half_0[:, :P], codes_first, 0, 5 * P, T, True, False)
         second_product(turned_2[0], first_3, 3, rounded_3, 0)
         second_product(turned_2[1], first_4, 4, rounded_4, 0)
         round_sums(last_a, rounded_last, 0, LT - 1)
         round_sums(last_b, rounded_last, LT - 1, 1)
 
-        group(grouped_3, 0, 1, turn_back(rounded_3, 0, 1, 0))
-        acc_b = bank(3)
-        merge_head(acc_b, codes_s, 2 * P, 3 * P, True)
-        merge_head(acc_b, codes_first, 2 * P, 3 * P, False)
-        group(grouped_4, 0, 1, turn_back(rounded_4, 0, 1, 6))
-        group(grouped_last, 0, 1, turn_back(rounded_last, 0, 1, 5))
+        group(grouped_3, 0, 1, turn_back(rounded_3, 0, 1, 5))
+        group(grouped_4, 0, 1, turn_back(rounded_4, 0, 1, 3))
+        group(grouped_last, 0, 1, turn_back(rounded_last, 0, 1, 6))
+        store(acc_a, 0, 2 * P, nc.vector.tensor_copy, "first3")
         codes_mid = quantize(grouped_mid, V_MID)
-        halves = [bank(7), bank(4)]
-        for h in range(N // P):
-            merge_pass(halves[h][:, :P], codes_first, h, 5 * P, T, True, False)
-        acc_3, acc_4 = bank(2), bank(0)
+        acc_3, acc_4 = bank(7), bank(5)
         merge_head(acc_3, codes_mid, 3 * P, 4 * P, True)
         merge_head(acc_4, codes_mid, 4 * P, 5 * P, True)
-        store(acc_a, 0, 2 * P, nc.vector.tensor_copy, "first3")
+        halves = [half_0, bank(3)]
+        merge_pass(halves[1][:, :P], codes_first, 1, 5 * P, T, True, False)
         codes_3 = quantize(grouped_3, S_MID)
         codes_4 = quantize(grouped_4, S_MID + P)
         codes_last = quantize(grouped_last, V_LAST)
-        store(acc_b, 2 * P, 3 * P, nc.scalar.copy, f"rounded{V_LAST}")
         merge_head(acc_3, codes_3, 3 * P, 4 * P, False)
         merge_head(acc_4, codes_4, 4 * P, 5 * P, False)
         for h in range(N // P):

@@ -26,8 +26,8 @@ BANK = 512
 BANKS = 8
 PER_COL = 16
 
-W_CUTS = (0, 1, 3, 6, 12)
-WS_CUTS = (0, 3, 6, 12)
+W_CUTS = (0, 1, 3, 7, 12)
+WS_CUTS = (0, 3, 7, 12)
 XW_FIRST = 4
 XS_FIRST = 3
 S_MID, V_FIRST, V_MID, V_LAST = 384, 640, 1152, 1408
@@ -118,10 +118,9 @@ def tile_moe_mhm_none_kernel(
             xw[:].bitcast(I32).rearrange("p (o t) -> p o t", o=D),
             x_words.rearrange("o p t d -> p o (t d)").bitcast(I32),
         )
+        nc.sync.dma_start(ww[0][:, 0, 2 * P :].bitcast(I32), w_words[0, 0, :, 2 * P :].bitcast(I32))
         for i in range(len(ws)):
             load_scale_rows(ws[i][:], w_scales[WS_CUTS[i] : WS_CUTS[i + 1], 0])
-            if i == 0:
-                nc.sync.dma_start(ww[0][:, 0, 2 * P :].bitcast(I32), w_words[0, 0, :, 2 * P :].bitcast(I32))
             load_words(i + 1)
         nc.sync.dma_start(pos_sb[0][:], pos1)
         nc.sync.dma_start(pos_sb[1][:], pos2)

@@ -26,11 +26,12 @@ BANK = 512
 BANKS = 8
 PER_COL = 16
 
-W_CUTS = (0, 1, 3, 7, 12)
-WS_CUTS = (0, 3, 7, 12)
+W_CUTS = (0, 1, 3, 5, 8, 12)
+WS_CUTS = (0, 3, 8, 12)
+X_HEAD = 256
 XW_FIRST = 4
 XS_FIRST = 3
-S_MID, V_FIRST, V_MID, V_LAST = 384, 640, 1152, 1408
+S_MID, V_FIRST, V_LAST, V_MID = 384, 640, 1152, 1280
 S_BLOCKS = V_FIRST // P
 RING = 5
 SLOT = 5120
@@ -99,6 +100,12 @@ def tile_moe_mhm_none_kernel(
                 w_words[W_CUTS[i] : W_CUTS[i + 1], 0].rearrange("e p b -> p e b").bitcast(I32),
             )
 
+        def load_x_words(z0, z1):
+            o = z0 // T
+            nc.sync.dma_start(
+                xw[:, z0:z1].bitcast(I32), x_words[o, :, z0 - o * T : z1 - o * T].rearrange("p t d -> p (t d)").bitcast(I32)
+            )
+
         def load_gate_columns(dst, r, z0, z1):
             with nc.allow_non_contiguous_dma(reason="one gate value a partition and block"):
                 nc.sync.dma_start(dst[:], gate[r, 0, z0:z1].rearrange("(b z) -> z b", z=P))
@@ -112,16 +119,18 @@ def tile_moe_mhm_none_kernel(
         make_identity(nc, ident[:], nomemset=True)
 
         nc.sync.dma_start(offs_sb[:], offs)
-        nc.sync.dma_start(w_head[:].bitcast(I32), w_words[0, 0, :, : 2 * P].bitcast(I32))
+        load_x_words(0, X_HEAD)
         load_scale_rows(xs[:].rearrange("p (o t) -> p o t", o=D), x_scales)
-        nc.sync.dma_start(
-            xw[:].bitcast(I32).rearrange("p (o t) -> p o t", o=D),
-            x_words.rearrange("o p t d -> p o (t d)").bitcast(I32),
-        )
+        load_x_words(X_HEAD, T)
+        load_x_words(T, Z)
+        nc.sync.dma_start(w_head[:].bitcast(I32), w_words[0, 0, :, : 2 * P].bitcast(I32))
+        load_scale_rows(ws[0][:], w_scales[: WS_CUTS[1], 0])
         nc.sync.dma_start(ww[0][:, 0, 2 * P :].bitcast(I32), w_words[0, 0, :, 2 * P :].bitcast(I32))
-        for i in range(len(ws)):
-            load_scale_rows(ws[i][:], w_scales[WS_CUTS[i] : WS_CUTS[i + 1], 0])
-            load_words(i + 1)
+        for i in range(1, len(ww)):
+            if W_CUTS[i] in WS_CUTS:
+                k = WS_CUTS.index(W_CUTS[i])
+                load_scale_rows(ws[k][:], w_scales[WS_CUTS[k] : WS_CUTS[k + 1], 0])
+            load_words(i)
         nc.sync.dma_start(pos_sb[0][:], pos1)
         nc.sync.dma_start(pos_sb[1][:], pos2)
         nc.sync.dma_start(gate_wide[:], gate[:, :, V_FIRST:].rearrange("r p z -> p r z"))
@@ -330,13 +339,13 @@ def tile_moe_mhm_none_kernel(
             copy(staged[:].rearrange("p h t -> p (h t)"), acc[:, : (N // P) * width])
             nc.sync.dma_start(out_v[:, :, t0:t1], staged[:])
 
-        rounded_s, rounded_first = rounded_tile(0, S_MID), rounded_tile(V_FIRST, V_MID)
-        rounded_mid, rounded_last = rounded_tile(V_MID, V_LAST), rounded_tile(V_LAST, Z)
+        rounded_s, rounded_first = rounded_tile(0, S_MID), rounded_tile(V_FIRST, V_LAST)
+        rounded_mid, rounded_last = rounded_tile(V_MID, Z), rounded_tile(V_LAST, V_MID)
         rounded_3, rounded_4 = rounded_tile(S_MID, S_MID + P), rounded_tile(S_MID + P, V_FIRST)
-        grouped_first, grouped_mid = grouped_tile(V_FIRST, V_MID), grouped_tile(V_MID, V_LAST)
-        grouped_last, grouped_s = grouped_tile(V_LAST, Z), grouped_tile(0, S_MID)
+        grouped_first, grouped_mid = grouped_tile(V_FIRST, V_LAST), grouped_tile(V_MID, Z)
+        grouped_last, grouped_s = grouped_tile(V_LAST, V_MID), grouped_tile(0, S_MID)
         grouped_3, grouped_4 = grouped_tile(S_MID, S_MID + P), grouped_tile(S_MID + P, V_FIRST)
-        wide, mid, narrow = V_MID - V_FIRST, V_LAST - V_MID, V_FIRST - S_MID
+        wide, mid, narrow = V_LAST - V_FIRST, Z - V_MID, V_FIRST - S_MID
 
         turned_1 = [bank(2 + b) for b in range(3)]
         turned_2 = [bank(5 + b) for b in range(3)]
@@ -352,7 +361,7 @@ def tile_moe_mhm_none_kernel(
                     round_sums(totals[-2], rounded_first, i // 2 - 2, 1)
                 totals.append(bank(1 - i // 2 % 2))
             gated = in_ring(2 * i + 1, [P, wide], f"gated{i}")
-            fetch_gated(i % 2, i // 2, V_FIRST, V_MID, gated[:])
+            fetch_gated(i % 2, i // 2, V_FIRST, V_LAST, gated[:])
             add_turned(totals[-1], 0, gated, i % 2 == 0, i % 2 == 1)
         round_sums(totals[-2], rounded_first, LT - 2, 1)
         firsts = [
@@ -362,7 +371,7 @@ def tile_moe_mhm_none_kernel(
         round_sums(totals[-1], rounded_first, LT - 1, 1)
 
         def fetch_mid(i, dst):
-            fetch_gated(i % 2, i // 2, V_MID, V_LAST, dst)
+            fetch_gated(i % 2, i // 2, V_MID, Z, dst)
             return dst
 
         def add_mid(i, total, fetched):
@@ -427,13 +436,11 @@ def tile_moe_mhm_none_kernel(
         last_a, last_b = bank(6), bank(7)
         for i in range(2 * LT):
             fetched = last[:, P * i : P * (i + 1)]
-            fetch_gated(i % 2, i // 2, V_LAST, Z, fetched)
+            fetch_gated(i % 2, i // 2, V_LAST, V_MID, fetched)
             if i < 2 * LT - 2:
                 add_turned(last_a, P * (i // 2), fetched, i == 0, i == 2 * LT - 3)
             else:
                 add_turned(last_b, 0, fetched, i % 2 == 0, i % 2 == 1)
-        half_0 = bank(0)
-        merge_pass(half_0[:, :P], codes_first, 0, 5 * P, T, True, False)
         second_product(turned_2[0], first_3, 3, rounded_3, 0)
         second_product(turned_2[1], first_4, 4, rounded_4, 0)
         round_sums(last_a, rounded_last, 0, LT - 1)
@@ -444,21 +451,22 @@ def tile_moe_mhm_none_kernel(
         group(grouped_last, 0, 1, turn_back(rounded_last, 0, 1, 6))
         store(acc_a, 0, 2 * P, nc.vector.tensor_copy, "first3")
         codes_mid = quantize(grouped_mid, V_MID)
-        acc_3, acc_4 = bank(7), bank(5)
-        merge_head(acc_3, codes_mid, 3 * P, 4 * P, True)
+        acc_5, acc_4 = bank(7), bank(5)
+        merge_head(acc_5, codes_first, 5 * P, T, True)
+        merge_head(acc_5, codes_mid, 5 * P, T, False)
         merge_head(acc_4, codes_mid, 4 * P, 5 * P, True)
-        halves = [half_0, bank(3)]
-        merge_pass(halves[1][:, :P], codes_first, 1, 5 * P, T, True, False)
+        store(acc_5, 5 * P, T, nc.scalar.copy, f"rounded{V_LAST}")
         codes_3 = quantize(grouped_3, S_MID)
         codes_4 = quantize(grouped_4, S_MID + P)
         codes_last = quantize(grouped_last, V_LAST)
-        merge_head(acc_3, codes_3, 3 * P, 4 * P, False)
+        halves = [bank(3), bank(6)]
+        for h in range(N // P):
+            merge_pass(halves[h][:, :P], codes_3, h, 3 * P, 4 * P, True, False)
         merge_head(acc_4, codes_4, 4 * P, 5 * P, False)
         for h in range(N // P):
-            merge_pass(halves[h][:, :P], codes_last, h, 5 * P, T, False, True)
-        store(acc_3, 3 * P, 4 * P, nc.vector.tensor_copy, "staged3")
-        store(acc_4, 4 * P, 5 * P, nc.scalar.copy, "staged4")
+            merge_pass(halves[h][:, :P], codes_last, h, 3 * P, 4 * P, False, True)
+        store(acc_4, 4 * P, 5 * P, nc.vector.tensor_copy, "staged4")
         staged_last = keep.tile([P, N // P, P], F32, name="staged_last")
         nc.vector.tensor_copy(staged_last[:, 0], halves[0][:, :P])
         nc.scalar.copy(staged_last[:, 1], halves[1][:, :P])
-        nc.sync.dma_start(out_v[:, :, 5 * P : T], staged_last[:])
+        nc.sync.dma_start(out_v[:, :, 3 * P : 4 * P], staged_last[:])

@@ -24,6 +24,7 @@ P = 128
 LT = H // P
 BANK = 512
 BANKS = 8
+FIRST_BANK = 5
 PER_COL = 16
 
 W_CUTS = (0, 1, 3, 5, 8, 12)
@@ -88,7 +89,7 @@ def tile_moe_mhm_none_kernel(
             return tiles[tile][:, i - cuts[tile]]
 
         def load_scale_rows(plane, rows):
-            for q in range(4):
+            for q in (2, 0, 3, 1):
                 nc.sync.dma_start(
                     plane[32 * q : 32 * q + 4].bitcast(I32),
                     rows[:, 4 * q : 4 * q + 4, :].rearrange("a r c -> r a c").bitcast(I32),
@@ -156,27 +157,29 @@ def tile_moe_mhm_none_kernel(
         taken = []
 
         def next_bank():
-            taken.append(len(taken) % BANKS)
+            taken.append((len(taken) + FIRST_BANK) % BANKS)
             return bank(taken[-1])
 
-        def slots(tiles, e0, e1):
-            first = tiles[0].shape[1] // C
-            if e0 < first:
-                return tiles[0][:, e0 * C : e1 * C]
-            return tiles[1][:, (e0 - first) * C : (e1 - first) * C]
+        def slots(tiles, s0, s1):
+            first = tiles[0].shape[1]
+            if s0 < first:
+                return tiles[0][:, s0:s1]
+            return tiles[1][:, s0 - first : s1 - first]
+
+        def gather(dst, window, s0, s1):
+            nc.vector.tensor_copy(slots(dst, s0, s1), window[:].indirect(offs_sb[:, s0 // PER_COL : s1 // PER_COL]))
 
         def gather_slots(dst, window, e0, e1):
-            cols = slice(e0 * C // PER_COL, e1 * C // PER_COL)
-            nc.vector.tensor_copy(slots(dst, e0, e1), window[:].indirect(offs_sb[:, cols]))
+            gather(dst, window, e0 * C, e1 * C)
 
-        def expert(acc, j, e):
+        def expert(acc, j, e, u0=0, u1=C):
             words = w_head[:] if e == 0 and j == 0 else part(ww, W_CUTS, e)[:, 2 * P * j : 2 * P * (j + 1)]
             nc.tensor.matmul_mx(
                 out=acc,
                 lhsT=words.bitcast(FP4X4),
                 lhsT_scale=part(ws, WS_CUTS, e)[:, P * j : P * (j + 1)],
-                rhs=slots(xw_slots, e, e + 1).bitcast(FP8X4),
-                rhs_scale=slots(xs_slots, e, e + 1),
+                rhs=slots(xw_slots, e * C + u0, e * C + u1).bitcast(FP8X4),
+                rhs_scale=slots(xs_slots, e * C + u0, e * C + u1),
                 start=True,
                 stop=True,
             )
@@ -200,23 +203,31 @@ def tile_moe_mhm_none_kernel(
             half_expert(e, 2)
 
         gather_slots(xs_slots, xs, 0, XS_FIRST)
-        gather_slots(xw_slots, xw, 0, 1)
-        for j in range(LT):
-            acc = next_bank()[:, :C]
-            expert(acc, j, 0)
-            nc.scalar.copy(y[j][:, :C], acc)
-        gather_slots(xw_slots, xw, 1, 2)
-        expert_tiles(1)
+        for e in range(2):
+            gather_slots(xw_slots, xw, e, e + 1)
+            for j in range(LT):
+                acc = next_bank()[:, :C]
+                expert(acc, j, e)
+                nc.scalar.copy(y[j][:, e * C : (e + 1) * C], acc)
         for e in range(2, E - 3):
             gather_slots(*((xw_slots, xw) if e % 2 == 0 else (xs_slots, xs)), e, e + 2)
             expert_tiles(e)
         gather_slots(xs_slots, xs, E - 3, E - 1)
-        gather_slots(xw_slots, xw, E - 2, E)
+        gather_slots(xw_slots, xw, E - 2, E - 1)
         gather_slots(xs_slots, xs, E - 1, E)
+        gather(xw_slots, xw, S - C, S - P)
+        gather(xw_slots, xw, S - P, S)
         half_expert(E - 3, 0)
         half_expert(E - 3, 2, nc.vector.tensor_copy)
-        expert_tiles(E - 2)
-        half_expert(E - 1, 0, nc.vector.tensor_copy)
+        half_expert(E - 2, 0)
+        half_expert(E - 2, 2)
+        acc = next_bank()
+        for u0 in (0, P):
+            expert(acc[:, u0 : u0 + P], 0, E - 1, u0, u0 + P)
+        nc.vector.tensor_copy(y[0][:, S - C :], acc[:, :C])
+        acc = next_bank()[:, :C]
+        expert(acc, 1, E - 1)
+        nc.vector.tensor_copy(y[1][:, S - C :], acc)
         last_23 = two_tiles(E - 1, 2)
         empty(last_23, E - 1, 2, nc.scalar.copy)
 

from contextlib import ExitStack

import concourse.mybir as mybir
from concourse.masks import make_identity

D, T, E, C, H, N = 2, 768, 12, 256, 512, 256
Z = D * T
S = E * C
FLOPS = 2 * H * H * S + 2 * D * H * N * T

F32 = mybir.dt.float32
BF16 = mybir.dt.bfloat16
I32 = mybir.dt.int32
U32 = mybir.dt.uint32
U16 = mybir.dt.uint16
U8 = mybir.dt.uint8
FP8X4 = mybir.dt.float8_e4m3fn_x4
FP4X4 = mybir.dt.float4_e2m1fn_x4
MULT = mybir.AluOpType.mult
ADD = mybir.AluOpType.add
COPY = mybir.ActivationFunctionType.Copy

P = 128
LT = H // P
BANK = 512
BANKS = 8
FIRST_BANK = 5
PER_COL = 16

W_CUTS = (0, 1, 3, 5, 8, 12)
WS_CUTS = (0, 3, 8, 12)
X_HEAD = 256
XW_FIRST = 4
XS_FIRST = 3
S_MID, V_FIRST, V_LAST, V_MID = 384, 640, 1152, 1280
S_BLOCKS = V_FIRST // P
RING = 5
SLOT = 5120
AT_RING = 1024
AT_MID_01, AT_FIRST_2 = AT_RING + SLOT - 1024, AT_RING + SLOT + 1024
AT_MID_5 = AT_FIRST_2 + 1024
AT_LAST = AT_RING + 1024
AT_FIRST_0, AT_FIRST_1 = AT_RING + 2 * SLOT - 1280, AT_RING + 2 * SLOT + 768
AT_MID_4 = AT_FIRST_1 + 1024
AT_MID_67 = AT_RING - 1024

AT_XS_REST, AT_W_HEAD, AT_XW_REST = 0, 2176, 2304


def tile_moe_mhm_none_kernel(
    tc, x_words, x_scales, w_words, w_scales, wm_words, wm_scales, gate, offs, pos1, pos2, out
):
    nc = tc.nc
    with ExitStack() as ctx:
        keep = ctx.enter_context(tc.tile_pool(name="keep", bufs=1))
        head = ctx.enter_context(tc.tile_pool(name="head", bufs=1))
        slot = ctx.enter_context(tc.tile_pool(name="slot", bufs=1))
        ring = ctx.enter_context(tc.tile_pool(name="ring", bufs=1))
        psum = ctx.enter_context(tc.psum_pool(name="psum", bufs=1))

        def in_slot(tag, shape, dtype, name):
            return slot.tile(shape, dtype, name=name, tag=tag, align_bytes=64)

        def at(offset, shape, name):
            return ring.tile(shape, F32, name=name, offset=offset)

        def in_ring(n, shape, name):
            return at(AT_RING + n % RING * SLOT, shape, name)

        offs_sb = keep.tile([P, S // PER_COL], U16, name="offs_sb")
        pos_sb = [keep.tile([P, Z // PER_COL], U16, name=f"pos_sb{r}") for r in range(2)]
        xw = keep.tile([P, Z], U32, name="xw")
        xs = keep.tile([P, Z], U8, name="xs", align_bytes=64)
        ws = [keep.tile([P, b - a, H], U8, name=f"ws{a}", align_bytes=64) for a, b in zip(WS_CUTS, WS_CUTS[1:])]
        ww = [keep.tile([P, b - a, 2 * H], U8, name=f"ww{a}", align_bytes=64) for a, b in zip(W_CUTS, W_CUTS[1:])]
        w_head = head.tile([P, 2 * P], U8, name="w_head", offset=AT_W_HEAD, align_bytes=64)
        wmw = keep.tile([P, D, 2 * N], U8, name="wmw", align_bytes=64)
        wms = keep.tile([P, D, N], U8, name="wms", align_bytes=64)
        ident = keep.tile([P, P], F32, name="ident")
        gate_first = [
            in_slot("after_first_products", [P, S_MID // P], F32, "gate_first_a"),
            keep.tile([P, (V_FIRST - S_MID) // P], F32, name="gate_first_b"),
        ]
        gate_second = keep.tile([P, S_BLOCKS], F32, name="gate_second")
        gate_wide = keep.tile([P, 2, Z - V_FIRST], F32, name="gate_wide")

        def part(tiles, cuts, i):
            tile = max(k for k in range(len(tiles)) if cuts[k] <= i)
            return tiles[tile][:, i - cuts[tile]]

        def load_scale_rows(plane, rows):
            for q in (2, 0, 3, 1):
                nc.sync.dma_start(
                    plane[32 * q : 32 * q + 4].bitcast(I32),
                    rows[:, 4 * q : 4 * q + 4, :].rearrange("a r c -> r a c").bitcast(I32),
                )

        def load_words(i):
            nc.sync.dma_start(
                ww[i][:].bitcast(I32),
                w_words[W_CUTS[i] : W_CUTS[i + 1], 0].rearrange("e p b -> p e b").bitcast(I32),
            )

        def load_x_words(z0, z1):
            o = z0 // T
            nc.sync.dma_start(
                xw[:, z0:z1].bitcast(I32), x_words[o, :, z0 - o * T : z1 - o * T].rearrange("p t d -> p (t d)").bitcast(I32)
            )

        def load_gate_columns(dst, r, z0, z1):
            with nc.allow_non_contiguous_dma(reason="one gate value a partition and block"):
                nc.sync.dma_start(dst[:], gate[r, 0, z0:z1].rearrange("(b z) -> z b", z=P))

        nc.vector.memset(xs[:].bitcast(I32), 0)
        nc.vector.memset(ws[0][:].rearrange("p e l -> p (e l)").bitcast(I32), 0)
        nc.vector.memset(ident[:], 0.0)
        nc.vector.memset(ws[1][:].rearrange("p e l -> p (e l)").bitcast(I32), 0)
        nc.vector.memset(ws[2][:].rearrange("p e l -> p (e l)").bitcast(I32), 0)
        nc.vector.memset(wms[:].rearrange("p o n -> p (o n)").bitcast(I32), 0)
        make_identity(nc, ident[:], nomemset=True)

        nc.sync.dma_start(offs_sb[:], offs)
        load_x_words(0, X_HEAD)
        load_scale_rows(xs[:].rearrange("p (o t) -> p o t", o=D), x_scales)
        load_x_words(X_HEAD, T)
        load_x_words(T, Z)
        nc.sync.dma_start(w_head[:].bitcast(I32), w_words[0, 0, :, : 2 * P].bitcast(I32))
        load_scale_rows(ws[0][:], w_scales[: WS_CUTS[1], 0])
        nc.sync.dma_start(ww[0][:, 0, 2 * P :].bitcast(I32), w_words[0, 0, :, 2 * P :].bitcast(I32))
        for i in range(1, len(ww)):
            if W_CUTS[i] in WS_CUTS:
                k = WS_CUTS.index(W_CUTS[i])
                load_scale_rows(ws[k][:], w_scales[WS_CUTS[k] : WS_CUTS[k + 1], 0])
            load_words(i)
        nc.sync.dma_start(pos_sb[0][:], pos1)
        nc.sync.dma_start(pos_sb[1][:], pos2)
        nc.sync.dma_start(gate_wide[:], gate[:, :, V_FIRST:].rearrange("r p z -> p r z"))
        load_gate_columns(gate_first[0], 0, 0, S_MID)
        load_gate_columns(gate_first[1], 0, S_MID, V_FIRST)
        load_gate_columns(gate_second, 1, 0, V_FIRST)
        nc.sync.dma_start(wmw[:].bitcast(I32), wm_words.rearrange("o p b -> p o b").bitcast(I32))
        load_scale_rows(wms[:], wm_scales)

        xw_slots = [
            keep.tile([P, XW_FIRST * C], U32, name="xw_first", align_bytes=64),
            head.tile([P, (E - XW_FIRST) * C], U32, name="xw_rest", offset=AT_XW_REST, align_bytes=64),
        ]
        xs_slots = [
            keep.tile([P, XS_FIRST * C], U8, name="xs_first", align_bytes=64),
            head.tile([P, (E - XS_FIRST) * C], U8, name="xs_rest", offset=AT_XS_REST, align_bytes=64),
        ]
        y = [keep.tile([P, S], F32, name=f"y{j}") for j in range(LT)]

        def bank(k):
            return psum.tile([P, BANK], F32, name=f"bank{k}")

        taken = []

        def next_bank():
            taken.append((len(taken) + FIRST_BANK) % BANKS)
            return bank(taken[-1])

        def slots(tiles, s0, s1):
            first = tiles[0].shape[1]
            if s0 < first:
                return tiles[0][:, s0:s1]
            return tiles[1][:, s0 - first : s1 - first]

        def gather(dst, window, s0, s1):
            nc.vector.tensor_copy(slots(dst, s0, s1), window[:].indirect(offs_sb[:, s0 // PER_COL : s1 // PER_COL]))

        def gather_slots(dst, window, e0, e1):
            gather(dst, window, e0 * C, e1 * C)

        def expert(acc, j, e, u0=0, u1=C):
            words = w_head[:] if e == 0 and j == 0 else part(ww, W_CUTS, e)[:, 2 * P * j : 2 * P * (j + 1)]
            nc.tensor.matmul_mx(
                out=acc,
                lhsT=words.bitcast(FP4X4),
                lhsT_scale=part(ws, WS_CUTS, e)[:, P * j : P * (j + 1)],
                rhs=slots(xw_slots, e * C + u0, e * C + u1).bitcast(FP8X4),
                rhs_scale=slots(xs_slots, e * C + u0, e * C + u1),
                start=True,
                stop=True,
            )

        def two_tiles(e, j0):
            acc = next_bank()
            for i in range(2):
                expert(acc[:, i * C : (i + 1) * C], j0 + i, e)
            return acc

        def empty(acc, e, j, copy):
            copy(y[j][:, e * C : (e + 1) * C], acc[:, j % 2 * C : (j % 2 + 1) * C])

        def half_expert(e, j0, copy=nc.scalar.copy):
            acc = two_tiles(e, j0)
            for j in range(j0, j0 + 2):
                empty(acc, e, j, copy)

        def expert_tiles(e):
            half_expert(e, 0)
            half_expert(e, 2)

        gather_slots(xs_slots, xs, 0, XS_FIRST)
        for e in range(2):
            gather_slots(xw_slots, xw, e, e + 1)
            for j in range(LT):
                acc = next_bank()[:, :C]
                expert(acc, j, e)
                nc.scalar.copy(y[j][:, e * C : (e + 1) * C], acc)
        for e in range(2, E - 3):
            gather_slots(*((xw_slots, xw) if e % 2 == 0 else (xs_slots, xs)), e, e + 2)
            expert_tiles(e)
        gather_slots(xs_slots, xs, E - 3, E - 1)
        gather_slots(xw_slots, xw, E - 2, E - 1)
        gather_slots(xs_slots, xs, E - 1, E)
        gather(xw_slots, xw, S - C, S - P)
        gather(xw_slots, xw, S - P, S)
        half_expert(E - 3, 0)
        half_expert(E - 3, 2, nc.vector.tensor_copy)
        half_expert(E - 2, 0)
        half_expert(E - 2, 2)
        acc = next_bank()
        for u0 in (0, P):
            expert(acc[:, u0 : u0 + P], 0, E - 1, u0, u0 + P)
        nc.vector.tensor_copy(y[0][:, S - C :], acc[:, :C])
        acc = next_bank()[:, :C]
        expert(acc, 1, E - 1)
        nc.vector.tensor_copy(y[1][:, S - C :], acc)
        last_23 = two_tiles(E - 1, 2)
        empty(last_23, E - 1, 2, nc.scalar.copy)

        out_v = out.rearrange("(h p) t -> p h t", p=P)

        def looked_up(r, j, z0, z1):
            return y[j][:].indirect(pos_sb[r][:, z0 // PER_COL : z1 // PER_COL])

        def fetch_gated(r, j, z0, z1, dst):
            nc.vector.tensor_tensor(dst, looked_up(r, j, z0, z1), gate_wide[:, r, z0 - V_FIRST : z1 - V_FIRST], MULT)

        def add_turned(total, col, fetched, first, last):
            blocks = fetched.shape[1] // P
            step = BANK // blocks
            for b in range(blocks):
                nc.tensor.matmul(
                    total[:, col + step * b : col + step * b + P],
                    lhsT=fetched[:, P * b : P * (b + 1)],
                    rhs=ident[:],
                    is_transpose=True,
                    start=(first and b == 0),
                    stop=(last and b == blocks - 1),
                )

        def round_sums(total, rounded, j0, tiles):
            blocks = rounded.shape[1]
            nc.scalar.copy(
                rounded[:, :, :, 32 * j0 : 32 * (j0 + tiles), :],
                total[:]
                .rearrange("z (b l) -> z b l", b=blocks)[:, :, : P * tiles]
                .rearrange("z b (p u e) -> z b u p e", u=2, e=2),
            )

        def fetch_plain(r, j, z0, z1, dst):
            nc.scalar.activation(dst, looked_up(r, j, z0, z1), COPY)

        def turn_plain(turned, j, fetched):
            for b in range(len(turned)):
                nc.tensor.transpose(turned[b][:, P * j : P * (j + 1)], fetched[:, P * b : P * (b + 1)], ident[:])

        def rounded_tile(z0, z1):
            return in_slot(f"rounded{z0}", [P, (z1 - z0) // P, 2, P, 2], BF16, f"rounded{z0}")

        def grouped_tile(z0, z1):
            return keep.tile([P, z1 - z0, 4], BF16, name=f"grouped{z0}", align_bytes=64)

        def first_tile(block):
            return in_slot(f"first{block}", [P, 2, P, 2], F32, f"first{block}")

        def first_product(turned, block, first):
            chunk = 0 if block < S_MID // P else 1
            column = block - chunk * (S_MID // P)
            nc.scalar.activation(
                first,
                turned[:].rearrange("z (p u e) -> z u p e", u=2, e=2),
                COPY,
                scale=gate_first[chunk][:, column : column + 1],
            )
            return first

        def second_product(turned, first, block, rounded, b):
            for u in range(2):
                nc.vector.scalar_tensor_tensor(
                    rounded[:, b, u],
                    turned[:].rearrange("z (p u e) -> z u p e", u=2, e=2)[:, u],
                    gate_second[:, block : block + 1],
                    first[:, u],
                    MULT,
                    ADD,
                )

        def turn_back(rounded, b0, b1, k):
            back = bank(k)
            for b in range(b0, b1):
                pairs = rounded[:, b].rearrange("z u p e -> z (u p e)").bitcast(F32)
                for u in range(2):
                    col = P * (2 * (b - b0) + u)
                    nc.tensor.transpose(back[:, col : col + P], pairs[:, P * u : P * (u + 1)], ident[:])
            return back

        def group(grouped, b0, b1, back):
            words = grouped[:, P * b0 : P * b1, :].rearrange("p z t -> p (z t)").bitcast(F32)
            nc.scalar.copy(
                words.rearrange("p (b z u) -> p b z u", z=P, u=2),
                back[:, : 2 * P * (b1 - b0)].rearrange("p (b u z) -> p b z u", u=2, z=P),
            )

        def quantize(grouped, z0):
            width = grouped.shape[1]
            codes = keep.tile([P, width], U32, name=f"codes{z0}", align_bytes=64)
            scales = keep.tile([P, width], U8, name=f"scales{z0}", align_bytes=64)
            nc.vector.quantize_mx(
                out=codes[:].bitcast(FP8X4), scales=scales[:], in_=grouped[:].rearrange("p z t -> p (z t)")
            )
            return codes, scales, z0

        def merge_pass(acc, quantized, h, t0, t1, start, stop):
            codes, scales, z0 = quantized
            o = 0 if z0 <= t0 < z0 + codes.shape[1] else 1
            cols = slice(o * T + t0 - z0, o * T + t1 - z0)
            nc.tensor.matmul_mx(
                out=acc,
                lhsT=wmw[:, o, 2 * P * h : 2 * P * (h + 1)].bitcast(FP4X4),
                lhsT_scale=wms[:, o, P * h : P * (h + 1)],
                rhs=codes[:, cols].bitcast(FP8X4),
                rhs_scale=scales[:, cols],
                start=start,
                stop=stop,
            )

        def merge_head(acc, quantized, t0, t1, first):
            width = t1 - t0
            for h in range(N // P):
                start, stop = first and h == 0, not first and h == N // P - 1
                merge_pass(acc[:, h * width : (h + 1) * width], quantized, h, t0, t1, start, stop)

        def store(acc, t0, t1, copy, tag):
            width = t1 - t0
            staged = in_slot(tag, [P, N // P, width], F32, f"staged{t0}")
            copy(staged[:].rearrange("p h t -> p (h t)"), acc[:, : (N // P) * width])
            nc.sync.dma_start(out_v[:, :, t0:t1], staged[:])

        rounded_s, rounded_first = rounded_tile(0, S_MID), rounded_tile(V_FIRST, V_LAST)
        rounded_mid, rounded_last = rounded_tile(V_MID, Z), rounded_tile(V_LAST, V_MID)
        rounded_3, rounded_4 = rounded_tile(S_MID, S_MID + P), rounded_tile(S_MID + P, V_FIRST)
        grouped_first, grouped_mid = grouped_tile(V_FIRST, V_LAST), grouped_tile(V_MID, Z)
        grouped_last, grouped_s = grouped_tile(V_LAST, V_MID), grouped_tile(0, S_MID)
        grouped_3, grouped_4 = grouped_tile(S_MID, S_MID + P), grouped_tile(S_MID + P, V_FIRST)
        wide, mid, narrow = V_LAST - V_FIRST, Z - V_MID, V_FIRST - S_MID

        turned_1 = [bank(2 + b) for b in range(3)]
        turned_2 = [bank(5 + b) for b in range(3)]
        totals = []
        for i in range(2 * LT):
            plain = in_ring(2 * i, [P, S_MID], f"plain{i}")
            fetch_plain(i // LT, i % LT, 0, S_MID, plain[:])
            turn_plain(turned_1 if i < LT else turned_2, i % LT, plain)
            if i == 0:
                empty(last_23, E - 1, LT - 1, nc.scalar.copy)
            if i % 2 == 0:
                if i >= LT:
                    round_sums(totals[-2], rounded_first, i // 2 - 2, 1)
                totals.append(bank(1 - i // 2 % 2))
            gated = in_ring(2 * i + 1, [P, wide], f"gated{i}")
            fetch_gated(i % 2, i // 2, V_FIRST, V_LAST, gated[:])
            add_turned(totals[-1], 0, gated, i % 2 == 0, i % 2 == 1)
        round_sums(totals[-2], rounded_first, LT - 2, 1)
        firsts = [
            first_product(turned_1[b], b, at(offset, [P, 2, P, 2], f"first{b}")[:])
            for b, offset in enumerate((AT_FIRST_0, AT_FIRST_1, AT_FIRST_2))
        ]
        round_sums(totals[-1], rounded_first, LT - 1, 1)

        def fetch_mid(i, dst):
            fetch_gated(i % 2, i // 2, V_MID, Z, dst)
            return dst

        def add_mid(i, total, fetched):
            add_turned(total, P * (i // 2 % 2), fetched, i % 4 == 0, i % 4 == 3)

        def fetch_late(i, dst):
            fetch_plain(i // LT, i % LT, S_MID, V_FIRST, dst)
            return dst

        mid_01 = at(AT_MID_01, [P, 2, mid], "mid_01")
        late_01 = [at(AT_RING + 4 * narrow * i, [P, narrow], f"late_{i}") for i in range(2)]
        mid_23 = in_slot("after_first_products", [P, 2, mid], F32, "mid_23")
        mid_a = bank(2)
        for i in range(2):
            add_mid(i, mid_a, fetch_mid(i, mid_01[:, i]))
        for b in range(3):
            second_product(turned_2[b], firsts[b], b, rounded_s, b)
        late = [fetch_late(i, late_01[i][:]) for i in range(2)]
        group(grouped_first, 0, 2, turn_back(rounded_first, 0, 2, 1))
        group(grouped_first, 2, 4, turn_back(rounded_first, 2, 4, 5))
        late.append(fetch_late(2, in_slot(f"rounded{V_FIRST}", [P, narrow], F32, "late_2")[:]))
        group(grouped_s, 0, 2, turn_back(rounded_s, 0, 2, 0))
        group(grouped_s, 2, 3, turn_back(rounded_s, 2, 3, 7))
        for i in range(2, 4):
            add_mid(i, mid_a, fetch_mid(i, mid_23[:, i - 2]))
        round_sums(mid_a, rounded_mid, 0, 2)
        mid_4 = at(AT_MID_4, [P, mid], "mid_4")
        mid_5 = at(AT_MID_5, [P, mid], "mid_5")
        mid_b = bank(5)
        add_mid(4, mid_b, fetch_mid(4, mid_4[:]))
        add_mid(5, mid_b, fetch_mid(5, mid_5[:]))
        turned_1 = [bank(0), bank(7)]
        for j in range(LT - 1):
            turn_plain(turned_1, j, late[j])
        codes_first = quantize(grouped_first, V_FIRST)
        late_3 = at(AT_MID_4, [P, narrow], "late_3")
        mid_67 = at(AT_MID_67, [P, 2, mid], "mid_67")
        last = at(AT_LAST, [P, 2 * LT * P], "last")
        late_second = in_slot("after_first_products", [P, LT, narrow], F32, "late_second")
        turned_2 = [bank(3), bank(4)]
        nc.vector.tensor_copy(late_3[:], looked_up(0, LT - 1, S_MID, V_FIRST))
        turn_plain(turned_1, LT - 1, late_3)
        codes_s = quantize(grouped_s, 0)
        acc_a = bank(1)
        merge_head(acc_a, codes_s, 0, 2 * P, True)
        merge_head(acc_a, codes_first, 0, 2 * P, False)
        for i in range(6, 8):
            add_mid(i, mid_b, fetch_mid(i, mid_67[:, i - 6]))
        for j in range(LT - 1):
            turn_plain(turned_2, j, fetch_late(LT + j, late_second[:, j]))
        first_3 = first_product(turned_1[0], 3, first_tile(3)[:])
        turn_plain(turned_2, LT - 1, fetch_late(2 * LT - 1, late_second[:, LT - 1]))
        acc_b = bank(0)
        merge_head(acc_b, codes_s, 2 * P, 3 * P, True)
        merge_head(acc_b, codes_first, 2 * P, 3 * P, False)
        round_sums(mid_b, rounded_mid, 2, 2)
        back_mid = turn_back(rounded_mid, 0, 2, 2)
        first_4 = first_product(turned_1[1], 4, at(AT_MID_67, [P, 2, P, 2], "first4")[:])
        store(acc_b, 2 * P, 3 * P, nc.scalar.copy, "staged2")
        group(grouped_mid, 0, 2, back_mid)

        last_a, last_b = bank(6), bank(7)
        for i in range(2 * LT):
            fetched = last[:, P * i : P * (i + 1)]
            fetch_gated(i % 2, i // 2, V_LAST, V_MID, fetched)
            if i < 2 * LT - 2:
                add_turned(last_a, P * (i // 2), fetched, i == 0, i == 2 * LT - 3)
            else:
                add_turned(last_b, 0, fetched, i % 2 == 0, i % 2 == 1)
        second_product(turned_2[0], first_3, 3, rounded_3, 0)
        second_product(turned_2[1], first_4, 4, rounded_4, 0)
        round_sums(last_a, rounded_last, 0, LT - 1)
        round_sums(last_b, rounded_last, LT - 1, 1)

        group(grouped_3, 0, 1, turn_back(rounded_3, 0, 1, 5))
        group(grouped_4, 0, 1, turn_back(rounded_4, 0, 1, 3))
        group(grouped_last, 0, 1, turn_back(rounded_last, 0, 1, 6))
        store(acc_a, 0, 2 * P, nc.vector.tensor_copy, "first3")
        codes_mid = quantize(grouped_mid, V_MID)
        acc_5, acc_4 = bank(7), bank(5)
        merge_head(acc_5, codes_first, 5 * P, T, True)
        merge_head(acc_5, codes_mid, 5 * P, T, False)
        merge_head(acc_4, codes_mid, 4 * P, 5 * P, True)
        store(acc_5, 5 * P, T, nc.scalar.copy, f"rounded{V_LAST}")
        codes_3 = quantize(grouped_3, S_MID)
        codes_4 = quantize(grouped_4, S_MID + P)
        codes_last = quantize(grouped_last, V_LAST)
        halves = [bank(3), bank(6)]
        for h in range(N // P):
            merge_pass(halves[h][:, :P], codes_3, h, 3 * P, 4 * P, True, False)
        merge_head(acc_4, codes_4, 4 * P, 5 * P, False)
        for h in range(N // P):
            merge_pass(halves[h][:, :P], codes_last, h, 3 * P, 4 * P, False, True)
        store(acc_4, 4 * P, 5 * P, nc.vector.tensor_copy, "staged4")
        staged_last = keep.tile([P, N // P, P], F32, name="staged_last")
        nc.vector.tensor_copy(staged_last[:, 0], halves[0][:, :P])
        nc.scalar.copy(staged_last[:, 1], halves[1][:, :P])
        nc.sync.dma_start(out_v[:, :, 3 * P : 4 * P], staged_last[:])
